import numpy as np
import ml_dtypes


def mxq(x, axis, fmt="e4m3"):
    dtype, down = {"e4m3": (ml_dtypes.float8_e4m3fn, 7), "e5m2": (ml_dtypes.float8_e5m2, 14)}[fmt]
    v = np.moveaxis(np.asarray(x, np.float32).astype(ml_dtypes.bfloat16).astype(np.float64), axis, -1)
    blocks = v.reshape(v.shape[:-1] + (-1, 32))
    amax = np.abs(blocks).max(-1, keepdims=True)
    byte = np.maximum(np.where(amax > 0, np.frexp(amax)[1] - 1 + 127, 0) - down, 1)
    scale = np.exp2(byte - 127.0)
    codes = (blocks / scale).astype(np.float32).astype(dtype).astype(np.float64)
    return np.moveaxis((codes * scale).reshape(v.shape), -1, axis)


WIDE = False


def mx_kscale(k):
    if not WIDE:
        return np.ones(k)
    levels = np.array([10, -10, 5, -5, 0])
    if k % 512:
        return np.exp2(np.random.permutation(np.resize(levels, k // 32))).repeat(32)
    a = np.empty((k // 512, 16))
    for p in range(k // 512):
        a[p, :8] = np.random.permutation(np.resize(levels, 8))
        for g in range(8):
            far = levels[np.abs(levels - a[p, g]) >= 10]
            a[p, g + 8] = far[np.random.randint(len(far))]
    return np.exp2(a.ravel()).repeat(32)


def f64(x):
    return np.asarray(x).astype(np.float64)


def striped(idx):
    return np.tile(idx.reshape(-1, 16).T, (8, 1)).astype(np.uint16)


def unstriped(offs):
    return offs[:16].T.reshape(-1).astype(np.int64)


def pack_weight(w):
    k, n = w.shape
    w = f64(np.asarray(w, np.float32).astype(ml_dtypes.bfloat16)).reshape(k // 32, 32, n)
    amax = np.abs(w).max(1)
    byte = np.clip(np.where(amax > 0, np.frexp(amax)[1] - 1 + 127 - 7, 1), 1, 254)
    scaled = (w * np.exp2(127.0 - byte)[:, None, :]).reshape(k, n).astype(np.float32)
    words = np.ascontiguousarray(scaled.reshape(k // 512, 128, 4, n).transpose(0, 1, 3, 2)).astype(ml_dtypes.float8_e4m3fn).view(np.uint8)
    return words, np.ascontiguousarray(byte.astype(np.uint8).reshape(k // 512, 16, n))


def unpack_weight(words, scales):
    g, p, n, _ = words.shape
    vals = np.ascontiguousarray(words).view(ml_dtypes.float8_e4m3fn).astype(np.float64) * np.repeat(np.exp2(scales.astype(np.float64) - 127.0), 8, axis=1)[..., None]
    return vals.transpose(0, 1, 3, 2).reshape(g * 512, n)


E2M1 = np.array([0.0, 0.5, 1.0, 1.5, 2.0, 3.0, 4.0, 6.0, -0.0, -0.5, -1.0, -1.5, -2.0, -3.0, -4.0, -6.0])


def pack_fp4(w):
    k, n = w.shape
    w = f64(np.asarray(w, np.float32).astype(ml_dtypes.bfloat16)).reshape(k // 32, 32, n)
    amax = np.abs(w).max(1)
    mant, ex = np.frexp(amax / 6.0)
    byte = np.clip(np.where(amax > 0, np.where(mant > 0.5, ex, ex - 1) + 127, 1), 1, 254)
    scaled = (w * np.exp2(127.0 - byte)[:, None, :]).reshape(k, n).astype(np.float32)
    c = np.ascontiguousarray(scaled.reshape(k // 512, 128, 4, n).transpose(0, 1, 3, 2)).astype(ml_dtypes.float4_e2m1fn).view(np.uint8) & 0xF
    words = (c[..., 0::2] | (c[..., 1::2] << 4)).reshape(k // 512, 128, 2 * n)
    return np.ascontiguousarray(words), np.ascontiguousarray(byte.astype(np.uint8).reshape(k // 512, 16, n))


def unpack_fp4(words, scales):
    g, _, n = scales.shape
    words = np.ascontiguousarray(words).reshape(g, 128, n, 2)
    nib = np.empty((g, 128, n, 4), np.uint8)
    nib[..., 0::2] = words & 0xF
    nib[..., 1::2] = words >> 4
    vals = E2M1[nib] * np.repeat(np.exp2(scales.astype(np.float64) - 127.0), 8, axis=1)[..., None]
    return vals.transpose(0, 1, 3, 2).reshape(g * 512, n)


def silu(v):
    return v / (1.0 + np.exp(-np.maximum(v, -700.0)))


K, T, S, H, N, U = 1024, 2048, 1024, 512, 256, 1024


def setup_inputs():
    n = np.random.standard_normal
    s = mx_kscale(K)[:, None]
    u = mx_kscale(H)
    packed_xT = pack_weight(n((K, T)) * s)
    packed_w3 = pack_fp4(n((H, N)) / np.sqrt(H) / u[:, None])
    return {
        "x_words": packed_xT[0],
        "x_scales": packed_xT[1],
        "w1": (n((K, H)) / np.sqrt(2 * K) / s * u).astype(np.float32),
        "w2": (n((K, H)) / np.sqrt(2 * K) / s * u).astype(np.float32),
        "w3_words": packed_w3[0],
        "w3_scales": packed_w3[1],
        "offs": striped(np.random.permutation(T)[:S]),
        "src": striped(np.random.permutation(S)[(S * np.random.uniform(0, 1, U) ** 4).astype(np.int64)]),
        "dst": striped(np.random.permutation(S)),
    }


def reference(x_words, x_scales, w1, w2, w3_words, w3_scales, offs, src, dst):
    xq = unpack_weight(x_words, x_scales)[:, unstriped(offs)]
    y = mxq(f64(w1), 0, "e4m3").T @ xq
    e = mxq(f64(w2), 0, "e4m3").T @ xq
    z = silu(y[:, unstriped(src)] + e[:, unstriped(dst)])
    return unpack_fp4(w3_words, w3_scales).T @ mxq(z, 0, "e4m3")

@@ -1,0 +1,194 @@
+from contextlib import ExitStack
+
+import concourse.mybir as mybir
+
+K, T, S, H, N = 1024, 2048, 1024, 512, 256
+FLOPS = 2 * (2 * K * H * S + H * N * S)
+
+F32 = mybir.dt.float32
+BF16 = mybir.dt.bfloat16
+I32 = mybir.dt.int32
+U32 = mybir.dt.uint32
+U16 = mybir.dt.uint16
+U8 = mybir.dt.uint8
+FP8X4 = mybir.dt.float8_e4m3fn_x4
+FP4X4 = mybir.dt.float4_e2m1fn_x4
+ADD = mybir.AluOpType.add
+SILU = mybir.ActivationFunctionType.Silu
+
+P = 128
+PACK = 4
+K_PASS = P * PACK
+PASSES = K // K_PASS
+BANK = 512
+LIST = 16
+EDGE_PIECES = (512, 256, 128, 128)
+
+
+def tile_picked_hub_silu_p_kernel(
+    tc, x_words, x_scales, w1, w2, w3_words, w3_scales, offs, src, dst, out
+):
+    nc = tc.nc
+    with ExitStack() as ctx:
+        lists = ctx.enter_context(tc.tile_pool(name="lists", bufs=1))
+        keep = ctx.enter_context(tc.tile_pool(name="keep", bufs=1))
+        ring = ctx.enter_context(tc.tile_pool(name="ring", bufs=2))
+        acc_pool = ctx.enter_context(tc.psum_pool(name="acc", bufs=6))
+        res_pool = ctx.enter_context(tc.psum_pool(name="res", bufs=2))
+
+        def held(name, shape, dtype):
+            return keep.tile(shape, dtype, name=name, align_bytes=64)
+
+        offs_sb = lists.tile([P, S // LIST], U16, name="offs_sb")
+        src_sb = lists.tile([P, S // LIST], U16, name="src_sb")
+        dst_sb = lists.tile([P, S // LIST], U16, name="dst_sb")
+
+        x_table = [held(f"x_table{g}", [P, T], U32) for g in range(PASSES)]
+        xs_table = held("xs_table", [P, T], U8)
+        w3_codes = held("w3_codes", [P, 2 * N], U8)
+        w3_plane = held("w3_plane", [P, N], U8)
+        nc.gpsimd.memset(xs_table[:].bitcast(I32), 0)
+        nc.gpsimd.memset(w3_plane[:].bitcast(I32), 0)
+
+        def load_words(g):
+            nc.sync.dma_start(x_table[g][:].bitcast(I32), x_words[g].rearrange("p n t -> p (n t)").bitcast(I32))
+
+        def load_weights(name, w, g, c0, c1):
+            raw = held(name, [P, PACK, c1 - c0], F32)
+            rows = w[g * K_PASS : (g + 1) * K_PASS, c0:c1]
+            nc.sync.dma_start(raw[:], rows.rearrange("(p j) c -> p j c", j=PACK))
+            return raw
+
+        nc.sync.dma_start(offs_sb[:], offs)
+        nc.sync.dma_start(src_sb[:], src)
+        nc.sync.dma_start(dst_sb[:], dst)
+        for q in range(4):
+            nc.sync.dma_start(
+                xs_table[32 * q : 32 * q + 4 * PASSES, :].bitcast(I32),
+                x_scales[:, 4 * q : 4 * q + 4, :].bitcast(I32),
+            )
+        load_words(0)
+        w1_raw0 = load_weights("w1_raw0", w1, 0, 0, H)
+        load_words(1)
+        w1_raw1a = load_weights("w1_raw1a", w1, 1, 0, H // 2)
+        w1_raw1b = load_weights("w1_raw1b", w1, 1, H // 2, H)
+        w2_raw = [load_weights(f"w2_raw{g}", w2, g, 0, H) for g in range(PASSES)]
+        nc.sync.dma_start(w3_codes[:].bitcast(I32), w3_words[0].bitcast(I32))
+        for q in range(4):
+            nc.sync.dma_start(
+                w3_plane[32 * q : 32 * q + 4, :].bitcast(I32), w3_scales[0, 4 * q : 4 * q + 4, :].bitcast(I32)
+            )
+
+        x_codes = [held(f"x_codes{g}", [P, S], U32) for g in range(PASSES)]
+        x_plane = held("x_plane", [P, S], U8)
+        nc.vector.tensor_copy(x_plane[:], xs_table[:].indirect(offs_sb[:]))
+        nc.vector.tensor_copy(x_codes[0][:], x_table[0][:].indirect(offs_sb[:]))
+
+        def deal(copy, grouped, raw_cols, m0, m1):
+            copy(
+                grouped[:, :, m0:m1, :].rearrange("p t m j -> p m j t"),
+                raw_cols.rearrange("p j (m t) -> p m j t", t=PACK),
+            )
+
+        def quantised(name, grouped, calls):
+            codes = held(name + "_codes", [P, H], U32)
+            plane = held(name + "_plane", [P, H], U8)
+            flat = grouped.rearrange("p t m j -> p (t m j)")
+            width = H // calls
+            for c in range(calls):
+                cols = slice(c * width, (c + 1) * width)
+                nc.vector.quantize_mx(
+                    out=codes[:, cols].bitcast(FP8X4),
+                    scales=plane[:, cols],
+                    in_=flat[:, PACK * c * width : PACK * (c + 1) * width],
+                )
+            return codes, plane
+
+        half = P // 2
+        w1_bf = held("grouped", [P, PASSES, PACK, P, PACK], BF16)
+        deal(nc.scalar.copy, w1_bf[:, 0], w1_raw0[:, :, : H // 4], 0, P // 4)
+        deal(nc.vector.tensor_copy, w1_bf[:, 0], w1_raw0[:, :, H // 4 :], P // 4, P)
+        w1_q = [quantised("w1_0", w1_bf[:, 0], 1)]
+        nc.vector.tensor_copy(x_codes[1][:], x_table[1][:].indirect(offs_sb[:]))
+        deal(nc.scalar.copy, w1_bf[:, 1], w1_raw1a[:], 0, half)
+        deal(nc.scalar.copy, w1_bf[:, 1], w1_raw1b[:, :, : H // 4], half, half + P // 4)
+        deal(nc.vector.tensor_copy, w1_bf[:, 1], w1_raw1b[:, :, H // 4 :], half + P // 4, P)
+        w1_q.append(quantised("w1_1", w1_bf[:, 1], PACK))
+        w2_bf = held("grouped", [P, PASSES, PACK, P, PACK], BF16)
+
+        def product(name, w_q, t, copies):
+            rows = held(name, [P, S], F32)
+            m_cols = slice(t * P, (t + 1) * P)
+            for h in range(S // BANK):
+                cols = slice(h * BANK, (h + 1) * BANK)
+                acc = acc_pool.tile([P, BANK], F32, name="acc")
+                for g in range(PASSES):
+                    codes, plane = w_q[g]
+                    nc.tensor.matmul_mx(
+                        out=acc[:],
+                        lhsT=codes[:, m_cols].bitcast(FP8X4),
+                        lhsT_scale=plane[:, m_cols],
+                        rhs=x_codes[g][:, cols].bitcast(FP8X4),
+                        rhs_scale=x_plane[4 * g :, cols],
+                        start=(g == 0),
+                        stop=(g == PASSES - 1),
+                    )
+                copies[h](rows[:, cols], acc[:])
+            return rows
+
+        y_at_src = []
+        w2_q = []
+        for t in range(PACK):
+            if t >= PACK - PASSES:
+                g = len(w2_q)
+                for c in range(4):
+                    deal(nc.scalar.copy, w2_bf[:, g], w2_raw[g][:, :, c * P : (c + 1) * P], c * P // 4, (c + 1) * P // 4)
+                w2_q.append(quantised(f"w2_{g}", w2_bf[:, g], 1))
+            copies = (nc.vector.tensor_copy if t == 0 else nc.scalar.copy,) * 2
+            y_rows = product(f"y{t}", w1_q, t, copies)
+            picked = held(f"y_at_src{t}", [P, S], F32)
+            for h in range(S // BANK):
+                nc.vector.tensor_copy(
+                    picked[:, h * BANK : (h + 1) * BANK],
+                    y_rows[:].indirect(src_sb[:, h * BANK // LIST : (h + 1) * BANK // LIST]),
+                )
+            y_at_src.append(picked)
+
+        e_rows = [product(f"e{t}", w2_q, t, (nc.scalar.copy, nc.scalar.copy)) for t in range(PACK)]
+
+        out_view = out.rearrange("(a p) r -> p a r", p=P)
+        r0 = 0
+        for i, n in enumerate(EDGE_PIECES):
+            r1 = r0 + n
+            u = ring.tile([P, PACK, n], F32, name="u", align_bytes=64)
+            for t in range(PACK):
+                nc.vector.tensor_tensor(
+                    u[:, t, :], e_rows[t][:].indirect(dst_sb[:, r0 // LIST : r1 // LIST]), y_at_src[t][:, r0:r1], ADD
+                )
+            z = held(f"z{i}", [P, n, PACK], BF16)
+            nc.scalar.activation(
+                z[:].rearrange("p (c i) t -> p c t i", i=4), u[:].rearrange("p t (c i) -> p c t i", i=4), SILU
+            )
+            z_codes = held(f"z_codes{i}", [P, n], U32)
+            z_plane = held(f"z_plane{i}", [P, n], U8)
+            nc.vector.quantize_mx(
+                out=z_codes[:].bitcast(FP8X4), scales=z_plane[:], in_=z[:].rearrange("p r t -> p (r t)")
+            )
+            result = held(f"result{i}", [P, N // P, n], F32)
+            per_bank = min(N // P, BANK // n)
+            for a0 in range(0, N // P, per_bank):
+                res = res_pool.tile([P, per_bank, n], F32, name="res")
+                for a in range(per_bank):
+                    m0 = (a0 + a) * P
+                    nc.tensor.matmul_mx(
+                        out=res[:, a, :],
+                        lhsT=w3_codes[:, 2 * m0 : 2 * (m0 + P)].bitcast(FP4X4),
+                        lhsT_scale=w3_plane[:, m0 : m0 + P],
+                        rhs=z_codes[:].bitcast(FP8X4),
+                        rhs_scale=z_plane[:],
+                        start=True,
+                        stop=True,
+                    )
+                nc.scalar.copy(result[:, a0 : a0 + per_bank, :], res[:])
+            nc.sync.dma_start(out_view[:, :, r0:r1], result[:])
+            r0 = r1

@@ -1,6 +1,7 @@
 from contextlib import ExitStack
 
 import concourse.mybir as mybir
+from concourse.masks import make_identity
 
 K, T, S, H, N = 1024, 2048, 1024, 512, 256
 FLOPS = 2 * (2 * K * H * S + H * N * S)
@@ -23,6 +24,9 @@ PASSES = K // K_PASS
 BANK = 512
 LIST = 16
 EDGE_PIECES = (512, 256, 128, 128)
+FINISH = 256
+TILES = H // P
+LEAD = 3
 
 
 def tile_picked_hub_silu_p_kernel(
@@ -32,12 +36,21 @@ def tile_picked_hub_silu_p_kernel(
     with ExitStack() as ctx:
         lists = ctx.enter_context(tc.tile_pool(name="lists", bufs=1))
         keep = ctx.enter_context(tc.tile_pool(name="keep", bufs=1))
-        ring = ctx.enter_context(tc.tile_pool(name="ring", bufs=2))
-        acc_pool = ctx.enter_context(tc.psum_pool(name="acc", bufs=6))
-        res_pool = ctx.enter_context(tc.psum_pool(name="res", bufs=2))
+        vector_out = ctx.enter_context(tc.tile_pool(name="vector_out", bufs=44))
+        scalar_out = ctx.enter_context(tc.tile_pool(name="scalar_out", bufs=18))
+        psum = ctx.enter_context(tc.psum_pool(name="psum", bufs=8))
 
         def held(name, shape, dtype):
             return keep.tile(shape, dtype, name=name, align_bytes=64)
+
+        def by_vector(shape, dtype):
+            return vector_out.tile(shape, dtype, name="by_vector", align_bytes=64)
+
+        def by_scalar(shape, dtype):
+            return scalar_out.tile(shape, dtype, name="by_scalar", align_bytes=64)
+
+        def next_bank():
+            return psum.tile([P, BANK], F32, name="bank")
 
         offs_sb = lists.tile([P, S // LIST], U16, name="offs_sb")
         src_sb = lists.tile([P, S // LIST], U16, name="src_sb")
@@ -49,15 +62,11 @@ def tile_picked_hub_silu_p_kernel(
         w3_plane = held("w3_plane", [P, N], U8)
         nc.gpsimd.memset(xs_table[:].bitcast(I32), 0)
         nc.gpsimd.memset(w3_plane[:].bitcast(I32), 0)
+        ident = held("ident", [P, P], F32)
+        make_identity(nc, ident[:])
 
         def load_words(g):
             nc.sync.dma_start(x_table[g][:].bitcast(I32), x_words[g].rearrange("p n t -> p (n t)").bitcast(I32))
-
-        def load_weights(name, w, g, c0, c1):
-            raw = held(name, [P, PACK, c1 - c0], F32)
-            rows = w[g * K_PASS : (g + 1) * K_PASS, c0:c1]
-            nc.sync.dma_start(raw[:], rows.rearrange("(p j) c -> p j c", j=PACK))
-            return raw
 
         nc.sync.dma_start(offs_sb[:], offs)
         nc.sync.dma_start(src_sb[:], src)
@@ -68,127 +77,197 @@ def tile_picked_hub_silu_p_kernel(
                 x_scales[:, 4 * q : 4 * q + 4, :].bitcast(I32),
             )
         load_words(0)
-        w1_raw0 = load_weights("w1_raw0", w1, 0, 0, H)
         load_words(1)
-        w1_raw1a = load_weights("w1_raw1a", w1, 1, 0, H // 2)
-        w1_raw1b = load_weights("w1_raw1b", w1, 1, H // 2, H)
-        w2_raw = [load_weights(f"w2_raw{g}", w2, g, 0, H) for g in range(PASSES)]
+        raw = []
+        for n in range(2 * TILES):
+            chunk = held(f"raw{n}", [P, PASSES, PACK, P], F32)
+            w, a = (w1, w2)[n % 2], n // 2
+            for g in range(PASSES):
+                rows = w[g * K_PASS : (g + 1) * K_PASS, a * P : (a + 1) * P]
+                nc.sync.dma_start(chunk[:, g], rows.rearrange("(p j) c -> p j c", j=PACK))
+            raw.append(chunk)
         nc.sync.dma_start(w3_codes[:].bitcast(I32), w3_words[0].bitcast(I32))
         for q in range(4):
             nc.sync.dma_start(
                 w3_plane[32 * q : 32 * q + 4, :].bitcast(I32), w3_scales[0, 4 * q : 4 * q + 4, :].bitcast(I32)
             )
 
-        x_codes = [held(f"x_codes{g}", [P, S], U32) for g in range(PASSES)]
+        x_codes = {}
         x_plane = held("x_plane", [P, S], U8)
         nc.vector.tensor_copy(x_plane[:], xs_table[:].indirect(offs_sb[:]))
-        nc.vector.tensor_copy(x_codes[0][:], x_table[0][:].indirect(offs_sb[:]))
 
-        def deal(copy, grouped, raw_cols, m0, m1):
-            copy(
-                grouped[:, :, m0:m1, :].rearrange("p t m j -> p m j t"),
-                raw_cols.rearrange("p j (m t) -> p m j t", t=PACK),
+        def gather_words(g, h):
+            x_codes[g, h] = by_vector([P, BANK], U32)
+            offsets = offs_sb[:, h * BANK // LIST : (h + 1) * BANK // LIST]
+            nc.vector.tensor_copy(x_codes[g, h][:], x_table[g][:].indirect(offsets))
+
+        def cast(n, part):
+            grouped = by_scalar([P, part.stop - part.start, P, PACK], BF16)
+            nc.scalar.copy(
+                grouped[:].rearrange("p g (c i) j -> p g c j i", i=4),
+                raw[n][:, part].rearrange("p g j (c i) -> p g c j i", i=4),
             )
+            return grouped
 
-        def quantised(name, grouped, calls):
-            codes = held(name + "_codes", [P, H], U32)
-            plane = held(name + "_plane", [P, H], U8)
-            flat = grouped.rearrange("p t m j -> p (t m j)")
-            width = H // calls
-            for c in range(calls):
-                cols = slice(c * width, (c + 1) * width)
-                nc.vector.quantize_mx(
-                    out=codes[:, cols].bitcast(FP8X4),
-                    scales=plane[:, cols],
-                    in_=flat[:, PACK * c * width : PACK * (c + 1) * width],
-                )
-            return codes, plane
+        def quantise(n, grouped):
+            passes = grouped.shape[1]
+            codes = by_vector([P, passes * P], U32)
+            plane = held(f"plane{n}_{passes}", [P, passes * P], U8)
+            nc.vector.quantize_mx(
+                out=codes[:].bitcast(FP8X4), scales=plane[:], in_=grouped[:].rearrange("p g c j -> p (g c j)")
+            )
+            return [(codes[:, g * P : (g + 1) * P], plane[:, g * P : (g + 1) * P]) for g in range(passes)]
 
-        half = P // 2
-        w1_bf = held("grouped", [P, PASSES, PACK, P, PACK], BF16)
-        deal(nc.scalar.copy, w1_bf[:, 0], w1_raw0[:, :, : H // 4], 0, P // 4)
-        deal(nc.vector.tensor_copy, w1_bf[:, 0], w1_raw0[:, :, H // 4 :], P // 4, P)
-        w1_q = [quantised("w1_0", w1_bf[:, 0], 1)]
-        nc.vector.tensor_copy(x_codes[1][:], x_table[1][:].indirect(offs_sb[:]))
-        deal(nc.scalar.copy, w1_bf[:, 1], w1_raw1a[:], 0, half)
-        deal(nc.scalar.copy, w1_bf[:, 1], w1_raw1b[:, :, : H // 4], half, half + P // 4)
-        deal(nc.vector.tensor_copy, w1_bf[:, 1], w1_raw1b[:, :, H // 4 :], half + P // 4, P)
-        w1_q.append(quantised("w1_1", w1_bf[:, 1], PACK))
-        w2_bf = held("grouped", [P, PASSES, PACK, P, PACK], BF16)
-
-        def product(name, w_q, t, copies):
-            rows = held(name, [P, S], F32)
-            m_cols = slice(t * P, (t + 1) * P)
+        def multiply(weights):
+            banks = []
             for h in range(S // BANK):
                 cols = slice(h * BANK, (h + 1) * BANK)
-                acc = acc_pool.tile([P, BANK], F32, name="acc")
+                bank = next_bank()
                 for g in range(PASSES):
-                    codes, plane = w_q[g]
                     nc.tensor.matmul_mx(
-                        out=acc[:],
-                        lhsT=codes[:, m_cols].bitcast(FP8X4),
-                        lhsT_scale=plane[:, m_cols],
-                        rhs=x_codes[g][:, cols].bitcast(FP8X4),
+                        out=bank[:],
+                        lhsT=weights[g][0].bitcast(FP8X4),
+                        lhsT_scale=weights[g][1],
+                        rhs=x_codes[g, h][:].bitcast(FP8X4),
                         rhs_scale=x_plane[4 * g :, cols],
                         start=(g == 0),
                         stop=(g == PASSES - 1),
                     )
-                copies[h](rows[:, cols], acc[:])
-            return rows
+                banks.append(bank)
+            return banks
 
-        y_at_src = []
-        w2_q = []
-        for t in range(PACK):
-            if t >= PACK - PASSES:
-                g = len(w2_q)
-                for c in range(4):
-                    deal(nc.scalar.copy, w2_bf[:, g], w2_raw[g][:, :, c * P : (c + 1) * P], c * P // 4, (c + 1) * P // 4)
-                w2_q.append(quantised(f"w2_{g}", w2_bf[:, g], 1))
-            copies = (nc.vector.tensor_copy if t == 0 else nc.scalar.copy,) * 2
-            y_rows = product(f"y{t}", w1_q, t, copies)
-            picked = held(f"y_at_src{t}", [P, S], F32)
-            for h in range(S // BANK):
-                nc.vector.tensor_copy(
-                    picked[:, h * BANK : (h + 1) * BANK],
-                    y_rows[:].indirect(src_sb[:, h * BANK // LIST : (h + 1) * BANK // LIST]),
-                )
-            y_at_src.append(picked)
+        starts = [sum(EDGE_PIECES[:i]) for i in range(len(EDGE_PIECES))]
+        zt = [held(f"zt{i}", [P, PACK * width], BF16) for i, width in enumerate(EDGE_PIECES)]
 
-        e_rows = [product(f"e{t}", w2_q, t, (nc.scalar.copy, nc.scalar.copy)) for t in range(PACK)]
+        rows, picked = {}, {}
+
+        def empty(n, banks, copies):
+            rows[n] = by_scalar([P, S], F32)
+            for h, bank in enumerate(banks):
+                copies[h](rows[n][:, h * BANK : (h + 1) * BANK], bank[:])
+
+        def gather_edges(n, r0, width):
+            offsets = (src_sb, dst_sb)[n % 2][:, r0 // LIST : (r0 + width) // LIST]
+            tile = by_vector([P, width], F32)
+            nc.vector.tensor_copy(tile[:], rows[n][:].indirect(offsets))
+            for r in range(0, width, P):
+                picked[n, r0 + r] = tile[:, r : r + P]
+
+        def add(a, r0, width):
+            bank = next_bank()
+            for r in range(0, width, P):
+                for side in range(2):
+                    nc.tensor.matmul(
+                        bank[:, r : r + P],
+                        lhsT=picked[2 * a + side, r0 + r],
+                        rhs=ident[:],
+                        start=(side == 0),
+                        stop=(side == 1),
+                        is_transpose=True,
+                    )
+            return bank
+
+        def activate(a, bank, r0, width):
+            for i, piece in enumerate(EDGE_PIECES):
+                if r0 <= starts[i] < r0 + width:
+                    view = zt[i][:].rearrange("q (u b p e) -> q u b p e", u=2, p=P, e=2)
+                    cols = bank[:, starts[i] - r0 : starts[i] - r0 + piece]
+                    nc.scalar.activation(
+                        view[:, :, :, 32 * a : 32 * (a + 1), :],
+                        cols.rearrange("q (b p u e) -> q u b p e", p=32, u=2, e=2),
+                        SILU,
+                    )
 
         out_view = out.rearrange("(a p) r -> p a r", p=P)
-        r0 = 0
-        for i, n in enumerate(EDGE_PIECES):
-            r1 = r0 + n
-            u = ring.tile([P, PACK, n], F32, name="u", align_bytes=64)
-            for t in range(PACK):
-                nc.vector.tensor_tensor(
-                    u[:, t, :], e_rows[t][:].indirect(dst_sb[:, r0 // LIST : r1 // LIST]), y_at_src[t][:, r0:r1], ADD
-                )
-            z = held(f"z{i}", [P, n, PACK], BF16)
-            nc.scalar.activation(
-                z[:].rearrange("p (c i) t -> p c t i", i=4), u[:].rearrange("p t (c i) -> p c t i", i=4), SILU
-            )
-            z_codes = held(f"z_codes{i}", [P, n], U32)
-            z_plane = held(f"z_plane{i}", [P, n], U8)
-            nc.vector.quantize_mx(
-                out=z_codes[:].bitcast(FP8X4), scales=z_plane[:], in_=z[:].rearrange("p r t -> p (r t)")
-            )
-            result = held(f"result{i}", [P, N // P, n], F32)
-            per_bank = min(N // P, BANK // n)
-            for a0 in range(0, N // P, per_bank):
-                res = res_pool.tile([P, per_bank, n], F32, name="res")
-                for a in range(per_bank):
-                    m0 = (a0 + a) * P
-                    nc.tensor.matmul_mx(
-                        out=res[:, a, :],
-                        lhsT=w3_codes[:, 2 * m0 : 2 * (m0 + P)].bitcast(FP4X4),
-                        lhsT_scale=w3_plane[:, m0 : m0 + P],
-                        rhs=z_codes[:].bitcast(FP8X4),
-                        rhs_scale=z_plane[:],
-                        start=True,
-                        stop=True,
+
+        def turn_back(i, r0, width):
+            turned = next_bank()
+            for u in range(2):
+                for b in range(width // P):
+                    at = 2 * (u * EDGE_PIECES[i] + r0 - starts[i] + b * P)
+                    nc.tensor.transpose(
+                        turned[:, u * width + b * P : u * width + (b + 1) * P],
+                        zt[i][:, at : at + 2 * P].bitcast(F32),
+                        ident[:],
                     )
-                nc.scalar.copy(result[:, a0 : a0 + per_bank, :], res[:])
-            nc.sync.dma_start(out_view[:, :, r0:r1], result[:])
-            r0 = r1
+            return turned
+
+        def interleave(turned, width, on_vector):
+            z = (by_vector if on_vector else by_scalar)([P, PACK * width], BF16)
+            (nc.vector.tensor_copy if on_vector else nc.scalar.copy)(
+                z[:].bitcast(F32).rearrange("p (r u) -> p r u", u=2),
+                turned[:, : 2 * width].rearrange("p (u r) -> p r u", u=2),
+            )
+            return z
+
+        def last_product(z, r0, width):
+            z_codes = by_vector([P, width], U32)
+            z_plane = held(f"z_plane{r0}", [P, width], U8)
+            nc.vector.quantize_mx(out=z_codes[:].bitcast(FP8X4), scales=z_plane[:], in_=z[:])
+            res = next_bank()
+            for a in range(N // P):
+                nc.tensor.matmul_mx(
+                    out=res[:, a * width : (a + 1) * width],
+                    lhsT=w3_codes[:, 2 * a * P : 2 * (a + 1) * P].bitcast(FP4X4),
+                    lhsT_scale=w3_plane[:, a * P : (a + 1) * P],
+                    rhs=z_codes[:].bitcast(FP8X4),
+                    rhs_scale=z_plane[:],
+                    start=True,
+                    stop=True,
+                )
+            return res
+
+        def store(res, r0, width, on_vector):
+            result = (by_vector if on_vector else by_scalar)([P, N // P, width], F32)
+            (nc.vector.tensor_copy if on_vector else nc.scalar.copy)(
+                result[:], res[:, : 2 * width].rearrange("p (a r) -> p a r", a=N // P)
+            )
+            nc.sync.dma_start(out_view[:, :, r0 : r0 + width], result[:])
+
+        both = slice(0, PASSES)
+        halves = range(0, S, BANK)
+        gather_words(0, 0)
+        gather_words(0, 1)
+        gather_words(1, 0)
+        weights0 = quantise(0, cast(0, slice(0, 1))) + quantise(8, cast(0, slice(1, 2)))
+        gather_words(1, 1)
+        sums = [multiply(weights0), multiply(quantise(1, cast(1, both)))]
+        empty(0, sums[0], (nc.scalar.copy, nc.vector.tensor_copy))
+        added = []
+        for n in range(2 * TILES - 2):
+            for r0 in halves:
+                gather_edges(n, r0, BANK)
+                if (n, r0) == (0, 0):
+                    sums.append(multiply(quantise(2, cast(2, both))))
+            if n % 2 == 1:
+                added.append([add(n // 2, r0, BANK) for r0 in halves])
+            if n + LEAD < 2 * TILES:
+                sums.append(multiply(quantise(n + LEAD, cast(n + LEAD, both))))
+            empty(n + 1, sums[n + 1], (nc.scalar.copy, nc.scalar.copy))
+            if n % 2 == 0 and n > 0:
+                for r0, bank in zip(halves, added[n // 2 - 1]):
+                    activate(n // 2 - 1, bank, r0, BANK)
+        empty(2 * TILES - 1, sums[-1], (nc.scalar.copy, nc.scalar.copy))
+        for r0, bank in zip(halves, added[-1]):
+            activate(TILES - 2, bank, r0, BANK)
+
+        def last_tile(i):
+            for side in range(2):
+                gather_edges(2 * (TILES - 1) + side, starts[i], EDGE_PIECES[i])
+            activate(TILES - 1, add(TILES - 1, starts[i], EDGE_PIECES[i]), starts[i], EDGE_PIECES[i])
+
+        last_tile(0)
+        last_tile(1)
+        t0 = turn_back(0, 0, 256)
+        t1 = turn_back(0, 256, 256)
+        z0 = interleave(t0, 256, False)
+        last_tile(2)
+        last_tile(3)
+        z1 = interleave(t1, 256, True)
+        z2 = interleave(turn_back(1, 512, 256), 256, False)
+        z3 = interleave(turn_back(2, 768, 128), 128, False)
+        z4 = interleave(turn_back(3, 896, 128), 128, False)
+        units = [(z0, 0, 256), (z1, 256, 256), (z2, 512, 256), (z3, 768, 128), (z4, 896, 128)]
+        results = [last_product(*unit) for unit in units]
+        for i, res in enumerate(results):
+            store(res, units[i][1], units[i][2], i % 2 == 1)

@@ -23,10 +23,9 @@ K_PASS = P * PACK
 PASSES = K // K_PASS
 BANK = 512
 LIST = 16
-EDGE_PIECES = (512, 256, 128, 128)
-FINISH = 256
-TILES = H // P
-LEAD = 3
+UNIT = 256
+TURNED_EDGES = 768
+TAIL = 128
 
 
 def tile_picked_hub_silu_p_kernel(
@@ -36,9 +35,9 @@ def tile_picked_hub_silu_p_kernel(
     with ExitStack() as ctx:
         lists = ctx.enter_context(tc.tile_pool(name="lists", bufs=1))
         keep = ctx.enter_context(tc.tile_pool(name="keep", bufs=1))
-        vector_out = ctx.enter_context(tc.tile_pool(name="vector_out", bufs=44))
-        scalar_out = ctx.enter_context(tc.tile_pool(name="scalar_out", bufs=18))
-        psum = ctx.enter_context(tc.psum_pool(name="psum", bufs=8))
+        vector_out = ctx.enter_context(tc.tile_pool(name="vector_out", bufs=38))
+        scalar_out = ctx.enter_context(tc.tile_pool(name="scalar_out", bufs=14))
+        psum = ctx.enter_context(tc.psum_pool(name="psum", bufs=4))
 
         def held(name, shape, dtype):
             return keep.tile(shape, dtype, name=name, align_bytes=64)
@@ -68,6 +67,12 @@ def tile_picked_hub_silu_p_kernel(
         def load_words(g):
             nc.sync.dma_start(x_table[g][:].bitcast(I32), x_words[g].rearrange("p n t -> p (n t)").bitcast(I32))
 
+        def load_weights(name, w, g, c0, c1):
+            raw = held(name, [P, PACK, c1 - c0], F32)
+            w_rows = w[g * K_PASS : (g + 1) * K_PASS, c0:c1]
+            nc.sync.dma_start(raw[:], w_rows.rearrange("(p j) c -> p j c", j=PACK))
+            return raw
+
         nc.sync.dma_start(offs_sb[:], offs)
         nc.sync.dma_start(src_sb[:], src)
         nc.sync.dma_start(dst_sb[:], dst)
@@ -77,15 +82,10 @@ def tile_picked_hub_silu_p_kernel(
                 x_scales[:, 4 * q : 4 * q + 4, :].bitcast(I32),
             )
         load_words(0)
+        w1_raw0 = load_weights("w1_raw0", w1, 0, 0, H)
         load_words(1)
-        raw = []
-        for n in range(2 * TILES):
-            chunk = held(f"raw{n}", [P, PASSES, PACK, P], F32)
-            w, a = (w1, w2)[n % 2], n // 2
-            for g in range(PASSES):
-                rows = w[g * K_PASS : (g + 1) * K_PASS, a * P : (a + 1) * P]
-                nc.sync.dma_start(chunk[:, g], rows.rearrange("(p j) c -> p j c", j=PACK))
-            raw.append(chunk)
+        w1_raw1 = [load_weights(f"w1_raw1{c}", w1, 1, c, c + H // 2) for c in (0, H // 2)]
+        w2_raw = [load_weights(f"w2_raw{g}", w2, g, 0, H) for g in range(PASSES)]
         nc.sync.dma_start(w3_codes[:].bitcast(I32), w3_words[0].bitcast(I32))
         for q in range(4):
             nc.sync.dma_start(
@@ -101,24 +101,26 @@ def tile_picked_hub_silu_p_kernel(
             offsets = offs_sb[:, h * BANK // LIST : (h + 1) * BANK // LIST]
             nc.vector.tensor_copy(x_codes[g, h][:], x_table[g][:].indirect(offsets))
 
-        def cast(n, part):
-            grouped = by_scalar([P, part.stop - part.start, P, PACK], BF16)
-            nc.scalar.copy(
-                grouped[:].rearrange("p g (c i) j -> p g c j i", i=4),
-                raw[n][:, part].rearrange("p g j (c i) -> p g c j i", i=4),
+        def deal(copy, grouped, raw_cols, m0):
+            copy(
+                grouped[:, :, m0 : m0 + raw_cols.shape[2] // PACK, :].rearrange("p t m j -> p m j t"),
+                raw_cols.rearrange("p j (m t) -> p m j t", t=PACK),
             )
-            return grouped
 
-        def quantise(n, grouped):
-            passes = grouped.shape[1]
-            codes = by_vector([P, passes * P], U32)
-            plane = held(f"plane{n}_{passes}", [P, passes * P], U8)
-            nc.vector.quantize_mx(
-                out=codes[:].bitcast(FP8X4), scales=plane[:], in_=grouped[:].rearrange("p g c j -> p (g c j)")
-            )
-            return [(codes[:, g * P : (g + 1) * P], plane[:, g * P : (g + 1) * P]) for g in range(passes)]
+        def quantise(name, grouped, calls):
+            codes = by_vector([P, H], U32)
+            plane = held(name, [P, H], U8)
+            flat = grouped[:].rearrange("p t m j -> p (t m j)")
+            width = H // calls
+            for c in range(0, H, width):
+                nc.vector.quantize_mx(
+                    out=codes[:, c : c + width].bitcast(FP8X4),
+                    scales=plane[:, c : c + width],
+                    in_=flat[:, PACK * c : PACK * (c + width)],
+                )
+            return codes, plane
 
-        def multiply(weights):
+        def multiply(weights, t):
             banks = []
             for h in range(S // BANK):
                 cols = slice(h * BANK, (h + 1) * BANK)
@@ -126,8 +128,8 @@ def tile_picked_hub_silu_p_kernel(
                 for g in range(PASSES):
                     nc.tensor.matmul_mx(
                         out=bank[:],
-                        lhsT=weights[g][0].bitcast(FP8X4),
-                        lhsT_scale=weights[g][1],
+                        lhsT=weights[g][0][:, t * P : (t + 1) * P].bitcast(FP8X4),
+                        lhsT_scale=weights[g][1][:, t * P : (t + 1) * P],
                         rhs=x_codes[g, h][:].bitcast(FP8X4),
                         rhs_scale=x_plane[4 * g :, cols],
                         start=(g == 0),
@@ -136,67 +138,46 @@ def tile_picked_hub_silu_p_kernel(
                 banks.append(bank)
             return banks
 
-        starts = [sum(EDGE_PIECES[:i]) for i in range(len(EDGE_PIECES))]
-        zt = [held(f"zt{i}", [P, PACK * width], BF16) for i, width in enumerate(EDGE_PIECES)]
-
-        rows, picked = {}, {}
-
-        def empty(n, banks, copies):
-            rows[n] = by_scalar([P, S], F32)
+        def empty(banks, copies):
+            rows = by_scalar([P, S], F32)
             for h, bank in enumerate(banks):
-                copies[h](rows[n][:, h * BANK : (h + 1) * BANK], bank[:])
+                copies[h](rows[:, h * BANK : (h + 1) * BANK], bank[:])
+            return rows
 
-        def gather_edges(n, r0, width):
-            offsets = (src_sb, dst_sb)[n % 2][:, r0 // LIST : (r0 + width) // LIST]
+        def gather_edges(picked, rows, offsets, t, r0, width):
             tile = by_vector([P, width], F32)
-            nc.vector.tensor_copy(tile[:], rows[n][:].indirect(offsets))
+            nc.vector.tensor_copy(tile[:], rows[:].indirect(offsets[:, r0 // LIST : (r0 + width) // LIST]))
             for r in range(0, width, P):
-                picked[n, r0 + r] = tile[:, r : r + P]
+                picked[t, r0 + r] = tile[:, r : r + P]
 
-        def add(a, r0, width):
-            bank = next_bank()
-            for r in range(0, width, P):
-                for side in range(2):
-                    nc.tensor.matmul(
-                        bank[:, r : r + P],
-                        lhsT=picked[2 * a + side, r0 + r],
-                        rhs=ident[:],
-                        start=(side == 0),
-                        stop=(side == 1),
-                        is_transpose=True,
-                    )
-            return bank
+        def turn_into(bank, picked, t, r0, first, last):
+            for b in range(UNIT // P):
+                at = (t % 2) * UNIT + b * P
+                nc.tensor.matmul(
+                    bank[:, at : at + P],
+                    lhsT=picked[t, r0 + b * P],
+                    rhs=ident[:],
+                    start=(first and b == 0),
+                    stop=(last and b == UNIT // P - 1),
+                    is_transpose=True,
+                )
 
-        def activate(a, bank, r0, width):
-            for i, piece in enumerate(EDGE_PIECES):
-                if r0 <= starts[i] < r0 + width:
-                    view = zt[i][:].rearrange("q (u b p e) -> q u b p e", u=2, p=P, e=2)
-                    cols = bank[:, starts[i] - r0 : starts[i] - r0 + piece]
-                    nc.scalar.activation(
-                        view[:, :, :, 32 * a : 32 * (a + 1), :],
-                        cols.rearrange("q (b p u e) -> q u b p e", p=32, u=2, e=2),
-                        SILU,
-                    )
+        def activate_turned(zt, bank, u):
+            nc.scalar.activation(
+                zt[:, u * BANK : (u + 1) * BANK].rearrange("q (c e) -> q c e", e=2),
+                bank[:].rearrange("q (e c) -> q c e", e=2),
+                SILU,
+            )
 
         out_view = out.rearrange("(a p) r -> p a r", p=P)
 
-        def turn_back(i, r0, width):
+        def turn_back(zt):
             turned = next_bank()
-            for u in range(2):
-                for b in range(width // P):
-                    at = 2 * (u * EDGE_PIECES[i] + r0 - starts[i] + b * P)
-                    nc.tensor.transpose(
-                        turned[:, u * width + b * P : u * width + (b + 1) * P],
-                        zt[i][:, at : at + 2 * P].bitcast(F32),
-                        ident[:],
-                    )
-            return turned
-
-        def interleave(turned, width, on_vector):
-            z = (by_vector if on_vector else by_scalar)([P, PACK * width], BF16)
-            (nc.vector.tensor_copy if on_vector else nc.scalar.copy)(
-                z[:].bitcast(F32).rearrange("p (r u) -> p r u", u=2),
-                turned[:, : 2 * width].rearrange("p (u r) -> p r u", u=2),
+            for c in range(0, BANK, P):
+                nc.tensor.transpose(turned[:, c : c + P], zt[:, 2 * c : 2 * (c + P)].bitcast(F32), ident[:])
+            z = by_scalar([P, PACK * UNIT], BF16)
+            nc.scalar.copy(
+                z[:].bitcast(F32).rearrange("p (r u) -> p r u", u=2), turned[:].rearrange("p (u r) -> p r u", u=2)
             )
             return z
 
@@ -224,50 +205,79 @@ def tile_picked_hub_silu_p_kernel(
             )
             nc.sync.dma_start(out_view[:, :, r0 : r0 + width], result[:])
 
-        both = slice(0, PASSES)
         halves = range(0, S, BANK)
+        on_scalar = (nc.scalar.copy, nc.scalar.copy)
         gather_words(0, 0)
         gather_words(0, 1)
+        grouped = held("w1_grouped0", [P, PACK, P, PACK], BF16)
+        deal(nc.scalar.copy, grouped, w1_raw0[:, :, : H // 2], 0)
+        deal(nc.vector.tensor_copy, grouped, w1_raw0[:, :, H // 2 :], P // 2)
+        w1_q = [quantise("w1_plane0", grouped, 1)]
         gather_words(1, 0)
-        weights0 = quantise(0, cast(0, slice(0, 1))) + quantise(8, cast(0, slice(1, 2)))
         gather_words(1, 1)
-        sums = [multiply(weights0), multiply(quantise(1, cast(1, both)))]
-        empty(0, sums[0], (nc.scalar.copy, nc.vector.tensor_copy))
-        added = []
-        for n in range(2 * TILES - 2):
+        grouped = held("w1_grouped1", [P, PACK, P, PACK], BF16)
+        deal(nc.scalar.copy, grouped, w1_raw1[0][:], 0)
+        deal(nc.scalar.copy, grouped, w1_raw1[1][:, :, : H // 4], P // 2)
+        deal(nc.vector.tensor_copy, grouped, w1_raw1[1][:, :, H // 4 :], P // 2 + P // 4)
+        w1_q.append(quantise("w1_plane1", grouped, PACK))
+
+        early = range(0, BANK, UNIT)
+        y_at, e_at, sums, w2_q = {}, {}, {}, []
+        for t in range(PACK):
+            if t >= PACK - PASSES:
+                grouped = by_scalar([P, PACK, P, PACK], BF16)
+                deal(nc.scalar.copy, grouped, w2_raw[len(w2_q)][:], 0)
+                w2_q.append(quantise(f"w2_plane{t}", grouped, 1))
+            y_rows = empty(multiply(w1_q, t), (nc.scalar.copy, nc.vector.tensor_copy) if t == 0 else on_scalar)
             for r0 in halves:
-                gather_edges(n, r0, BANK)
-                if (n, r0) == (0, 0):
-                    sums.append(multiply(quantise(2, cast(2, both))))
-            if n % 2 == 1:
-                added.append([add(n // 2, r0, BANK) for r0 in halves])
-            if n + LEAD < 2 * TILES:
-                sums.append(multiply(quantise(n + LEAD, cast(n + LEAD, both))))
-            empty(n + 1, sums[n + 1], (nc.scalar.copy, nc.scalar.copy))
-            if n % 2 == 0 and n > 0:
-                for r0, bank in zip(halves, added[n // 2 - 1]):
-                    activate(n // 2 - 1, bank, r0, BANK)
-        empty(2 * TILES - 1, sums[-1], (nc.scalar.copy, nc.scalar.copy))
-        for r0, bank in zip(halves, added[-1]):
-            activate(TILES - 2, bank, r0, BANK)
+                gather_edges(y_at, y_rows, src_sb, t, r0, BANK)
+            for r0 in early:
+                if t % 2 == 0:
+                    sums[r0, t // 2] = psum.tile([P, BANK], F32, name="early_sum")
+                turn_into(sums[r0, t // 2], y_at, t, r0, t % 2 == 0, False)
+        e_rows = [empty(multiply(w2_q, t), on_scalar) for t in range(PACK)]
 
-        def last_tile(i):
-            for side in range(2):
-                gather_edges(2 * (TILES - 1) + side, starts[i], EDGE_PIECES[i])
-            activate(TILES - 1, add(TILES - 1, starts[i], EDGE_PIECES[i]), starts[i], EDGE_PIECES[i])
+        zt = {r0: held(f"zt{r0}", [P, PACK * UNIT], BF16) for r0 in range(0, TURNED_EDGES, UNIT)}
+        for t in range(PACK):
+            gather_edges(e_at, e_rows[t], dst_sb, t, 0, BANK)
+            for r0 in early:
+                turn_into(sums[r0, t // 2], e_at, t, r0, False, t % 2 == 1)
+                if t % 2 == 1:
+                    activate_turned(zt[r0], sums[r0, t // 2], t // 2)
+        z = {}
+        for t in range(PACK):
+            gather_edges(e_at, e_rows[t], dst_sb, t, BANK, UNIT)
+            if t % 2 == 0:
+                late_sum = next_bank()
+            turn_into(late_sum, y_at, t, BANK, t % 2 == 0, False)
+            turn_into(late_sum, e_at, t, BANK, False, t % 2 == 1)
+            if t % 2 == 1:
+                activate_turned(zt[BANK], late_sum, t // 2)
+                z[early[t // 2]] = turn_back(zt[early[t // 2]])
 
-        last_tile(0)
-        last_tile(1)
-        t0 = turn_back(0, 0, 256)
-        t1 = turn_back(0, 256, 256)
-        z0 = interleave(t0, 256, False)
-        last_tile(2)
-        last_tile(3)
-        z1 = interleave(t1, 256, True)
-        z2 = interleave(turn_back(1, 512, 256), 256, False)
-        z3 = interleave(turn_back(2, 768, 128), 128, False)
-        z4 = interleave(turn_back(3, 896, 128), 128, False)
-        units = [(z0, 0, 256), (z1, 256, 256), (z2, 512, 256), (z3, 768, 128), (z4, 896, 128)]
-        results = [last_product(*unit) for unit in units]
-        for i, res in enumerate(results):
-            store(res, units[i][1], units[i][2], i % 2 == 1)
+        def add_gathered(r0):
+            total = by_vector([P, PACK, TAIL], F32)
+            for t in range(PACK):
+                offsets = dst_sb[:, r0 // LIST : (r0 + TAIL) // LIST]
+                nc.vector.tensor_tensor(total[:, t, :], e_rows[t][:].indirect(offsets), y_at[t, r0], ADD)
+            values = by_scalar([P, PACK * TAIL], BF16)
+            nc.scalar.activation(
+                values[:].rearrange("p (c i t) -> p c t i", i=4, t=PACK),
+                total[:].rearrange("p t (c i) -> p c t i", i=4),
+                SILU,
+            )
+            return values
+
+        z[768] = add_gathered(768)
+        res0 = last_product(z[0], 0, UNIT)
+        z[BANK] = turn_back(zt[BANK])
+        store(res0, 0, UNIT, False)
+        z[896] = add_gathered(896)
+        res1 = last_product(z[256], 256, UNIT)
+        res2 = last_product(z[512], 512, UNIT)
+        res3 = last_product(z[768], 768, TAIL)
+        res4 = last_product(z[896], 896, TAIL)
+        store(res1, 256, UNIT, True)
+        store(res2, 512, UNIT, False)
+        store(res3, 768, TAIL, True)
+        store(res4, 896, TAIL, False)

@@ -21,11 +21,15 @@ P = 128
 PACK = 4
 K_PASS = P * PACK
 PASSES = K // K_PASS
+QUADRANTS = 4
 BANK = 512
 LIST = 16
 UNIT = 256
-TURNED_EDGES = 768
 TAIL = 128
+TURNED_EDGES = S - 2 * TAIL
+VECTOR_TILES = 33
+SCALAR_TILES = 18
+RING_BANKS = 4
 
 
 def tile_picked_hub_silu_p_kernel(
@@ -35,9 +39,9 @@ def tile_picked_hub_silu_p_kernel(
     with ExitStack() as ctx:
         lists = ctx.enter_context(tc.tile_pool(name="lists", bufs=1))
         keep = ctx.enter_context(tc.tile_pool(name="keep", bufs=1))
-        vector_out = ctx.enter_context(tc.tile_pool(name="vector_out", bufs=38))
-        scalar_out = ctx.enter_context(tc.tile_pool(name="scalar_out", bufs=14))
-        psum = ctx.enter_context(tc.psum_pool(name="psum", bufs=4))
+        vector_out = ctx.enter_context(tc.tile_pool(name="vector_out", bufs=VECTOR_TILES))
+        scalar_out = ctx.enter_context(tc.tile_pool(name="scalar_out", bufs=SCALAR_TILES))
+        psum = ctx.enter_context(tc.psum_pool(name="psum", bufs=RING_BANKS))
 
         def held(name, shape, dtype):
             return keep.tile(shape, dtype, name=name, align_bytes=64)
@@ -51,15 +55,18 @@ def tile_picked_hub_silu_p_kernel(
         def next_bank():
             return psum.tile([P, BANK], F32, name="bank")
 
+        def entries(list_tile, r0, width):
+            return list_tile[:, r0 // LIST : (r0 + width) // LIST]
+
         offs_sb = lists.tile([P, S // LIST], U16, name="offs_sb")
         src_sb = lists.tile([P, S // LIST], U16, name="src_sb")
         dst_sb = lists.tile([P, S // LIST], U16, name="dst_sb")
 
         x_table = [held(f"x_table{g}", [P, T], U32) for g in range(PASSES)]
-        xs_table = held("xs_table", [P, T], U8)
+        x_scale_table = held("x_scale_table", [P, T], U8)
         w3_codes = held("w3_codes", [P, 2 * N], U8)
         w3_plane = held("w3_plane", [P, N], U8)
-        nc.gpsimd.memset(xs_table[:].bitcast(I32), 0)
+        nc.gpsimd.memset(x_scale_table[:].bitcast(I32), 0)
         nc.gpsimd.memset(w3_plane[:].bitcast(I32), 0)
         ident = held("ident", [P, P], F32)
         make_identity(nc, ident[:])
@@ -76,9 +83,9 @@ def tile_picked_hub_silu_p_kernel(
         nc.sync.dma_start(offs_sb[:], offs)
         nc.sync.dma_start(src_sb[:], src)
         nc.sync.dma_start(dst_sb[:], dst)
-        for q in range(4):
+        for q in range(QUADRANTS):
             nc.sync.dma_start(
-                xs_table[32 * q : 32 * q + 4 * PASSES, :].bitcast(I32),
+                x_scale_table[32 * q : 32 * q + 4 * PASSES, :].bitcast(I32),
                 x_scales[:, 4 * q : 4 * q + 4, :].bitcast(I32),
             )
         load_words(0)
@@ -87,30 +94,31 @@ def tile_picked_hub_silu_p_kernel(
         w1_raw1 = [load_weights(f"w1_raw1{c}", w1, 1, c, c + H // 2) for c in (0, H // 2)]
         w2_raw = [load_weights(f"w2_raw{g}", w2, g, 0, H) for g in range(PASSES)]
         nc.sync.dma_start(w3_codes[:].bitcast(I32), w3_words[0].bitcast(I32))
-        for q in range(4):
+        for q in range(QUADRANTS):
             nc.sync.dma_start(
                 w3_plane[32 * q : 32 * q + 4, :].bitcast(I32), w3_scales[0, 4 * q : 4 * q + 4, :].bitcast(I32)
             )
 
         x_codes = {}
         x_plane = held("x_plane", [P, S], U8)
-        nc.vector.tensor_copy(x_plane[:], xs_table[:].indirect(offs_sb[:]))
+        nc.vector.tensor_copy(x_plane[:], x_scale_table[:].indirect(offs_sb[:]))
 
-        def gather_words(g, h):
-            x_codes[g, h] = by_vector([P, BANK], U32)
-            offsets = offs_sb[:, h * BANK // LIST : (h + 1) * BANK // LIST]
-            nc.vector.tensor_copy(x_codes[g, h][:], x_table[g][:].indirect(offsets))
+        def gather_words(g):
+            for r0 in range(0, S, BANK):
+                x_codes[g, r0] = by_vector([P, BANK], U32)
+                nc.vector.tensor_copy(x_codes[g, r0][:], x_table[g][:].indirect(entries(offs_sb, r0, BANK)))
 
-        def deal(copy, grouped, raw_cols, m0):
+        def deal(copy, dealt, raw_cols, c0):
+            m0, m1 = c0 // PACK, (c0 + raw_cols.shape[2]) // PACK
             copy(
-                grouped[:, :, m0 : m0 + raw_cols.shape[2] // PACK, :].rearrange("p t m j -> p m j t"),
-                raw_cols.rearrange("p j (m t) -> p m j t", t=PACK),
+                dealt[:, :, m0:m1, :].rearrange("p (u e) m j -> p u m j e", e=2),
+                raw_cols.rearrange("p j (m u e) -> p u m j e", u=2, e=2),
             )
 
-        def quantise(name, grouped, calls):
+        def quantise_weights(name, dealt, calls):
             codes = by_vector([P, H], U32)
             plane = held(name, [P, H], U8)
-            flat = grouped[:].rearrange("p t m j -> p (t m j)")
+            flat = dealt[:].rearrange("p t m j -> p (t m j)")
             width = H // calls
             for c in range(0, H, width):
                 nc.vector.quantize_mx(
@@ -120,75 +128,73 @@ def tile_picked_hub_silu_p_kernel(
                 )
             return codes, plane
 
-        def multiply(weights, t):
+        def hidden_rows(weights, t, second_copy):
             banks = []
-            for h in range(S // BANK):
-                cols = slice(h * BANK, (h + 1) * BANK)
+            for r0 in range(0, S, BANK):
                 bank = next_bank()
-                for g in range(PASSES):
+                for g, (codes, plane) in enumerate(weights):
                     nc.tensor.matmul_mx(
                         out=bank[:],
-                        lhsT=weights[g][0][:, t * P : (t + 1) * P].bitcast(FP8X4),
-                        lhsT_scale=weights[g][1][:, t * P : (t + 1) * P],
-                        rhs=x_codes[g, h][:].bitcast(FP8X4),
-                        rhs_scale=x_plane[4 * g :, cols],
+                        lhsT=codes[:, t * P : (t + 1) * P].bitcast(FP8X4),
+                        lhsT_scale=plane[:, t * P : (t + 1) * P],
+                        rhs=x_codes[g, r0][:].bitcast(FP8X4),
+                        rhs_scale=x_plane[4 * g :, r0 : r0 + BANK],
                         start=(g == 0),
                         stop=(g == PASSES - 1),
                     )
                 banks.append(bank)
-            return banks
-
-        def empty(banks, copies):
             rows = by_scalar([P, S], F32)
-            for h, bank in enumerate(banks):
-                copies[h](rows[:, h * BANK : (h + 1) * BANK], bank[:])
+            nc.scalar.copy(rows[:, :BANK], banks[0][:])
+            second_copy(rows[:, BANK:], banks[1][:])
             return rows
 
-        def gather_edges(picked, rows, offsets, t, r0, width):
-            tile = by_vector([P, width], F32)
-            nc.vector.tensor_copy(tile[:], rows[:].indirect(offsets[:, r0 // LIST : (r0 + width) // LIST]))
+        def gather_edges(picked, rows, list_tile, t, r0, width):
+            columns = by_vector([P, width], F32)
+            nc.vector.tensor_copy(columns[:], rows[:].indirect(entries(list_tile, r0, width)))
             for r in range(0, width, P):
-                picked[t, r0 + r] = tile[:, r : r + P]
+                picked[t, r0 + r] = columns[:, r : r + P]
 
-        def turn_into(bank, picked, t, r0, first, last):
+        def turn_into(bank, picked, t, r0, opens, closes):
             for b in range(UNIT // P):
                 at = (t % 2) * UNIT + b * P
                 nc.tensor.matmul(
                     bank[:, at : at + P],
                     lhsT=picked[t, r0 + b * P],
                     rhs=ident[:],
-                    start=(first and b == 0),
-                    stop=(last and b == UNIT // P - 1),
+                    start=(opens and b == 0),
+                    stop=(closes and b == UNIT // P - 1),
                     is_transpose=True,
                 )
 
-        def activate_turned(zt, bank, u):
+        def activate_turned(z_turned, bank, u):
             nc.scalar.activation(
-                zt[:, u * BANK : (u + 1) * BANK].rearrange("q (c e) -> q c e", e=2),
+                z_turned[:, u * BANK : (u + 1) * BANK].rearrange("q (c e) -> q c e", e=2),
                 bank[:].rearrange("q (e c) -> q c e", e=2),
                 SILU,
             )
 
         out_view = out.rearrange("(a p) r -> p a r", p=P)
 
-        def turn_back(zt):
-            turned = next_bank()
+        def turn_back(z_turned):
+            bank = next_bank()
             for c in range(0, BANK, P):
-                nc.tensor.transpose(turned[:, c : c + P], zt[:, 2 * c : 2 * (c + P)].bitcast(F32), ident[:])
-            z = by_scalar([P, PACK * UNIT], BF16)
+                nc.tensor.transpose(bank[:, c : c + P], z_turned[:, 2 * c : 2 * (c + P)].bitcast(F32), ident[:])
+            z_values = by_scalar([P, PACK * UNIT], BF16)
             nc.scalar.copy(
-                z[:].bitcast(F32).rearrange("p (r u) -> p r u", u=2), turned[:].rearrange("p (u r) -> p r u", u=2)
+                z_values[:].bitcast(F32).rearrange("p (r u) -> p r u", u=2),
+                bank[:].rearrange("p (u r) -> p r u", u=2),
             )
-            return z
+            return z_values
 
-        def last_product(z, r0, width):
+        def last_product(z_values, r0):
+            width = z_values.shape[1] // PACK
             z_codes = by_vector([P, width], U32)
             z_plane = held(f"z_plane{r0}", [P, width], U8)
-            nc.vector.quantize_mx(out=z_codes[:].bitcast(FP8X4), scales=z_plane[:], in_=z[:])
-            res = next_bank()
+            nc.vector.quantize_mx(out=z_codes[:].bitcast(FP8X4), scales=z_plane[:], in_=z_values[:])
+            bank = next_bank()
             for a in range(N // P):
                 nc.tensor.matmul_mx(
-                    out=res[:, a * width : (a + 1) * width],
+                    out=bank[:, a * width : (a + 1) * width],
                     lhsT=w3_codes[:, 2 * a * P : 2 * (a + 1) * P].bitcast(FP4X4),
                     lhsT_scale=w3_plane[:, a * P : (a + 1) * P],
                     rhs=z_codes[:].bitcast(FP8X4),
@@ -196,54 +202,49 @@ def tile_picked_hub_silu_p_kernel(
                     start=True,
                     stop=True,
                 )
-            return res
+            return bank[:, : N // P * width].rearrange("p (a r) -> p a r", a=N // P)
 
-        def store(res, r0, width, on_vector):
-            result = (by_vector if on_vector else by_scalar)([P, N // P, width], F32)
-            (nc.vector.tensor_copy if on_vector else nc.scalar.copy)(
-                result[:], res[:, : 2 * width].rearrange("p (a r) -> p a r", a=N // P)
-            )
-            nc.sync.dma_start(out_view[:, :, r0 : r0 + width], result[:])
+        def store(product, r0, new_tile, copy):
+            result = new_tile(list(product.shape), F32)
+            copy(result[:], product)
+            nc.sync.dma_start(out_view[:, :, r0 : r0 + product.shape[2]], result[:])
 
-        halves = range(0, S, BANK)
-        on_scalar = (nc.scalar.copy, nc.scalar.copy)
-        gather_words(0, 0)
-        gather_words(0, 1)
-        grouped = held("w1_grouped0", [P, PACK, P, PACK], BF16)
-        deal(nc.scalar.copy, grouped, w1_raw0[:, :, : H // 2], 0)
-        deal(nc.vector.tensor_copy, grouped, w1_raw0[:, :, H // 2 :], P // 2)
-        w1_q = [quantise("w1_plane0", grouped, 1)]
-        gather_words(1, 0)
-        gather_words(1, 1)
-        grouped = held("w1_grouped1", [P, PACK, P, PACK], BF16)
-        deal(nc.scalar.copy, grouped, w1_raw1[0][:], 0)
-        deal(nc.scalar.copy, grouped, w1_raw1[1][:, :, : H // 4], P // 2)
-        deal(nc.vector.tensor_copy, grouped, w1_raw1[1][:, :, H // 4 :], P // 2 + P // 4)
-        w1_q.append(quantise("w1_plane1", grouped, PACK))
+        gather_words(0)
+        dealt = held("w1_dealt0", [P, PACK, P, PACK], BF16)
+        deal(nc.scalar.copy, dealt, w1_raw0[:, :, : H // 2], 0)
+        deal(nc.vector.tensor_copy, dealt, w1_raw0[:, :, H // 2 :], H // 2)
+        w1_mx = [quantise_weights("w1_plane0", dealt, 1)]
+        gather_words(1)
+        dealt = held("w1_dealt1", [P, PACK, P, PACK], BF16)
+        deal(nc.scalar.copy, dealt, w1_raw1[0][:], 0)
+        deal(nc.scalar.copy, dealt, w1_raw1[1][:, :, : H // 4], H // 2)
+        deal(nc.vector.tensor_copy, dealt, w1_raw1[1][:, :, H // 4 :], H // 2 + H // 4)
+        w1_mx.append(quantise_weights("w1_plane1", dealt, PACK))
 
         early = range(0, BANK, UNIT)
-        y_at, e_at, sums, w2_q = {}, {}, {}, []
+        y_at, e_at, sums, w2_mx = {}, {}, {}, []
         for t in range(PACK):
             if t >= PACK - PASSES:
-                grouped = by_scalar([P, PACK, P, PACK], BF16)
-                deal(nc.scalar.copy, grouped, w2_raw[len(w2_q)][:], 0)
-                w2_q.append(quantise(f"w2_plane{t}", grouped, 1))
-            y_rows = empty(multiply(w1_q, t), (nc.scalar.copy, nc.vector.tensor_copy) if t == 0 else on_scalar)
-            for r0 in halves:
+                dealt = by_scalar([P, PACK, P, PACK], BF16)
+                deal(nc.scalar.copy, dealt, w2_raw[len(w2_mx)][:], 0)
+                w2_mx.append(quantise_weights(f"w2_plane{len(w2_mx)}", dealt, 1))
+            y_rows = hidden_rows(w1_mx, t, nc.vector.tensor_copy if t == 0 else nc.scalar.copy)
+            for r0 in range(0, S, BANK):
                 gather_edges(y_at, y_rows, src_sb, t, r0, BANK)
             for r0 in early:
                 if t % 2 == 0:
                     sums[r0, t // 2] = psum.tile([P, BANK], F32, name="early_sum")
                 turn_into(sums[r0, t // 2], y_at, t, r0, t % 2 == 0, False)
-        e_rows = [empty(multiply(w2_q, t), on_scalar) for t in range(PACK)]
+        e_rows = [hidden_rows(w2_mx, t, nc.scalar.copy) for t in range(PACK)]
 
-        zt = {r0: held(f"zt{r0}", [P, PACK * UNIT], BF16) for r0 in range(0, TURNED_EDGES, UNIT)}
+        z_turned = {r0: held(f"z_turned{r0}", [P, PACK * UNIT], BF16) for r0 in range(0, TURNED_EDGES, UNIT)}
         for t in range(PACK):
             gather_edges(e_at, e_rows[t], dst_sb, t, 0, BANK)
             for r0 in early:
                 turn_into(sums[r0, t // 2], e_at, t, r0, False, t % 2 == 1)
                 if t % 2 == 1:
-                    activate_turned(zt[r0], sums[r0, t // 2], t // 2)
+                    activate_turned(z_turned[r0], sums[r0, t // 2], t // 2)
+
         z = {}
         for t in range(PACK):
             gather_edges(e_at, e_rows[t], dst_sb, t, BANK, UNIT)
@@ -252,32 +253,34 @@ def tile_picked_hub_silu_p_kernel(
             turn_into(late_sum, y_at, t, BANK, t % 2 == 0, False)
             turn_into(late_sum, e_at, t, BANK, False, t % 2 == 1)
             if t % 2 == 1:
-                activate_turned(zt[BANK], late_sum, t // 2)
-                z[early[t // 2]] = turn_back(zt[early[t // 2]])
+                activate_turned(z_turned[BANK], late_sum, t // 2)
+                z[early[t // 2]] = turn_back(z_turned[early[t // 2]])
 
         def add_gathered(r0):
             total = by_vector([P, PACK, TAIL], F32)
             for t in range(PACK):
-                offsets = dst_sb[:, r0 // LIST : (r0 + TAIL) // LIST]
-                nc.vector.tensor_tensor(total[:, t, :], e_rows[t][:].indirect(offsets), y_at[t, r0], ADD)
-            values = by_scalar([P, PACK * TAIL], BF16)
+                e_side = e_rows[t][:].indirect(entries(dst_sb, r0, TAIL))
+                nc.vector.tensor_tensor(total[:, t, :], e_side, y_at[t, r0], ADD)
+            z_values = by_scalar([P, PACK * TAIL], BF16)
             nc.scalar.activation(
-                values[:].rearrange("p (c i t) -> p c t i", i=4, t=PACK),
+                z_values[:].rearrange("p (c i t) -> p c t i", i=4, t=PACK),
                 total[:].rearrange("p t (c i) -> p c t i", i=4),
                 SILU,
             )
-            return values
+            return z_values
 
-        z[768] = add_gathered(768)
-        res0 = last_product(z[0], 0, UNIT)
-        z[BANK] = turn_back(zt[BANK])
-        store(res0, 0, UNIT, False)
-        z[896] = add_gathered(896)
-        res1 = last_product(z[256], 256, UNIT)
-        res2 = last_product(z[512], 512, UNIT)
-        res3 = last_product(z[768], 768, TAIL)
-        res4 = last_product(z[896], 896, TAIL)
-        store(res1, 256, UNIT, True)
-        store(res2, 512, UNIT, False)
-        store(res3, 768, TAIL, True)
-        store(res4, 896, TAIL, False)
+        on_scalar = (by_scalar, nc.scalar.copy)
+        on_vector = (by_vector, nc.vector.tensor_copy)
+        first_tail, second_tail = TURNED_EDGES, TURNED_EDGES + TAIL
+        z[first_tail] = add_gathered(first_tail)
+        product = {0: last_product(z[0], 0)}
+        z[BANK] = turn_back(z_turned[BANK])
+        store(product[0], 0, *on_scalar)
+        z[second_tail] = add_gathered(second_tail)
+        for r0 in (UNIT, BANK, first_tail):
+            product[r0] = last_product(z[r0], r0)
+        store(product[UNIT], UNIT, *on_vector)
+        product[second_tail] = last_product(z[second_tail], second_tail)
+        store(product[BANK], BANK, *on_scalar)
+        store(product[first_tail], first_tail, *on_vector)
+        store(product[second_tail], second_tail, *on_scalar)

@@ -1,7 +1,6 @@
 from contextlib import ExitStack
 
 import concourse.mybir as mybir
-from concourse.masks import make_identity
 
 K, T, S, H, N = 1024, 2048, 1024, 512, 256
 FLOPS = 2 * (2 * K * H * S + H * N * S)
@@ -15,6 +14,7 @@ U8 = mybir.dt.uint8
 FP8X4 = mybir.dt.float8_e4m3fn_x4
 FP4X4 = mybir.dt.float4_e2m1fn_x4
 ADD = mybir.AluOpType.add
+MULT = mybir.AluOpType.mult
 SILU = mybir.ActivationFunctionType.Silu
 
 P = 128
@@ -24,12 +24,9 @@ PASSES = K // K_PASS
 QUADRANTS = 4
 BANK = 512
 LIST = 16
-UNIT = 256
-TAIL = 128
-TURNED_EDGES = S - 2 * TAIL
-VECTOR_TILES = 33
-SCALAR_TILES = 18
-RING_BANKS = 4
+VECTOR_TILES = 22
+SCALAR_TILES = 19
+EARLY_TILES = 2
 
 
 def tile_picked_hub_silu_p_kernel(
@@ -41,7 +38,7 @@ def tile_picked_hub_silu_p_kernel(
         keep = ctx.enter_context(tc.tile_pool(name="keep", bufs=1))
         vector_out = ctx.enter_context(tc.tile_pool(name="vector_out", bufs=VECTOR_TILES))
         scalar_out = ctx.enter_context(tc.tile_pool(name="scalar_out", bufs=SCALAR_TILES))
-        psum = ctx.enter_context(tc.psum_pool(name="psum", bufs=RING_BANKS))
+        psum = ctx.enter_context(tc.psum_pool(name="psum", bufs=4))
 
         def held(name, shape, dtype):
             return keep.tile(shape, dtype, name=name, align_bytes=64)
@@ -68,8 +65,6 @@ def tile_picked_hub_silu_p_kernel(
         w3_plane = held("w3_plane", [P, N], U8)
         nc.gpsimd.memset(x_scale_table[:].bitcast(I32), 0)
         nc.gpsimd.memset(w3_plane[:].bitcast(I32), 0)
-        ident = held("ident", [P, P], F32)
-        make_identity(nc, ident[:])
 
         def load_words(g):
             nc.sync.dma_start(x_table[g][:].bitcast(I32), x_words[g].rearrange("p n t -> p (n t)").bitcast(I32))
@@ -81,206 +76,210 @@ def tile_picked_hub_silu_p_kernel(
             return raw
 
         nc.sync.dma_start(offs_sb[:], offs)
-        nc.sync.dma_start(src_sb[:], src)
-        nc.sync.dma_start(dst_sb[:], dst)
+        load_words(0)
         for q in range(QUADRANTS):
             nc.sync.dma_start(
                 x_scale_table[32 * q : 32 * q + 4 * PASSES, :].bitcast(I32),
                 x_scales[:, 4 * q : 4 * q + 4, :].bitcast(I32),
             )
-        load_words(0)
         w1_raw0 = load_weights("w1_raw0", w1, 0, 0, H)
         load_words(1)
         w1_raw1 = [load_weights(f"w1_raw1{c}", w1, 1, c, c + H // 2) for c in (0, H // 2)]
+        nc.sync.dma_start(src_sb[:], src)
         w2_raw = [load_weights(f"w2_raw{g}", w2, g, 0, H) for g in range(PASSES)]
+        nc.sync.dma_start(dst_sb[:], dst)
         nc.sync.dma_start(w3_codes[:].bitcast(I32), w3_words[0].bitcast(I32))
         for q in range(QUADRANTS):
             nc.sync.dma_start(
                 w3_plane[32 * q : 32 * q + 4, :].bitcast(I32), w3_scales[0, 4 * q : 4 * q + 4, :].bitcast(I32)
             )
 
-        x_codes = {}
-        x_plane = held("x_plane", [P, S], U8)
-        nc.vector.tensor_copy(x_plane[:], x_scale_table[:].indirect(offs_sb[:]))
-
-        def gather_words(g):
+        def gather_halves(dtype, table, list_tile):
+            picked = by_vector([P, S], dtype)
             for r0 in range(0, S, BANK):
-                x_codes[g, r0] = by_vector([P, BANK], U32)
-                nc.vector.tensor_copy(x_codes[g, r0][:], x_table[g][:].indirect(entries(offs_sb, r0, BANK)))
+                nc.vector.tensor_copy(picked[:, r0 : r0 + BANK], table[:].indirect(entries(list_tile, r0, BANK)))
+            return picked
 
-        def deal(copy, dealt, raw_cols, c0):
+        def gather_words(g, b):
+            x_codes[g, b] = by_vector([P, BANK], U32)
+            nc.vector.tensor_copy(x_codes[g, b][:], x_table[g][:].indirect(entries(offs_sb, b * BANK, BANK)))
+
+        def deal(copy, dealt, raw_cols, c0, u):
             m0, m1 = c0 // PACK, (c0 + raw_cols.shape[2]) // PACK
             copy(
-                dealt[:, :, m0:m1, :].rearrange("p (u e) m j -> p u m j e", e=2),
-                raw_cols.rearrange("p j (m u e) -> p u m j e", u=2, e=2),
+                dealt[u][:, :, m0:m1, :].rearrange("p e m j -> p m j e"),
+                raw_cols.rearrange("p j (m t) -> p m j t", t=PACK)[:, :, :, 2 * u : 2 * u + 2],
             )
 
-        def quantise_weights(name, dealt, calls):
-            codes = by_vector([P, H], U32)
-            plane = held(name, [P, H], U8)
+        def quantise_weights(mx, name, g, dealt, t0, calls):
             flat = dealt[:].rearrange("p t m j -> p (t m j)")
-            width = H // calls
-            for c in range(0, H, width):
+            columns = flat.shape[1] // PACK
+            codes = by_vector([P, columns], U32)
+            plane = held(name, [P, columns], U8)
+            width = columns // calls
+            for c in range(0, columns, width):
                 nc.vector.quantize_mx(
                     out=codes[:, c : c + width].bitcast(FP8X4),
                     scales=plane[:, c : c + width],
                     in_=flat[:, PACK * c : PACK * (c + width)],
                 )
-            return codes, plane
+            for c in range(0, columns, P):
+                mx[g, t0 + c // P] = (codes[:, c : c + P], plane[:, c : c + P])
 
-        def hidden_rows(weights, t, second_copy):
-            banks = []
-            for r0 in range(0, S, BANK):
-                bank = next_bank()
-                for g, (codes, plane) in enumerate(weights):
-                    nc.tensor.matmul_mx(
-                        out=bank[:],
-                        lhsT=codes[:, t * P : (t + 1) * P].bitcast(FP8X4),
-                        lhsT_scale=plane[:, t * P : (t + 1) * P],
-                        rhs=x_codes[g, r0][:].bitcast(FP8X4),
-                        rhs_scale=x_plane[4 * g :, r0 : r0 + BANK],
-                        start=(g == 0),
-                        stop=(g == PASSES - 1),
-                    )
-                banks.append(bank)
+        x_codes = {}
+
+        def hidden_pass(banks, weights, t, g):
+            codes, plane = weights[g, t]
+            for b, bank in enumerate(banks):
+                nc.tensor.matmul_mx(
+                    out=bank[:],
+                    lhsT=codes.bitcast(FP8X4),
+                    lhsT_scale=plane,
+                    rhs=x_codes[g, b][:].bitcast(FP8X4),
+                    rhs_scale=x_plane[4 * g :, b * BANK : (b + 1) * BANK],
+                    start=(g == 0),
+                    stop=(g == PASSES - 1),
+                )
+
+        def rows_out(banks, second_copy):
             rows = by_scalar([P, S], F32)
             nc.scalar.copy(rows[:, :BANK], banks[0][:])
             second_copy(rows[:, BANK:], banks[1][:])
             return rows
 
-        def gather_edges(picked, rows, list_tile, t, r0, width):
-            columns = by_vector([P, width], F32)
-            nc.vector.tensor_copy(columns[:], rows[:].indirect(entries(list_tile, r0, width)))
-            for r in range(0, width, P):
-                picked[t, r0 + r] = columns[:, r : r + P]
+        def two_banks():
+            return [psum.tile([P, BANK], F32, name="hidden_bank") for b in range(S // BANK)]
 
-        def turn_into(bank, picked, t, r0, opens, closes):
-            for b in range(UNIT // P):
-                at = (t % 2) * UNIT + b * P
-                nc.tensor.matmul(
-                    bank[:, at : at + P],
-                    lhsT=picked[t, r0 + b * P],
-                    rhs=ident[:],
-                    start=(opens and b == 0),
-                    stop=(closes and b == UNIT // P - 1),
-                    is_transpose=True,
-                )
+        gather_words(0, 0)
+        gather_words(0, 1)
+        x_plane = by_vector([P, S], U8)
+        nc.vector.tensor_copy(x_plane[:], x_scale_table[:].indirect(offs_sb[:]))
+        dealt = [held(f"w1_dealt0{u}", [P, 2, P, PACK], BF16) for u in range(2)]
+        deal(nc.scalar.copy, dealt, w1_raw0[:], 0, 0)
+        deal(nc.scalar.copy, dealt, w1_raw0[:], 0, 1)
+        w1_mx = {}
+        quantise_weights(w1_mx, "w1_plane0a", 0, dealt[0], 0, 1)
+        gather_words(1, 0)
+        late_pair = dealt[1]
+        y_banks = {}
+        for t in range(EARLY_TILES):
+            y_banks[t] = two_banks()
+            hidden_pass(y_banks[t], w1_mx, t, 0)
+        gather_words(1, 1)
+        dealt = [held(f"w1_dealt1{u}", [P, 2, P, PACK], BF16) for u in range(2)]
+        deal(nc.scalar.copy, dealt, w1_raw1[0][:], 0, 0)
+        deal(nc.scalar.copy, dealt, w1_raw1[0][:], 0, 1)
+        deal(nc.scalar.copy, dealt, w1_raw1[1][:], H // 2, 0)
+        deal(nc.scalar.copy, dealt, w1_raw1[1][:], H // 2, 1)
+        quantise_weights(w1_mx, "w1_plane1a", 1, dealt[0], 0, 2)
+        quantise_weights(w1_mx, "w1_plane0b", 0, late_pair, 2, 1)
+        quantise_weights(w1_mx, "w1_plane1b", 1, dealt[1], 2, 1)
 
-        def activate_turned(z_turned, bank, u):
+        y_at, w2_dealt, w2_mx = [], [], {}
+        for t in range(PACK):
+            if t >= EARLY_TILES:
+                y_banks[t] = two_banks()
+                hidden_pass(y_banks[t], w1_mx, t, 0)
+            hidden_pass(y_banks[t], w1_mx, t, 1)
+            y_rows = rows_out(y_banks[t], nc.vector.tensor_copy if t == 0 else nc.scalar.copy)
+            if t >= PACK - PASSES:
+                g = t - (PACK - PASSES)
+                quantise_weights(w2_mx, f"w2_plane{g}", g, w2_dealt[g], 0, 1)
+            y_at.append(gather_halves(F32, y_rows, src_sb))
+            if 1 <= t <= PASSES:
+                dealt = by_scalar([P, PACK, P, PACK], BF16)
+                for u in range(2):
+                    deal(nc.scalar.copy, [dealt[:, :2], dealt[:, 2:]], w2_raw[t - 1][:], 0, u)
+                w2_dealt.append(dealt)
+
+        e_rows = []
+        for t in range(PACK):
+            banks = two_banks()
+            for g in range(PASSES):
+                hidden_pass(banks, w2_mx, t, g)
+            e_rows.append(rows_out(banks, nc.scalar.copy))
+
+        def add_gathered(total, t, r0):
+            width = total.shape[2]
+            e_side = e_rows[t][:].indirect(entries(dst_sb, r0, width))
+            nc.vector.tensor_tensor(total[:, t, :], e_side, y_at[t][:, r0 : r0 + width], ADD)
+
+        def sums(r0, width):
+            total = by_vector([P, PACK, width], F32)
+            for t in range(PACK):
+                add_gathered(total, t, r0)
+            return total
+
+        def activate(z_values, total):
             nc.scalar.activation(
-                z_turned[:, u * BANK : (u + 1) * BANK].rearrange("q (c e) -> q c e", e=2),
-                bank[:].rearrange("q (e c) -> q c e", e=2),
+                z_values.rearrange("p (c i t) -> p c t i", i=4, t=PACK),
+                total[:].rearrange("p t (c i) -> p c t i", i=4),
                 SILU,
             )
 
-        out_view = out.rearrange("(a p) r -> p a r", p=P)
-
-        def turn_back(z_turned):
-            bank = next_bank()
-            for c in range(0, BANK, P):
-                nc.tensor.transpose(bank[:, c : c + P], z_turned[:, 2 * c : 2 * (c + P)].bitcast(F32), ident[:])
-            z_values = by_scalar([P, PACK * UNIT], BF16)
-            nc.scalar.copy(
-                z_values[:].bitcast(F32).rearrange("p (r u) -> p r u", u=2),
-                bank[:].rearrange("p (u r) -> p r u", u=2),
-            )
+        def activated(total):
+            z_values = by_scalar([P, PACK * total.shape[2]], BF16)
+            activate(z_values[:], total)
             return z_values
 
-        def last_product(z_values, r0):
+        out_view = out.rearrange("(a p) r -> p a r", p=P)
+
+        def quantise_z(z_values, r0):
             width = z_values.shape[1] // PACK
             z_codes = by_vector([P, width], U32)
             z_plane = held(f"z_plane{r0}", [P, width], U8)
             nc.vector.quantize_mx(out=z_codes[:].bitcast(FP8X4), scales=z_plane[:], in_=z_values[:])
+            return z_codes, z_plane
+
+        def multiply(into, a, z_mx):
+            nc.tensor.matmul_mx(
+                out=into,
+                lhsT=w3_codes[:, 2 * a * P : 2 * (a + 1) * P].bitcast(FP4X4),
+                lhsT_scale=w3_plane[:, a * P : (a + 1) * P],
+                rhs=z_mx[0][:].bitcast(FP8X4),
+                rhs_scale=z_mx[1][:],
+                start=True,
+                stop=True,
+            )
+
+        def product(z_mx):
+            width = z_mx[0].shape[1]
             bank = next_bank()
             for a in range(N // P):
-                nc.tensor.matmul_mx(
-                    out=bank[:, a * width : (a + 1) * width],
-                    lhsT=w3_codes[:, 2 * a * P : 2 * (a + 1) * P].bitcast(FP4X4),
-                    lhsT_scale=w3_plane[:, a * P : (a + 1) * P],
-                    rhs=z_codes[:].bitcast(FP8X4),
-                    rhs_scale=z_plane[:],
-                    start=True,
-                    stop=True,
-                )
+                multiply(bank[:, a * width : (a + 1) * width], a, z_mx)
             return bank[:, : N // P * width].rearrange("p (a r) -> p a r", a=N // P)
 
-        def store(product, r0, new_tile, copy):
-            result = new_tile(list(product.shape), F32)
-            copy(result[:], product)
-            nc.sync.dma_start(out_view[:, :, r0 : r0 + product.shape[2]], result[:])
-
-        gather_words(0)
-        dealt = held("w1_dealt0", [P, PACK, P, PACK], BF16)
-        deal(nc.scalar.copy, dealt, w1_raw0[:, :, : H // 2], 0)
-        deal(nc.vector.tensor_copy, dealt, w1_raw0[:, :, H // 2 :], H // 2)
-        w1_mx = [quantise_weights("w1_plane0", dealt, 1)]
-        gather_words(1)
-        dealt = held("w1_dealt1", [P, PACK, P, PACK], BF16)
-        deal(nc.scalar.copy, dealt, w1_raw1[0][:], 0)
-        deal(nc.scalar.copy, dealt, w1_raw1[1][:, :, : H // 4], H // 2)
-        deal(nc.vector.tensor_copy, dealt, w1_raw1[1][:, :, H // 4 :], H // 2 + H // 4)
-        w1_mx.append(quantise_weights("w1_plane1", dealt, PACK))
-
-        early = range(0, BANK, UNIT)
-        y_at, e_at, sums, w2_mx = {}, {}, {}, []
-        for t in range(PACK):
-            if t >= PACK - PASSES:
-                dealt = by_scalar([P, PACK, P, PACK], BF16)
-                deal(nc.scalar.copy, dealt, w2_raw[len(w2_mx)][:], 0)
-                w2_mx.append(quantise_weights(f"w2_plane{len(w2_mx)}", dealt, 1))
-            y_rows = hidden_rows(w1_mx, t, nc.vector.tensor_copy if t == 0 else nc.scalar.copy)
-            for r0 in range(0, S, BANK):
-                gather_edges(y_at, y_rows, src_sb, t, r0, BANK)
-            for r0 in early:
-                if t % 2 == 0:
-                    sums[r0, t // 2] = psum.tile([P, BANK], F32, name="early_sum")
-                turn_into(sums[r0, t // 2], y_at, t, r0, t % 2 == 0, False)
-        e_rows = [hidden_rows(w2_mx, t, nc.scalar.copy) for t in range(PACK)]
-
-        z_turned = {r0: held(f"z_turned{r0}", [P, PACK * UNIT], BF16) for r0 in range(0, TURNED_EDGES, UNIT)}
-        for t in range(PACK):
-            gather_edges(e_at, e_rows[t], dst_sb, t, 0, BANK)
-            for r0 in early:
-                turn_into(sums[r0, t // 2], e_at, t, r0, False, t % 2 == 1)
-                if t % 2 == 1:
-                    activate_turned(z_turned[r0], sums[r0, t // 2], t // 2)
-
-        z = {}
-        for t in range(PACK):
-            gather_edges(e_at, e_rows[t], dst_sb, t, BANK, UNIT)
-            if t % 2 == 0:
-                late_sum = next_bank()
-            turn_into(late_sum, y_at, t, BANK, t % 2 == 0, False)
-            turn_into(late_sum, e_at, t, BANK, False, t % 2 == 1)
-            if t % 2 == 1:
-                activate_turned(z_turned[BANK], late_sum, t // 2)
-                z[early[t // 2]] = turn_back(z_turned[early[t // 2]])
-
-        def add_gathered(r0):
-            total = by_vector([P, PACK, TAIL], F32)
-            for t in range(PACK):
-                e_side = e_rows[t][:].indirect(entries(dst_sb, r0, TAIL))
-                nc.vector.tensor_tensor(total[:, t, :], e_side, y_at[t, r0], ADD)
-            z_values = by_scalar([P, PACK * TAIL], BF16)
-            nc.scalar.activation(
-                z_values[:].rearrange("p (c i t) -> p c t i", i=4, t=PACK),
-                total[:].rearrange("p t (c i) -> p c t i", i=4),
-                SILU,
-            )
-            return z_values
+        def store(values, where, new_tile, copy):
+            result = new_tile(list(values.shape), F32)
+            copy(result[:], values)
+            nc.sync.dma_start(where, result[:])
 
         on_scalar = (by_scalar, nc.scalar.copy)
         on_vector = (by_vector, nc.vector.tensor_copy)
-        first_tail, second_tail = TURNED_EDGES, TURNED_EDGES + TAIL
-        z[first_tail] = add_gathered(first_tail)
-        product = {0: last_product(z[0], 0)}
-        z[BANK] = turn_back(z_turned[BANK])
-        store(product[0], 0, *on_scalar)
-        z[second_tail] = add_gathered(second_tail)
-        for r0 in (UNIT, BANK, first_tail):
-            product[r0] = last_product(z[r0], r0)
-        store(product[UNIT], UNIT, *on_vector)
-        product[second_tail] = last_product(z[second_tail], second_tail)
-        store(product[BANK], BANK, *on_scalar)
-        store(product[first_tail], first_tail, *on_vector)
-        store(product[second_tail], second_tail, *on_scalar)
+
+        half = BANK // 2
+        first = [by_vector([P, PACK, half], F32) for h in range(2)]
+        for t in range(PACK):
+            for h in range(2):
+                add_gathered(first[h], t, h * half)
+        z_first = by_scalar([P, PACK * BANK], BF16)
+        for h in range(2):
+            activate(z_first[:, h * PACK * half : (h + 1) * PACK * half], first[h])
+        r_b, r_c, r_d = 512, 768, 896
+        z_b = activated(sums(r_b, 256))
+        mx_first = quantise_z(z_first, 0)
+        banks_first = [next_bank() for a in range(N // P)]
+        for a in range(N // P):
+            multiply(banks_first[a][:], a, mx_first)
+        total_c = sums(r_c, 128)
+        store(banks_first[0][:], out_view[:, 0, :BANK], *on_scalar)
+        z_c = activated(total_c)
+        prod_b = product(quantise_z(z_b, r_b))
+        total_d = sums(r_d, 128)
+        store(banks_first[1][:], out_view[:, 1, :BANK], *on_scalar)
+        z_d = activated(total_d)
+        prod_c = product(quantise_z(z_c, r_c))
+        store(prod_b, out_view[:, :, r_b : r_b + 256], *on_vector)
+        prod_d = product(quantise_z(z_d, r_d))
+        store(prod_c, out_view[:, :, r_c : r_c + 128], *on_scalar)
+        store(prod_d, out_view[:, :, r_d : r_d + 128], *on_vector)

@@ -24,8 +24,8 @@ PASSES = K // K_PASS
 QUADRANTS = 4
 BANK = 512
 LIST = 16
-VECTOR_TILES = 22
-SCALAR_TILES = 19
+VECTOR_TILES = 20
+SCALAR_TILES = 12
 EARLY_TILES = 2
 
 
@@ -38,6 +38,7 @@ def tile_picked_hub_silu_p_kernel(
         keep = ctx.enter_context(tc.tile_pool(name="keep", bufs=1))
         vector_out = ctx.enter_context(tc.tile_pool(name="vector_out", bufs=VECTOR_TILES))
         scalar_out = ctx.enter_context(tc.tile_pool(name="scalar_out", bufs=SCALAR_TILES))
+        behind = ctx.enter_context(tc.tile_pool(name="behind", bufs=3))
         psum = ctx.enter_context(tc.psum_pool(name="psum", bufs=4))
 
         def held(name, shape, dtype):
@@ -61,38 +62,33 @@ def tile_picked_hub_silu_p_kernel(
 
         x_table = [held(f"x_table{g}", [P, T], U32) for g in range(PASSES)]
         x_scale_table = held("x_scale_table", [P, T], U8)
-        w3_codes = held("w3_codes", [P, 2 * N], U8)
-        w3_plane = held("w3_plane", [P, N], U8)
-        nc.gpsimd.memset(x_scale_table[:].bitcast(I32), 0)
-        nc.gpsimd.memset(w3_plane[:].bitcast(I32), 0)
+        nc.vector.memset(x_scale_table[32:64, :].bitcast(I32), 0)
+        nc.vector.memset(x_scale_table[64:, :].bitcast(I32), 0)
+        x_plane = held("x_plane", [P, PASSES * S], U8)
+        nc.gpsimd.memset(x_plane[:].bitcast(I32), 0)
 
         def load_words(g):
             nc.sync.dma_start(x_table[g][:].bitcast(I32), x_words[g].rearrange("p n t -> p (n t)").bitcast(I32))
 
-        def load_weights(name, w, g, c0, c1):
-            raw = held(name, [P, PACK, c1 - c0], F32)
+        def in_turn(tag, shape, dtype):
+            return behind.tile(shape, dtype, name=tag, align_bytes=64)
+
+        def load_weights(new_tile, name, w, g, c0, c1):
+            raw = new_tile(name, [P, PACK, c1 - c0], F32)
             w_rows = w[g * K_PASS : (g + 1) * K_PASS, c0:c1]
             nc.sync.dma_start(raw[:], w_rows.rearrange("(p j) c -> p j c", j=PACK))
             return raw
 
         nc.sync.dma_start(offs_sb[:], offs)
+        nc.sync.dma_start(
+            x_scale_table[:32, :].bitcast(I32),
+            x_scales.bitcast(I32).rearrange("z b c -> b z c"),
+        )
         load_words(0)
-        for q in range(QUADRANTS):
-            nc.sync.dma_start(
-                x_scale_table[32 * q : 32 * q + 4 * PASSES, :].bitcast(I32),
-                x_scales[:, 4 * q : 4 * q + 4, :].bitcast(I32),
-            )
-        w1_raw0 = load_weights("w1_raw0", w1, 0, 0, H)
-        load_words(1)
-        w1_raw1 = [load_weights(f"w1_raw1{c}", w1, 1, c, c + H // 2) for c in (0, H // 2)]
         nc.sync.dma_start(src_sb[:], src)
-        w2_raw = [load_weights(f"w2_raw{g}", w2, g, 0, H) for g in range(PASSES)]
         nc.sync.dma_start(dst_sb[:], dst)
-        nc.sync.dma_start(w3_codes[:].bitcast(I32), w3_words[0].bitcast(I32))
-        for q in range(QUADRANTS):
-            nc.sync.dma_start(
-                w3_plane[32 * q : 32 * q + 4, :].bitcast(I32), w3_scales[0, 4 * q : 4 * q + 4, :].bitcast(I32)
-            )
+        w1_raw0 = load_weights(held, "w1_raw0", w1, 0, 0, H)
+        load_words(1)
 
         def gather_halves(dtype, table, list_tile):
             picked = by_vector([P, S], dtype)
@@ -100,8 +96,8 @@ def tile_picked_hub_silu_p_kernel(
                 nc.vector.tensor_copy(picked[:, r0 : r0 + BANK], table[:].indirect(entries(list_tile, r0, BANK)))
             return picked
 
-        def gather_words(g, b):
-            x_codes[g, b] = by_vector([P, BANK], U32)
+        def gather_words(g, b, tile):
+            x_codes[g, b] = tile
             nc.vector.tensor_copy(x_codes[g, b][:], x_table[g][:].indirect(entries(offs_sb, b * BANK, BANK)))
 
         def deal(copy, dealt, raw_cols, c0, u):
@@ -136,7 +132,7 @@ def tile_picked_hub_silu_p_kernel(
                     lhsT=codes.bitcast(FP8X4),
                     lhsT_scale=plane,
                     rhs=x_codes[g, b][:].bitcast(FP8X4),
-                    rhs_scale=x_plane[4 * g :, b * BANK : (b + 1) * BANK],
+                    rhs_scale=x_plane[:, g * S + b * BANK : g * S + (b + 1) * BANK],
                     start=(g == 0),
                     stop=(g == PASSES - 1),
                 )
@@ -150,24 +146,38 @@ def tile_picked_hub_silu_p_kernel(
         def two_banks():
             return [psum.tile([P, BANK], F32, name="hidden_bank") for b in range(S // BANK)]
 
-        gather_words(0, 0)
-        gather_words(0, 1)
-        x_plane = by_vector([P, S], U8)
-        nc.vector.tensor_copy(x_plane[:], x_scale_table[:].indirect(offs_sb[:]))
-        dealt = [held(f"w1_dealt0{u}", [P, 2, P, PACK], BF16) for u in range(2)]
+        x_picked = by_vector([P, S], U8)
+        nc.vector.tensor_copy(x_picked[:], x_scale_table[:].indirect(offs_sb[:]))
+        for q in range(QUADRANTS):
+            nc.sync.dma_start(
+                x_plane[32 * q : 32 * q + 4, :].bitcast(I32).rearrange("p (z c) -> p z c", z=PASSES), x_picked[8 * q : 8 * q + 8, :].bitcast(I32)
+            )
+        gather_words(0, 0, by_vector([P, BANK], U32))
+        gather_words(0, 1, by_vector([P, BANK], U32))
+        dealt = [in_turn(tag, [P, 2, P, PACK], BF16) for tag in ("w1_turn", "w2_turn")]
         deal(nc.scalar.copy, dealt, w1_raw0[:], 0, 0)
+        w1_raw1 = [load_weights(in_turn, "w1_turn", w1, 1, c, c + H // 2) for c in (0, H // 2)]
         deal(nc.scalar.copy, dealt, w1_raw0[:], 0, 1)
+        w2_raw = [load_weights(in_turn, "w2_turn", w2, g, 0, H) for g in range(PASSES)]
         w1_mx = {}
         quantise_weights(w1_mx, "w1_plane0a", 0, dealt[0], 0, 1)
-        gather_words(1, 0)
+        gather_words(1, 0, by_vector([P, BANK], U32))
+        gather_words(1, 1, by_vector([P, BANK], U32))
         late_pair = dealt[1]
         y_banks = {}
         for t in range(EARLY_TILES):
             y_banks[t] = two_banks()
             hidden_pass(y_banks[t], w1_mx, t, 0)
-        gather_words(1, 1)
-        dealt = [held(f"w1_dealt1{u}", [P, 2, P, PACK], BF16) for u in range(2)]
+        dealt = [in_turn("w3_turn", [P, 2, P, PACK], BF16), held("w1_dealt11", [P, 2, P, PACK], BF16)]
         deal(nc.scalar.copy, dealt, w1_raw1[0][:], 0, 0)
+        w3_codes = in_turn("w3_turn", [P, 2 * N], U8)
+        w3_plane = in_turn("w3_turn", [P, N], U8)
+        nc.gpsimd.memset(w3_plane[:].bitcast(I32), 0)
+        nc.sync.dma_start(w3_codes[:].bitcast(I32), w3_words[0].bitcast(I32))
+        for q in range(QUADRANTS):
+            nc.sync.dma_start(
+                w3_plane[32 * q : 32 * q + 4, :].bitcast(I32), w3_scales[0, 4 * q : 4 * q + 4, :].bitcast(I32)
+            )
         deal(nc.scalar.copy, dealt, w1_raw1[0][:], 0, 1)
         deal(nc.scalar.copy, dealt, w1_raw1[1][:], H // 2, 0)
         deal(nc.scalar.copy, dealt, w1_raw1[1][:], H // 2, 1)

@@ -24,9 +24,9 @@ PASSES = K // K_PASS
 QUADRANTS = 4
 BANK = 512
 LIST = 16
-VECTOR_TILES = 20
-SCALAR_TILES = 12
-EARLY_TILES = 2
+VECTOR_TILES = 19
+SCALAR_TILES = 11
+EARLY_TILES = 3
 
 
 def tile_picked_hub_silu_p_kernel(
@@ -45,6 +45,9 @@ def tile_picked_hub_silu_p_kernel(
             return keep.tile(shape, dtype, name=name, align_bytes=64)
 
         def by_vector(shape, dtype):
+            return vector_out.tile(shape, dtype, name="by_vector", align_bytes=64)
+
+        def by_late(shape, dtype):
             return vector_out.tile(shape, dtype, name="by_vector", align_bytes=64)
 
         def by_scalar(shape, dtype):
@@ -85,10 +88,10 @@ def tile_picked_hub_silu_p_kernel(
             x_scales.bitcast(I32).rearrange("z b c -> b z c"),
         )
         load_words(0)
-        nc.sync.dma_start(src_sb[:], src)
-        nc.sync.dma_start(dst_sb[:], dst)
         w1_raw0 = load_weights(held, "w1_raw0", w1, 0, 0, H)
         load_words(1)
+        nc.sync.dma_start(src_sb[:], src)
+        nc.sync.dma_start(dst_sb[:], dst)
 
         def gather_halves(dtype, table, list_tile):
             picked = by_vector([P, S], dtype)
@@ -157,16 +160,17 @@ def tile_picked_hub_silu_p_kernel(
         dealt = [in_turn(tag, [P, 2, P, PACK], BF16) for tag in ("w1_turn", "w2_turn")]
         deal(nc.scalar.copy, dealt, w1_raw0[:], 0, 0)
         w1_raw1 = [load_weights(in_turn, "w1_turn", w1, 1, c, c + H // 2) for c in (0, H // 2)]
-        deal(nc.scalar.copy, dealt, w1_raw0[:], 0, 1)
+        deal(nc.scalar.copy, dealt, w1_raw0[:, :, : H // 2], 0, 1)
         w2_raw = [load_weights(in_turn, "w2_turn", w2, g, 0, H) for g in range(PASSES)]
         w1_mx = {}
         quantise_weights(w1_mx, "w1_plane0a", 0, dealt[0], 0, 1)
+        deal(nc.vector.tensor_copy, dealt, w1_raw0[:, :, H // 2 :], H // 2, 1)
+        quantise_weights(w1_mx, "w1_plane0b", 0, dealt[1], 2, 1)
         gather_words(1, 0, by_vector([P, BANK], U32))
         gather_words(1, 1, by_vector([P, BANK], U32))
-        late_pair = dealt[1]
         y_banks = {}
         for t in range(EARLY_TILES):
-            y_banks[t] = two_banks()
+            y_banks[t] = two_banks() if t < 2 else [next_bank() for b in range(S // BANK)]
             hidden_pass(y_banks[t], w1_mx, t, 0)
         dealt = [in_turn("w3_turn", [P, 2, P, PACK], BF16), held("w1_dealt11", [P, 2, P, PACK], BF16)]
         deal(nc.scalar.copy, dealt, w1_raw1[0][:], 0, 0)
@@ -179,10 +183,10 @@ def tile_picked_hub_silu_p_kernel(
                 w3_plane[32 * q : 32 * q + 4, :].bitcast(I32), w3_scales[0, 4 * q : 4 * q + 4, :].bitcast(I32)
             )
         deal(nc.scalar.copy, dealt, w1_raw1[0][:], 0, 1)
-        deal(nc.scalar.copy, dealt, w1_raw1[1][:], H // 2, 0)
+        deal(nc.scalar.copy, dealt, w1_raw1[1][:, :, : H // 4], H // 2, 0)
+        deal(nc.vector.tensor_copy, dealt, w1_raw1[1][:, :, H // 4 :], 3 * H // 4, 0)
         deal(nc.scalar.copy, dealt, w1_raw1[1][:], H // 2, 1)
         quantise_weights(w1_mx, "w1_plane1a", 1, dealt[0], 0, 2)
-        quantise_weights(w1_mx, "w1_plane0b", 0, late_pair, 2, 1)
         quantise_weights(w1_mx, "w1_plane1b", 1, dealt[1], 2, 1)
 
         y_at, w2_dealt, w2_mx = [], [], {}
@@ -209,27 +213,27 @@ def tile_picked_hub_silu_p_kernel(
                 hidden_pass(banks, w2_mx, t, g)
             e_rows.append(rows_out(banks, nc.scalar.copy))
 
-        def add_gathered(total, t, r0):
-            width = total.shape[2]
+        def add_gathered(to, t, r0):
+            width = to.shape[1]
             e_side = e_rows[t][:].indirect(entries(dst_sb, r0, width))
-            nc.vector.tensor_tensor(total[:, t, :], e_side, y_at[t][:, r0 : r0 + width], ADD)
+            nc.vector.tensor_tensor(to, e_side, y_at[t][:, r0 : r0 + width], ADD)
 
         def sums(r0, width):
             total = by_vector([P, PACK, width], F32)
             for t in range(PACK):
-                add_gathered(total, t, r0)
+                add_gathered(total[:, t, :], t, r0)
             return total
 
         def activate(z_values, total):
             nc.scalar.activation(
                 z_values.rearrange("p (c i t) -> p c t i", i=4, t=PACK),
-                total[:].rearrange("p t (c i) -> p c t i", i=4),
+                total.rearrange("p t (c i) -> p c t i", i=4),
                 SILU,
             )
 
         def activated(total):
             z_values = by_scalar([P, PACK * total.shape[2]], BF16)
-            activate(z_values[:], total)
+            activate(z_values[:], total[:])
             return z_values
 
         out_view = out.rearrange("(a p) r -> p a r", p=P)
@@ -259,24 +263,26 @@ def tile_picked_hub_silu_p_kernel(
                 multiply(bank[:, a * width : (a + 1) * width], a, z_mx)
             return bank[:, : N // P * width].rearrange("p (a r) -> p a r", a=N // P)
 
-        def store(values, where, new_tile, copy):
+        def store(values, where, new_tile, copy, queue=nc.sync):
             result = new_tile(list(values.shape), F32)
             copy(result[:], values)
-            nc.sync.dma_start(where, result[:])
+            queue.dma_start(where, result[:])
 
         on_scalar = (by_scalar, nc.scalar.copy)
         on_vector = (by_vector, nc.vector.tensor_copy)
 
         half = BANK // 2
-        first = [by_vector([P, PACK, half], F32) for h in range(2)]
-        for t in range(PACK):
-            for h in range(2):
-                add_gathered(first[h], t, h * half)
-        z_first = by_scalar([P, PACK * BANK], BF16)
+        first = held("first_sums", [P, PACK, BANK], F32)
+        for t in range(PACK - 1):
+            add_gathered(first[:, t, :], t, 0)
+        for r0 in (0, half):
+            add_gathered(first[:, PACK - 1, r0 : r0 + half], PACK - 1, r0)
+        z_first = by_vector([P, PACK * BANK], BF16)
         for h in range(2):
-            activate(z_first[:, h * PACK * half : (h + 1) * PACK * half], first[h])
+            activate(z_first[:, h * PACK * half : (h + 1) * PACK * half], first[:, :, h * half : (h + 1) * half])
         r_b, r_c, r_d = 512, 768, 896
-        z_b = activated(sums(r_b, 256))
+        total_b = sums(r_b, 256)
+        z_b = activated(total_b)
         mx_first = quantise_z(z_first, 0)
         banks_first = [next_bank() for a in range(N // P)]
         for a in range(N // P):
@@ -284,12 +290,20 @@ def tile_picked_hub_silu_p_kernel(
         total_c = sums(r_c, 128)
         store(banks_first[0][:], out_view[:, 0, :BANK], *on_scalar)
         z_c = activated(total_c)
-        prod_b = product(quantise_z(z_b, r_b))
         total_d = sums(r_d, 128)
         store(banks_first[1][:], out_view[:, 1, :BANK], *on_scalar)
         z_d = activated(total_d)
+        mx_b = quantise_z(z_b, r_b)
+        banks_b = two_banks()
+        for a in range(N // P):
+            multiply(banks_b[a][:, :256], a, mx_b)
         prod_c = product(quantise_z(z_c, r_c))
-        store(prod_b, out_view[:, :, r_b : r_b + 256], *on_vector)
-        prod_d = product(quantise_z(z_d, r_d))
+        mx_d = quantise_z(z_d, r_d)
+        banks_d = [next_bank() for a in range(N // P)]
+        for a in range(N // P):
+            multiply(banks_d[a][:, :128], a, mx_d)
+        store(banks_b[0][:, :256], out_view[:, 0, r_b : r_b + 256], *on_scalar)
+        store(banks_b[1][:, :256], out_view[:, 1, r_b : r_b + 256], *on_vector)
         store(prod_c, out_view[:, :, r_c : r_c + 128], *on_scalar)
-        store(prod_d, out_view[:, :, r_d : r_d + 128], *on_vector)
+        store(banks_d[0][:, :128], out_view[:, 0, r_d : r_d + 128], *on_scalar, nc.scalar)
+        store(banks_d[1][:, :128], out_view[:, 1, r_d : r_d + 128], *on_vector)

@@ -14,7 +14,6 @@ U8 = mybir.dt.uint8
 FP8X4 = mybir.dt.float8_e4m3fn_x4
 FP4X4 = mybir.dt.float4_e2m1fn_x4
 ADD = mybir.AluOpType.add
-MULT = mybir.AluOpType.mult
 SILU = mybir.ActivationFunctionType.Silu
 
 P = 128
@@ -24,9 +23,15 @@ PASSES = K // K_PASS
 QUADRANTS = 4
 BANK = 512
 LIST = 16
-VECTOR_TILES = 19
+ROW_TILES = N // P
+MIDDLE = 256
+TAIL = 128
+RING_BANKS = 4
+EARLY_TILES = RING_BANKS * BANK // S
+SCALAR_SHARE = 160
+VECTOR_TILES = 17
 SCALAR_TILES = 11
-EARLY_TILES = 3
+LOADS_BEHIND = {"behind_w1": 2, "behind_w2": 4, "behind_w3": 4}
 
 
 def tile_picked_hub_silu_p_kernel(
@@ -38,31 +43,28 @@ def tile_picked_hub_silu_p_kernel(
         keep = ctx.enter_context(tc.tile_pool(name="keep", bufs=1))
         vector_out = ctx.enter_context(tc.tile_pool(name="vector_out", bufs=VECTOR_TILES))
         scalar_out = ctx.enter_context(tc.tile_pool(name="scalar_out", bufs=SCALAR_TILES))
-        behind = ctx.enter_context(tc.tile_pool(name="behind", bufs=3))
-        psum = ctx.enter_context(tc.psum_pool(name="psum", bufs=4))
+        late_loads = ctx.enter_context(tc.tile_pool(name="late_loads", bufs=1))
+        psum = ctx.enter_context(tc.psum_pool(name="psum", bufs=RING_BANKS))
 
         def held(name, shape, dtype):
             return keep.tile(shape, dtype, name=name, align_bytes=64)
 
-        def by_vector(shape, dtype):
-            return vector_out.tile(shape, dtype, name="by_vector", align_bytes=64)
+        def behind(tag, shape, dtype):
+            return late_loads.tile(shape, dtype, name=tag, align_bytes=64, bufs=LOADS_BEHIND[tag])
 
-        def by_late(shape, dtype):
+        def by_vector(shape, dtype):
             return vector_out.tile(shape, dtype, name="by_vector", align_bytes=64)
 
         def by_scalar(shape, dtype):
             return scalar_out.tile(shape, dtype, name="by_scalar", align_bytes=64)
 
-        def next_bank():
-            return psum.tile([P, BANK], F32, name="bank")
+        def banks_of(tag, count):
+            return [psum.tile([P, BANK], F32, name=tag) for b in range(count)]
 
         def entries(list_tile, r0, width):
             return list_tile[:, r0 // LIST : (r0 + width) // LIST]
 
         offs_sb = lists.tile([P, S // LIST], U16, name="offs_sb")
-        src_sb = lists.tile([P, S // LIST], U16, name="src_sb")
-        dst_sb = lists.tile([P, S // LIST], U16, name="dst_sb")
-
         x_table = [held(f"x_table{g}", [P, T], U32) for g in range(PASSES)]
         x_scale_table = held("x_scale_table", [P, T], U8)
         nc.vector.memset(x_scale_table[32:64, :].bitcast(I32), 0)
@@ -73,41 +75,26 @@ def tile_picked_hub_silu_p_kernel(
         def load_words(g):
             nc.sync.dma_start(x_table[g][:].bitcast(I32), x_words[g].rearrange("p n t -> p (n t)").bitcast(I32))
 
-        def in_turn(tag, shape, dtype):
-            return behind.tile(shape, dtype, name=tag, align_bytes=64)
-
-        def load_weights(new_tile, name, w, g, c0, c1):
-            raw = new_tile(name, [P, PACK, c1 - c0], F32)
-            w_rows = w[g * K_PASS : (g + 1) * K_PASS, c0:c1]
-            nc.sync.dma_start(raw[:], w_rows.rearrange("(p j) c -> p j c", j=PACK))
+        def load_weights(new_tile, name, w, g):
+            raw = new_tile(name, [P, PACK, H], F32)
+            nc.sync.dma_start(raw[:], w[g * K_PASS : (g + 1) * K_PASS, :].rearrange("(p j) c -> p j c", j=PACK))
             return raw
 
         nc.sync.dma_start(offs_sb[:], offs)
-        nc.sync.dma_start(
-            x_scale_table[:32, :].bitcast(I32),
-            x_scales.bitcast(I32).rearrange("z b c -> b z c"),
-        )
+        nc.sync.dma_start(x_scale_table[:32, :].bitcast(I32), x_scales.bitcast(I32).rearrange("g b c -> b g c"))
         load_words(0)
-        w1_raw0 = load_weights(held, "w1_raw0", w1, 0, 0, H)
+        w1_raw = [load_weights(held, "w1_raw0", w1, 0)]
         load_words(1)
-        nc.sync.dma_start(src_sb[:], src)
-        nc.sync.dma_start(dst_sb[:], dst)
 
-        def gather_halves(dtype, table, list_tile):
-            picked = by_vector([P, S], dtype)
-            for r0 in range(0, S, BANK):
-                nc.vector.tensor_copy(picked[:, r0 : r0 + BANK], table[:].indirect(entries(list_tile, r0, BANK)))
-            return picked
+        def gather_words(g):
+            words = by_vector([P, S], U32)
+            nc.vector.tensor_copy(words[:], x_table[g][:].indirect(offs_sb[:]))
+            return words
 
-        def gather_words(g, b, tile):
-            x_codes[g, b] = tile
-            nc.vector.tensor_copy(x_codes[g, b][:], x_table[g][:].indirect(entries(offs_sb, b * BANK, BANK)))
-
-        def deal(copy, dealt, raw_cols, c0, u):
-            m0, m1 = c0 // PACK, (c0 + raw_cols.shape[2]) // PACK
+        def deal(copy, pair, raw, u, c0, c1):
             copy(
-                dealt[u][:, :, m0:m1, :].rearrange("p e m j -> p m j e"),
-                raw_cols.rearrange("p j (m t) -> p m j t", t=PACK)[:, :, :, 2 * u : 2 * u + 2],
+                pair[:, :, c0 // PACK : c1 // PACK, :].rearrange("p e m j -> p m j e"),
+                raw[:, :, c0:c1].rearrange("p j (m t) -> p m j t", t=PACK)[:, :, :, 2 * u : 2 * u + 2],
             )
 
         def quantise_weights(mx, name, g, dealt, t0, calls):
@@ -125,16 +112,14 @@ def tile_picked_hub_silu_p_kernel(
             for c in range(0, columns, P):
                 mx[g, t0 + c // P] = (codes[:, c : c + P], plane[:, c : c + P])
 
-        x_codes = {}
-
-        def hidden_pass(banks, weights, t, g):
-            codes, plane = weights[g, t]
+        def hidden_pass(banks, mx, t, g):
+            codes, plane = mx[g, t]
             for b, bank in enumerate(banks):
                 nc.tensor.matmul_mx(
                     out=bank[:],
                     lhsT=codes.bitcast(FP8X4),
                     lhsT_scale=plane,
-                    rhs=x_codes[g, b][:].bitcast(FP8X4),
+                    rhs=x_codes[g][:, b * BANK : (b + 1) * BANK].bitcast(FP8X4),
                     rhs_scale=x_plane[:, g * S + b * BANK : g * S + (b + 1) * BANK],
                     start=(g == 0),
                     stop=(g == PASSES - 1),
@@ -146,164 +131,163 @@ def tile_picked_hub_silu_p_kernel(
             second_copy(rows[:, BANK:], banks[1][:])
             return rows
 
-        def two_banks():
-            return [psum.tile([P, BANK], F32, name="hidden_bank") for b in range(S // BANK)]
-
-        x_picked = by_vector([P, S], U8)
-        nc.vector.tensor_copy(x_picked[:], x_scale_table[:].indirect(offs_sb[:]))
+        picked_scales = by_vector([P, S], U8)
+        nc.vector.tensor_copy(picked_scales[:], x_scale_table[:].indirect(offs_sb[:]))
         for q in range(QUADRANTS):
             nc.sync.dma_start(
-                x_plane[32 * q : 32 * q + 4, :].bitcast(I32).rearrange("p (z c) -> p z c", z=PASSES), x_picked[8 * q : 8 * q + 8, :].bitcast(I32)
+                x_plane[32 * q : 32 * q + 4, :].bitcast(I32).rearrange("p (g c) -> p g c", g=PASSES),
+                picked_scales[8 * q : 8 * q + 8, :].bitcast(I32),
             )
-        gather_words(0, 0, by_vector([P, BANK], U32))
-        gather_words(0, 1, by_vector([P, BANK], U32))
-        dealt = [in_turn(tag, [P, 2, P, PACK], BF16) for tag in ("w1_turn", "w2_turn")]
-        deal(nc.scalar.copy, dealt, w1_raw0[:], 0, 0)
-        w1_raw1 = [load_weights(in_turn, "w1_turn", w1, 1, c, c + H // 2) for c in (0, H // 2)]
-        deal(nc.scalar.copy, dealt, w1_raw0[:, :, : H // 2], 0, 1)
-        w2_raw = [load_weights(in_turn, "w2_turn", w2, g, 0, H) for g in range(PASSES)]
+        x_codes = [gather_words(0)]
+
         w1_mx = {}
-        quantise_weights(w1_mx, "w1_plane0a", 0, dealt[0], 0, 1)
-        deal(nc.vector.tensor_copy, dealt, w1_raw0[:, :, H // 2 :], H // 2, 1)
-        quantise_weights(w1_mx, "w1_plane0b", 0, dealt[1], 2, 1)
-        gather_words(1, 0, by_vector([P, BANK], U32))
-        gather_words(1, 1, by_vector([P, BANK], U32))
+        pairs = [behind(tag, [P, 2, P, PACK], BF16) for tag in ("behind_w1", "behind_w2")]
+        deal(nc.scalar.copy, pairs[0], w1_raw[0], 0, 0, H)
+        w1_raw.append(load_weights(behind, "behind_w1", w1, 1))
+        deal(nc.scalar.copy, pairs[1], w1_raw[0], 1, 0, H // 2)
+        src_sb = behind("behind_w2", [P, S // LIST], U16)
+        nc.sync.dma_start(src_sb[:], src)
+        w2_raw = [load_weights(behind, "behind_w2", w2, g) for g in range(PASSES)]
+        quantise_weights(w1_mx, "w1_plane00", 0, pairs[0], 0, 1)
+        deal(nc.vector.tensor_copy, pairs[1], w1_raw[0], 1, H // 2, H)
+        quantise_weights(w1_mx, "w1_plane01", 0, pairs[1], 2, 1)
+        x_codes.append(gather_words(1))
         y_banks = {}
         for t in range(EARLY_TILES):
-            y_banks[t] = two_banks() if t < 2 else [next_bank() for b in range(S // BANK)]
+            y_banks[t] = banks_of("hidden_bank", S // BANK)
             hidden_pass(y_banks[t], w1_mx, t, 0)
-        dealt = [in_turn("w3_turn", [P, 2, P, PACK], BF16), held("w1_dealt11", [P, 2, P, PACK], BF16)]
-        deal(nc.scalar.copy, dealt, w1_raw1[0][:], 0, 0)
-        w3_codes = in_turn("w3_turn", [P, 2 * N], U8)
-        w3_plane = in_turn("w3_turn", [P, N], U8)
+
+        pairs = [behind("behind_w3", [P, 2, P, PACK], BF16), held("w1_last_pair", [P, 2, P, PACK], BF16)]
+        deal(nc.scalar.copy, pairs[0], w1_raw[1], 0, 0, SCALAR_SHARE)
+        deal(nc.vector.tensor_copy, pairs[0], w1_raw[1], 0, SCALAR_SHARE, H)
+        dst_sb = behind("behind_w3", [P, S // LIST], U16)
+        nc.sync.dma_start(dst_sb[:], dst)
+        w3_codes = behind("behind_w3", [P, 2 * N], U8)
+        w3_plane = behind("behind_w3", [P, N], U8)
         nc.gpsimd.memset(w3_plane[:].bitcast(I32), 0)
         nc.sync.dma_start(w3_codes[:].bitcast(I32), w3_words[0].bitcast(I32))
         for q in range(QUADRANTS):
             nc.sync.dma_start(
                 w3_plane[32 * q : 32 * q + 4, :].bitcast(I32), w3_scales[0, 4 * q : 4 * q + 4, :].bitcast(I32)
             )
-        deal(nc.scalar.copy, dealt, w1_raw1[0][:], 0, 1)
-        deal(nc.scalar.copy, dealt, w1_raw1[1][:, :, : H // 4], H // 2, 0)
-        deal(nc.vector.tensor_copy, dealt, w1_raw1[1][:, :, H // 4 :], 3 * H // 4, 0)
-        deal(nc.scalar.copy, dealt, w1_raw1[1][:], H // 2, 1)
-        quantise_weights(w1_mx, "w1_plane1a", 1, dealt[0], 0, 2)
-        quantise_weights(w1_mx, "w1_plane1b", 1, dealt[1], 2, 1)
+        quantise_weights(w1_mx, "w1_plane10", 1, pairs[0], 0, 2)
+        deal(nc.scalar.copy, pairs[1], w1_raw[1], 1, 0, H // 2)
+        deal(nc.vector.tensor_copy, pairs[1], w1_raw[1], 1, H // 2, H)
+        quantise_weights(w1_mx, "w1_plane11", 1, pairs[1], 2, 1)
 
         y_at, w2_dealt, w2_mx = [], [], {}
         for t in range(PACK):
             if t >= EARLY_TILES:
-                y_banks[t] = two_banks()
+                y_banks[t] = banks_of("hidden_bank", S // BANK)
                 hidden_pass(y_banks[t], w1_mx, t, 0)
             hidden_pass(y_banks[t], w1_mx, t, 1)
             y_rows = rows_out(y_banks[t], nc.vector.tensor_copy if t == 0 else nc.scalar.copy)
             if t >= PACK - PASSES:
                 g = t - (PACK - PASSES)
                 quantise_weights(w2_mx, f"w2_plane{g}", g, w2_dealt[g], 0, 1)
-            y_at.append(gather_halves(F32, y_rows, src_sb))
+            picked = by_vector([P, S], F32)
+            for r0 in range(0, S, BANK):
+                nc.vector.tensor_copy(picked[:, r0 : r0 + BANK], y_rows[:].indirect(entries(src_sb, r0, BANK)))
+            y_at.append(picked)
             if 1 <= t <= PASSES:
                 dealt = by_scalar([P, PACK, P, PACK], BF16)
                 for u in range(2):
-                    deal(nc.scalar.copy, [dealt[:, :2], dealt[:, 2:]], w2_raw[t - 1][:], 0, u)
+                    deal(nc.scalar.copy, dealt[:, 2 * u : 2 * u + 2], w2_raw[t - 1], u, 0, H)
                 w2_dealt.append(dealt)
 
         e_rows = []
         for t in range(PACK):
-            banks = two_banks()
+            banks = banks_of("hidden_bank", S // BANK)
             for g in range(PASSES):
                 hidden_pass(banks, w2_mx, t, g)
             e_rows.append(rows_out(banks, nc.scalar.copy))
 
-        def add_gathered(to, t, r0):
-            width = to.shape[1]
+        def add_gathered(total, t, r0):
+            width = total.shape[1]
             e_side = e_rows[t][:].indirect(entries(dst_sb, r0, width))
-            nc.vector.tensor_tensor(to, e_side, y_at[t][:, r0 : r0 + width], ADD)
+            nc.vector.tensor_tensor(total, e_side, y_at[t][:, r0 : r0 + width], ADD)
 
         def sums(r0, width):
-            total = by_vector([P, PACK, width], F32)
+            totals = by_vector([P, PACK, width], F32)
             for t in range(PACK):
-                add_gathered(total[:, t, :], t, r0)
-            return total
+                add_gathered(totals[:, t, :], t, r0)
+            return totals
 
-        def activate(z_values, total):
+        def activate(z_values, totals):
             nc.scalar.activation(
                 z_values.rearrange("p (c i t) -> p c t i", i=4, t=PACK),
-                total.rearrange("p t (c i) -> p c t i", i=4),
+                totals.rearrange("p t (c i) -> p c t i", i=4),
                 SILU,
             )
 
-        def activated(total):
-            z_values = by_scalar([P, PACK * total.shape[2]], BF16)
-            activate(z_values[:], total[:])
+        def activated(totals):
+            z_values = by_scalar([P, PACK * totals.shape[2]], BF16)
+            activate(z_values[:], totals[:])
             return z_values
 
-        out_view = out.rearrange("(a p) r -> p a r", p=P)
-
-        def quantise_z(z_values, r0):
+        def last_product(z_values, r0, places):
             width = z_values.shape[1] // PACK
             z_codes = by_vector([P, width], U32)
             z_plane = held(f"z_plane{r0}", [P, width], U8)
             nc.vector.quantize_mx(out=z_codes[:].bitcast(FP8X4), scales=z_plane[:], in_=z_values[:])
-            return z_codes, z_plane
+            products = places(width)
+            for a in range(ROW_TILES):
+                nc.tensor.matmul_mx(
+                    out=products[a],
+                    lhsT=w3_codes[:, 2 * a * P : 2 * (a + 1) * P].bitcast(FP4X4),
+                    lhsT_scale=w3_plane[:, a * P : (a + 1) * P],
+                    rhs=z_codes[:].bitcast(FP8X4),
+                    rhs_scale=z_plane[:],
+                    start=True,
+                    stop=True,
+                )
+            return products
 
-        def multiply(into, a, z_mx):
-            nc.tensor.matmul_mx(
-                out=into,
-                lhsT=w3_codes[:, 2 * a * P : 2 * (a + 1) * P].bitcast(FP4X4),
-                lhsT_scale=w3_plane[:, a * P : (a + 1) * P],
-                rhs=z_mx[0][:].bitcast(FP8X4),
-                rhs_scale=z_mx[1][:],
-                start=True,
-                stop=True,
-            )
+        def a_bank_each(tag):
+            return lambda width: [bank[:, :width] for bank in banks_of(tag, ROW_TILES)]
 
-        def product(z_mx):
-            width = z_mx[0].shape[1]
-            bank = next_bank()
-            for a in range(N // P):
-                multiply(bank[:, a * width : (a + 1) * width], a, z_mx)
-            return bank[:, : N // P * width].rearrange("p (a r) -> p a r", a=N // P)
+        out_view = out.rearrange("(a p) r -> p a r", p=P)
 
-        def store(values, where, new_tile, copy, queue=nc.sync):
-            result = new_tile(list(values.shape), F32)
-            copy(result[:], values)
+        def store(product, where, new_tile, copy, queue=nc.sync):
+            result = new_tile(list(product.shape), F32)
+            copy(result[:], product)
             queue.dma_start(where, result[:])
 
         on_scalar = (by_scalar, nc.scalar.copy)
         on_vector = (by_vector, nc.vector.tensor_copy)
+        second, third, fourth = BANK, BANK + MIDDLE, BANK + MIDDLE + TAIL
 
         half = BANK // 2
-        first = held("first_sums", [P, PACK, BANK], F32)
+        first_totals = held("first_totals", [P, PACK, BANK], F32)
         for t in range(PACK - 1):
-            add_gathered(first[:, t, :], t, 0)
+            add_gathered(first_totals[:, t, :], t, 0)
         for r0 in (0, half):
-            add_gathered(first[:, PACK - 1, r0 : r0 + half], PACK - 1, r0)
+            add_gathered(first_totals[:, PACK - 1, r0 : r0 + half], PACK - 1, r0)
         z_first = by_vector([P, PACK * BANK], BF16)
-        for h in range(2):
-            activate(z_first[:, h * PACK * half : (h + 1) * PACK * half], first[:, :, h * half : (h + 1) * half])
-        r_b, r_c, r_d = 512, 768, 896
-        total_b = sums(r_b, 256)
-        z_b = activated(total_b)
-        mx_first = quantise_z(z_first, 0)
-        banks_first = [next_bank() for a in range(N // P)]
-        for a in range(N // P):
-            multiply(banks_first[a][:], a, mx_first)
-        total_c = sums(r_c, 128)
-        store(banks_first[0][:], out_view[:, 0, :BANK], *on_scalar)
-        z_c = activated(total_c)
-        total_d = sums(r_d, 128)
-        store(banks_first[1][:], out_view[:, 1, :BANK], *on_scalar)
-        z_d = activated(total_d)
-        mx_b = quantise_z(z_b, r_b)
-        banks_b = two_banks()
-        for a in range(N // P):
-            multiply(banks_b[a][:, :256], a, mx_b)
-        prod_c = product(quantise_z(z_c, r_c))
-        mx_d = quantise_z(z_d, r_d)
-        banks_d = [next_bank() for a in range(N // P)]
-        for a in range(N // P):
-            multiply(banks_d[a][:, :128], a, mx_d)
-        store(banks_b[0][:, :256], out_view[:, 0, r_b : r_b + 256], *on_scalar)
-        store(banks_b[1][:, :256], out_view[:, 1, r_b : r_b + 256], *on_vector)
-        store(prod_c, out_view[:, :, r_c : r_c + 128], *on_scalar)
-        store(banks_d[0][:, :128], out_view[:, 0, r_d : r_d + 128], *on_scalar, nc.scalar)
-        store(banks_d[1][:, :128], out_view[:, 1, r_d : r_d + 128], *on_vector)
+        for r0 in (0, half):
+            activate(z_first[:, PACK * r0 : PACK * (r0 + half)], first_totals[:, :, r0 : r0 + half])
+
+        z_second = activated(sums(second, MIDDLE))
+        first_out = last_product(z_first, 0, a_bank_each("product_bank"))
+        third_totals = sums(third, TAIL)
+        store(first_out[0], out_view[:, 0, :second], *on_scalar)
+        z_third = activated(third_totals)
+        fourth_totals = sums(fourth, TAIL)
+        store(first_out[1], out_view[:, 1, :second], *on_scalar)
+        z_fourth = activated(fourth_totals)
+        second_out = last_product(z_second, second, a_bank_each("hidden_bank"))
+        shared = []
+
+        def side_by_side(width):
+            shared.extend(banks_of("product_bank", 1))
+            return [shared[0][:, a * width : (a + 1) * width] for a in range(ROW_TILES)]
+
+        last_product(z_third, third, side_by_side)
+        third_out = shared[0][:, : ROW_TILES * TAIL].rearrange("p (a r) -> p a r", a=ROW_TILES)
+        fourth_out = last_product(z_fourth, fourth, a_bank_each("product_bank"))
+
+        store(second_out[0], out_view[:, 0, second:third], *on_scalar)
+        store(second_out[1], out_view[:, 1, second:third], *on_vector)
+        store(third_out, out_view[:, :, third:fourth], *on_scalar)
+        store(fourth_out[0], out_view[:, 0, fourth:], *on_scalar, nc.scalar)
+        store(fourth_out[1], out_view[:, 1, fourth:], *on_vector)

@@ -72,6 +72,11 @@ def tile_picked_hub_silu_p_kernel(
         x_plane = held("x_plane", [P, PASSES * S], U8)
         nc.gpsimd.memset(x_plane[:].bitcast(I32), 0)
 
+        warm_in = held("warm_in", [P, 1], F32)
+        warm_out = held("warm_out", [P, 1], F32)
+        nc.gpsimd.memset(warm_in[:], 0.0)
+        nc.scalar.activation(warm_out[:], warm_in[:], SILU)
+
         def load_words(g):
             nc.sync.dma_start(x_table[g][:].bitcast(I32), x_words[g].rearrange("p n t -> p (n t)").bitcast(I32))
 

@@ -29,8 +29,8 @@ TAIL = 128
 RING_BANKS = 4
 EARLY_TILES = RING_BANKS * BANK // S
 SCALAR_SHARE = 160
-VECTOR_TILES = 17
-SCALAR_TILES = 11
+VECTOR_TILES = 18
+SCALAR_TILES = 13
 LOADS_BEHIND = {"behind_w1": 2, "behind_w2": 4, "behind_w3": 4}
 
 
@@ -180,37 +180,61 @@ def tile_picked_hub_silu_p_kernel(
         deal(nc.vector.tensor_copy, pairs[1], w1_raw[1], 1, H // 2, H)
         quantise_weights(w1_mx, "w1_plane11", 1, pairs[1], 2, 1)
 
-        y_at, w2_dealt, w2_mx = [], [], {}
-        for t in range(PACK):
+        def y_tile(t, second_copy):
             if t >= EARLY_TILES:
                 y_banks[t] = banks_of("hidden_bank", S // BANK)
                 hidden_pass(y_banks[t], w1_mx, t, 0)
             hidden_pass(y_banks[t], w1_mx, t, 1)
-            y_rows = rows_out(y_banks[t], nc.vector.tensor_copy if t == 0 else nc.scalar.copy)
-            if t >= PACK - PASSES:
-                g = t - (PACK - PASSES)
-                quantise_weights(w2_mx, f"w2_plane{g}", g, w2_dealt[g], 0, 1)
-            picked = by_vector([P, S], F32)
-            for r0 in range(0, S, BANK):
-                nc.vector.tensor_copy(picked[:, r0 : r0 + BANK], y_rows[:].indirect(entries(src_sb, r0, BANK)))
-            y_at.append(picked)
-            if 1 <= t <= PASSES:
-                dealt = by_scalar([P, PACK, P, PACK], BF16)
-                for u in range(2):
-                    deal(nc.scalar.copy, dealt[:, 2 * u : 2 * u + 2], w2_raw[t - 1], u, 0, H)
-                w2_dealt.append(dealt)
+            return rows_out(y_banks[t], second_copy)
 
-        e_rows = []
-        for t in range(PACK):
-            banks = banks_of("hidden_bank", S // BANK)
+        def gather_y(t, y_rows, halves):
+            picked = by_vector([P, len(halves) * BANK], F32)
+            for n, h in enumerate(halves):
+                y_at[t, h] = picked[:, n * BANK : (n + 1) * BANK]
+                nc.vector.tensor_copy(y_at[t, h], y_rows[:].indirect(entries(src_sb, h * BANK, BANK)))
+
+        def deal_w2(u, g):
+            pair = by_scalar([P, 2, P, PACK], BF16)
+            deal(nc.scalar.copy, pair, w2_raw[g], u, 0, H)
+            return pair
+
+        def quantise_w2(u, dealt):
+            codes = by_vector([P, PASSES, 2 * P], U32)
+            plane = held(f"w2_plane{u}", [P, PASSES, 2 * P], U8)
+            for g in range(PASSES):
+                flat = dealt[g][:].rearrange("p t m j -> p (t m j)")
+                nc.vector.quantize_mx(out=codes[:, g, :].bitcast(FP8X4), scales=plane[:, g, :], in_=flat)
+                for e in range(2):
+                    w2_mx[g, 2 * u + e] = (codes[:, g, e * P : (e + 1) * P], plane[:, g, e * P : (e + 1) * P])
+
+        def e_tile(t, tag):
+            banks = banks_of(tag, S // BANK)
             for g in range(PASSES):
                 hidden_pass(banks, w2_mx, t, g)
-            e_rows.append(rows_out(banks, nc.scalar.copy))
+            return banks
+
+        y_at, w2_mx = {}, {}
+        gather_y(0, y_tile(0, nc.vector.tensor_copy), (0, 1))
+        gather_y(1, y_tile(1, nc.scalar.copy), (0, 1))
+        first_pair = [deal_w2(0, 0)]
+        y_third = y_tile(2, nc.scalar.copy)
+        first_pair.append(deal_w2(0, 1))
+        quantise_w2(0, first_pair)
+        gather_y(2, y_third, (0, 1))
+        y_last = y_tile(3, nc.scalar.copy)
+        e_banks = [e_tile(t, "product_bank") for t in range(2)]
+        second_pair = [deal_w2(1, g) for g in range(PASSES)]
+        gather_y(3, y_last, (0,))
+        quantise_w2(1, second_pair)
+        gather_y(3, y_last, (1,))
+        e_banks.extend(e_tile(t, "hidden_bank") for t in range(2, PACK))
+        e_rows = [rows_out(banks, nc.scalar.copy) for banks in e_banks]
 
         def add_gathered(total, t, r0):
             width = total.shape[1]
             e_side = e_rows[t][:].indirect(entries(dst_sb, r0, width))
-            nc.vector.tensor_tensor(total, e_side, y_at[t][:, r0 : r0 + width], ADD)
+            y_side = y_at[t, r0 // BANK][:, r0 % BANK : r0 % BANK + width]
+            nc.vector.tensor_tensor(total, e_side, y_side, ADD)
 
         def sums(r0, width):
             totals = by_vector([P, PACK, width], F32)

@@ -29,9 +29,9 @@ TAIL = 128
 RING_BANKS = 4
 EARLY_TILES = RING_BANKS * BANK // S
 SCALAR_SHARE = 160
-VECTOR_TILES = 18
+VECTOR_TILES = 19
 SCALAR_TILES = 13
-LOADS_BEHIND = {"behind_w1": 2, "behind_w2": 4, "behind_w3": 4}
+LOADS_BEHIND = {"behind_w1": 5, "behind_w3": 4}
 
 
 def tile_picked_hub_silu_p_kernel(
@@ -146,15 +146,14 @@ def tile_picked_hub_silu_p_kernel(
         x_codes = [gather_words(0)]
 
         w1_mx = {}
-        pairs = [behind(tag, [P, 2, P, PACK], BF16) for tag in ("behind_w1", "behind_w2")]
+        pairs = [behind("behind_w1", [P, 2, P, PACK], BF16), by_vector([P, 2, P, PACK], BF16)]
         deal(nc.scalar.copy, pairs[0], w1_raw[0], 0, 0, H)
         w1_raw.append(load_weights(behind, "behind_w1", w1, 1))
-        deal(nc.scalar.copy, pairs[1], w1_raw[0], 1, 0, H // 2)
-        src_sb = behind("behind_w2", [P, S // LIST], U16)
+        src_sb = behind("behind_w1", [P, S // LIST], U16)
         nc.sync.dma_start(src_sb[:], src)
-        w2_raw = [load_weights(behind, "behind_w2", w2, g) for g in range(PASSES)]
+        w2_raw = [load_weights(behind, "behind_w1", w2, g) for g in range(PASSES)]
+        deal(nc.vector.tensor_copy, pairs[1], w1_raw[0], 1, 0, H)
         quantise_weights(w1_mx, "w1_plane00", 0, pairs[0], 0, 1)
-        deal(nc.vector.tensor_copy, pairs[1], w1_raw[0], 1, H // 2, H)
         quantise_weights(w1_mx, "w1_plane01", 0, pairs[1], 2, 1)
         x_codes.append(gather_words(1))
         y_banks = {}

@@ -130,10 +130,10 @@ def tile_picked_hub_silu_p_kernel(
                     stop=(g == PASSES - 1),
                 )
 
-        def rows_out(banks, second_copy):
+        def rows_out(banks, first_copy):
             rows = by_scalar([P, S], F32)
-            nc.scalar.copy(rows[:, :BANK], banks[0][:])
-            second_copy(rows[:, BANK:], banks[1][:])
+            first_copy(rows[:, :BANK], banks[0][:])
+            nc.scalar.copy(rows[:, BANK:], banks[1][:])
             return rows
 
         picked_scales = by_vector([P, S], U8)
@@ -164,6 +164,8 @@ def tile_picked_hub_silu_p_kernel(
         pairs = [behind("behind_w3", [P, 2, P, PACK], BF16), held("w1_last_pair", [P, 2, P, PACK], BF16)]
         deal(nc.scalar.copy, pairs[0], w1_raw[1], 0, 0, SCALAR_SHARE)
         deal(nc.vector.tensor_copy, pairs[0], w1_raw[1], 0, SCALAR_SHARE, H)
+        deal(nc.vector.tensor_copy, pairs[1], w1_raw[1], 1, H // 2, H)
+        deal(nc.scalar.copy, pairs[1], w1_raw[1], 1, 0, H // 2)
         dst_sb = behind("behind_w3", [P, S // LIST], U16)
         nc.sync.dma_start(dst_sb[:], dst)
         w3_codes = behind("behind_w3", [P, 2 * N], U8)
@@ -175,8 +177,6 @@ def tile_picked_hub_silu_p_kernel(
                 w3_plane[32 * q : 32 * q + 4, :].bitcast(I32), w3_scales[0, 4 * q : 4 * q + 4, :].bitcast(I32)
             )
         quantise_weights(w1_mx, "w1_plane10", 1, pairs[0], 0, 2)
-        deal(nc.scalar.copy, pairs[1], w1_raw[1], 1, 0, H // 2)
-        deal(nc.vector.tensor_copy, pairs[1], w1_raw[1], 1, H // 2, H)
         quantise_weights(w1_mx, "w1_plane11", 1, pairs[1], 2, 1)
 
         def y_tile(t, second_copy):

@@ -22,6 +22,7 @@ K_PASS = P * PACK
 PASSES = K // K_PASS
 QUADRANTS = 4
 BANK = 512
+WINDOW = 1376
 LIST = 16
 ROW_TILES = N // P
 MIDDLE = 256
@@ -130,15 +131,15 @@ def tile_picked_hub_silu_p_kernel(
                     stop=(g == PASSES - 1),
                 )
 
-        def rows_out(banks, first_copy):
-            rows = by_scalar([P, S], F32)
+        def rows_out(banks, first_copy, columns=S):
+            rows = by_scalar([P, columns], F32)
             first_copy(rows[:, :BANK], banks[0][:])
-            nc.scalar.copy(rows[:, BANK:], banks[1][:])
+            nc.scalar.copy(rows[:, BANK:S], banks[1][:])
             return rows
 
         picked_scales = by_vector([P, S], U8)
         nc.vector.tensor_copy(picked_scales[:], x_scale_table[:].indirect(offs_sb[:]))
-        for q in range(QUADRANTS):
+        for q in (0, 2, 1, 3):
             nc.sync.dma_start(
                 x_plane[32 * q : 32 * q + 4, :].bitcast(I32).rearrange("p (g c) -> p g c", g=PASSES),
                 picked_scales[8 * q : 8 * q + 8, :].bitcast(I32),
@@ -184,13 +185,14 @@ def tile_picked_hub_silu_p_kernel(
                 y_banks[t] = banks_of("hidden_bank", S // BANK)
                 hidden_pass(y_banks[t], w1_mx, t, 0)
             hidden_pass(y_banks[t], w1_mx, t, 1)
-            return rows_out(y_banks[t], second_copy)
+            return rows_out(y_banks[t], second_copy, WINDOW)
 
         def gather_y(t, y_rows, halves):
             picked = by_vector([P, len(halves) * BANK], F32)
             for n, h in enumerate(halves):
                 y_at[t, h] = picked[:, n * BANK : (n + 1) * BANK]
-                nc.vector.tensor_copy(y_at[t, h], y_rows[:].indirect(entries(src_sb, h * BANK, BANK)))
+            listed = entries(src_sb, halves[0] * BANK, len(halves) * BANK)
+            nc.vector.tensor_copy(picked[:], y_rows[:].indirect(listed))
 
         def deal_w2(u, g):
             pair = by_scalar([P, 2, P, PACK], BF16)
@@ -250,7 +252,7 @@ def tile_picked_hub_silu_p_kernel(
 
         def activated(totals):
             z_values = by_scalar([P, PACK * totals.shape[2]], BF16)
-            activate(z_values[:], totals[:])
+            activate(z_values[:], totals[:, :, :])
             return z_values
 
         def last_product(z_values, r0, places):
@@ -297,12 +299,16 @@ def tile_picked_hub_silu_p_kernel(
 
         z_second = activated(sums(second, MIDDLE))
         first_out = last_product(z_first, 0, a_bank_each("product_bank"))
-        third_totals = sums(third, TAIL)
+        last_totals = by_vector([P, PACK, 2 * TAIL], F32)
+        for t in range(2):
+            add_gathered(last_totals[:, t, :], t, third)
+        for r0 in (0, TAIL):
+            for t in range(2, PACK):
+                add_gathered(last_totals[:, t, r0 : r0 + TAIL], t, third + r0)
         store(first_out[0], out_view[:, 0, :second], *on_scalar)
-        z_third = activated(third_totals)
-        fourth_totals = sums(fourth, TAIL)
         store(first_out[1], out_view[:, 1, :second], *on_scalar)
-        z_fourth = activated(fourth_totals)
+        z_third = activated(last_totals[:, :, :TAIL])
+        z_fourth = activated(last_totals[:, :, TAIL:])
         second_out = last_product(z_second, second, a_bank_each("hidden_bank"))
         shared = []
 

@@ -14,6 +14,7 @@ U8 = mybir.dt.uint8
 FP8X4 = mybir.dt.float8_e4m3fn_x4
 FP4X4 = mybir.dt.float4_e2m1fn_x4
 ADD = mybir.AluOpType.add
+MULT = mybir.AluOpType.mult
 SILU = mybir.ActivationFunctionType.Silu
 
 P = 128
@@ -30,8 +31,8 @@ TAIL = 128
 RING_BANKS = 4
 EARLY_TILES = RING_BANKS * BANK // S
 SCALAR_SHARE = 160
-VECTOR_TILES = 19
-SCALAR_TILES = 13
+VECTOR_TILES = 20
+SCALAR_TILES = 12
 LOADS_BEHIND = {"behind_w1": 5, "behind_w3": 4}
 
 
@@ -199,36 +200,32 @@ def tile_picked_hub_silu_p_kernel(
             deal(nc.scalar.copy, pair, w2_raw[g], u, 0, H)
             return pair
 
-        def quantise_w2(u, dealt):
-            codes = by_vector([P, PASSES, 2 * P], U32)
-            plane = held(f"w2_plane{u}", [P, PASSES, 2 * P], U8)
-            for g in range(PASSES):
-                flat = dealt[g][:].rearrange("p t m j -> p (t m j)")
-                nc.vector.quantize_mx(out=codes[:, g, :].bitcast(FP8X4), scales=plane[:, g, :], in_=flat)
-                for e in range(2):
-                    w2_mx[g, 2 * u + e] = (codes[:, g, e * P : (e + 1) * P], plane[:, g, e * P : (e + 1) * P])
-
-        def e_tile(t, tag):
-            banks = banks_of(tag, S // BANK)
-            for g in range(PASSES):
-                hidden_pass(banks, w2_mx, t, g)
-            return banks
+        def e_pass(u, g, dealt):
+            quantise_weights(w2_mx, f"w2_plane{g}{u}", g, dealt, 2 * u, 1)
+            for t in (2 * u, 2 * u + 1):
+                if g == 0:
+                    e_banks.append(banks_of(("product_bank", "hidden_bank")[u], S // BANK))
+                hidden_pass(e_banks[t], w2_mx, t, g)
 
         y_at, w2_mx = {}, {}
         gather_y(0, y_tile(0, nc.vector.tensor_copy), (0, 1))
         gather_y(1, y_tile(1, nc.scalar.copy), (0, 1))
+        e_banks = []
         first_pair = [deal_w2(0, 0)]
         y_third = y_tile(2, nc.scalar.copy)
         first_pair.append(deal_w2(0, 1))
-        quantise_w2(0, first_pair)
-        gather_y(2, y_third, (0, 1))
         y_last = y_tile(3, nc.scalar.copy)
-        e_banks = [e_tile(t, "product_bank") for t in range(2)]
-        second_pair = [deal_w2(1, g) for g in range(PASSES)]
+        second_pair = [held("w2_by_gpsimd", [P, 2, P, PACK], BF16), deal_w2(1, 1)]
+        for e in range(2):
+            columns = w2_raw[0][:].rearrange("p j (m t) -> p m j t", t=PACK)[:, :, :, 2 + e]
+            nc.gpsimd.tensor_scalar(second_pair[0][:, e], columns, 1.0, 0.0, MULT, ADD)
+        e_pass(0, 0, first_pair[0])
+        gather_y(2, y_third, (0, 1))
+        e_pass(0, 1, first_pair[1])
+        e_pass(1, 0, second_pair[0])
         gather_y(3, y_last, (0,))
-        quantise_w2(1, second_pair)
+        e_pass(1, 1, second_pair[1])
         gather_y(3, y_last, (1,))
-        e_banks.extend(e_tile(t, "hidden_bank") for t in range(2, PACK))
         e_rows = [rows_out(banks, nc.scalar.copy) for banks in e_banks]
 
         def add_gathered(total, t, r0):

@@ -14,7 +14,7 @@ U8 = mybir.dt.uint8
 FP8X4 = mybir.dt.float8_e4m3fn_x4
 FP4X4 = mybir.dt.float4_e2m1fn_x4
 ADD = mybir.AluOpType.add
-MULT = mybir.AluOpType.mult
+COPY = mybir.ActivationFunctionType.Copy
 SILU = mybir.ActivationFunctionType.Silu
 
 P = 128
@@ -23,16 +23,14 @@ K_PASS = P * PACK
 PASSES = K // K_PASS
 QUADRANTS = 4
 BANK = 512
-WINDOW = 1376
 LIST = 16
 ROW_TILES = N // P
 MIDDLE = 256
 TAIL = 128
-RING_BANKS = 4
-EARLY_TILES = RING_BANKS * BANK // S
+BANKS = 8
 SCALAR_SHARE = 160
 VECTOR_TILES = 20
-SCALAR_TILES = 12
+SCALAR_TILES = 16
 LOADS_BEHIND = {"behind_w1": 5, "behind_w3": 4}
 
 
@@ -46,7 +44,7 @@ def tile_picked_hub_silu_p_kernel(
         vector_out = ctx.enter_context(tc.tile_pool(name="vector_out", bufs=VECTOR_TILES))
         scalar_out = ctx.enter_context(tc.tile_pool(name="scalar_out", bufs=SCALAR_TILES))
         late_loads = ctx.enter_context(tc.tile_pool(name="late_loads", bufs=1))
-        psum = ctx.enter_context(tc.psum_pool(name="psum", bufs=RING_BANKS))
+        psum = ctx.enter_context(tc.psum_pool(name="psum", bufs=BANKS))
 
         def held(name, shape, dtype):
             return keep.tile(shape, dtype, name=name, align_bytes=64)
@@ -60,8 +58,8 @@ def tile_picked_hub_silu_p_kernel(
         def by_scalar(shape, dtype):
             return scalar_out.tile(shape, dtype, name="by_scalar", align_bytes=64)
 
-        def banks_of(tag, count):
-            return [psum.tile([P, BANK], F32, name=tag) for b in range(count)]
+        def banks_of(count):
+            return [psum.tile([P, BANK], F32, name="bank") for b in range(count)]
 
         def entries(list_tile, r0, width):
             return list_tile[:, r0 // LIST : (r0 + width) // LIST]
@@ -93,10 +91,13 @@ def tile_picked_hub_silu_p_kernel(
         w1_raw = [load_weights(held, "w1_raw0", w1, 0)]
         load_words(1)
 
-        def gather_words(g):
-            words = by_vector([P, S], U32)
-            nc.vector.tensor_copy(words[:], x_table[g][:].indirect(offs_sb[:]))
-            return words
+        x_codes = {}
+
+        def gather_words(g, r0, width):
+            words = by_vector([P, width], U32)
+            nc.vector.tensor_copy(words[:], x_table[g][:].indirect(entries(offs_sb, r0, width)))
+            for c in range(0, width, BANK):
+                x_codes[g, (r0 + c) // BANK] = words[:, c : c + BANK]
 
         def deal(copy, pair, raw, u, c0, c1):
             copy(
@@ -126,14 +127,14 @@ def tile_picked_hub_silu_p_kernel(
                     out=bank[:],
                     lhsT=codes.bitcast(FP8X4),
                     lhsT_scale=plane,
-                    rhs=x_codes[g][:, b * BANK : (b + 1) * BANK].bitcast(FP8X4),
+                    rhs=x_codes[g, b].bitcast(FP8X4),
                     rhs_scale=x_plane[:, g * S + b * BANK : g * S + (b + 1) * BANK],
                     start=(g == 0),
                     stop=(g == PASSES - 1),
                 )
 
-        def rows_out(banks, first_copy, columns=S):
-            rows = by_scalar([P, columns], F32)
+        def rows_out(banks, new_tile, first_copy):
+            rows = new_tile([P, S], F32)
             first_copy(rows[:, :BANK], banks[0][:])
             nc.scalar.copy(rows[:, BANK:S], banks[1][:])
             return rows
@@ -145,23 +146,23 @@ def tile_picked_hub_silu_p_kernel(
                 x_plane[32 * q : 32 * q + 4, :].bitcast(I32).rearrange("p (g c) -> p g c", g=PASSES),
                 picked_scales[8 * q : 8 * q + 8, :].bitcast(I32),
             )
-        x_codes = [gather_words(0)]
+        gather_words(0, 0, S)
 
         w1_mx = {}
-        pairs = [behind("behind_w1", [P, 2, P, PACK], BF16), by_vector([P, 2, P, PACK], BF16)]
+        pairs = [behind("behind_w1", [P, 2, P, PACK], BF16), by_scalar([P, 2, P, PACK], BF16)]
         deal(nc.scalar.copy, pairs[0], w1_raw[0], 0, 0, H)
         w1_raw.append(load_weights(behind, "behind_w1", w1, 1))
         src_sb = behind("behind_w1", [P, S // LIST], U16)
         nc.sync.dma_start(src_sb[:], src)
         w2_raw = [load_weights(behind, "behind_w1", w2, g) for g in range(PASSES)]
-        deal(nc.vector.tensor_copy, pairs[1], w1_raw[0], 1, 0, H)
-        quantise_weights(w1_mx, "w1_plane00", 0, pairs[0], 0, 1)
-        quantise_weights(w1_mx, "w1_plane01", 0, pairs[1], 2, 1)
-        x_codes.append(gather_words(1))
-        y_banks = {}
-        for t in range(EARLY_TILES):
-            y_banks[t] = banks_of("hidden_bank", S // BANK)
-            hidden_pass(y_banks[t], w1_mx, t, 0)
+        deal(nc.scalar.copy, pairs[1], w1_raw[0], 1, 0, H)
+        y_banks = []
+        for u in range(2):
+            quantise_weights(w1_mx, f"w1_plane0{u}", 0, pairs[u], 2 * u, 1)
+            gather_words(1, u * BANK, BANK)
+            for t in (2 * u, 2 * u + 1):
+                y_banks.append(banks_of(S // BANK))
+                hidden_pass(y_banks[t], w1_mx, t, 0)
 
         pairs = [behind("behind_w3", [P, 2, P, PACK], BF16), held("w1_last_pair", [P, 2, P, PACK], BF16)]
         deal(nc.scalar.copy, pairs[0], w1_raw[1], 0, 0, SCALAR_SHARE)
@@ -180,65 +181,72 @@ def tile_picked_hub_silu_p_kernel(
             )
         quantise_weights(w1_mx, "w1_plane10", 1, pairs[0], 0, 2)
         quantise_weights(w1_mx, "w1_plane11", 1, pairs[1], 2, 1)
-
-        def y_tile(t, second_copy):
-            if t >= EARLY_TILES:
-                y_banks[t] = banks_of("hidden_bank", S // BANK)
-                hidden_pass(y_banks[t], w1_mx, t, 0)
+        for t in range(PACK):
             hidden_pass(y_banks[t], w1_mx, t, 1)
-            return rows_out(y_banks[t], second_copy, WINDOW)
 
-        def gather_y(t, y_rows, halves):
-            picked = by_vector([P, len(halves) * BANK], F32)
-            for n, h in enumerate(halves):
-                y_at[t, h] = picked[:, n * BANK : (n + 1) * BANK]
-            listed = entries(src_sb, halves[0] * BANK, len(halves) * BANK)
-            nc.vector.tensor_copy(picked[:], y_rows[:].indirect(listed))
+        y_at = []
+
+        def gather_y(on_scalar_engine, t, r0, width):
+            window = y_rows[t][:].indirect(entries(src_sb, r0, width))
+            if on_scalar_engine:
+                picked = by_scalar([P, width], F32)
+                nc.scalar.activation(picked[:], window, COPY)
+            else:
+                picked = by_vector([P, width], F32)
+                nc.vector.tensor_copy(picked[:], window)
+            y_at.append((t, r0, picked))
 
         def deal_w2(u, g):
-            pair = by_scalar([P, 2, P, PACK], BF16)
-            deal(nc.scalar.copy, pair, w2_raw[g], u, 0, H)
+            pair = by_vector([P, 2, P, PACK], BF16)
+            deal(nc.vector.tensor_copy, pair, w2_raw[g], u, 0, H)
             return pair
 
         def e_pass(u, g, dealt):
             quantise_weights(w2_mx, f"w2_plane{g}{u}", g, dealt, 2 * u, 1)
             for t in (2 * u, 2 * u + 1):
                 if g == 0:
-                    e_banks.append(banks_of(("product_bank", "hidden_bank")[u], S // BANK))
+                    e_banks.append(banks_of(S // BANK))
                 hidden_pass(e_banks[t], w2_mx, t, g)
-
-        y_at, w2_mx = {}, {}
-        gather_y(0, y_tile(0, nc.vector.tensor_copy), (0, 1))
-        gather_y(1, y_tile(1, nc.scalar.copy), (0, 1))
-        e_banks = []
-        first_pair = [deal_w2(0, 0)]
-        y_third = y_tile(2, nc.scalar.copy)
-        first_pair.append(deal_w2(0, 1))
-        y_last = y_tile(3, nc.scalar.copy)
-        second_pair = [held("w2_by_gpsimd", [P, 2, P, PACK], BF16), deal_w2(1, 1)]
-        for e in range(2):
-            columns = w2_raw[0][:].rearrange("p j (m t) -> p m j t", t=PACK)[:, :, :, 2 + e]
-            nc.gpsimd.tensor_scalar(second_pair[0][:, e], columns, 1.0, 0.0, MULT, ADD)
-        e_pass(0, 0, first_pair[0])
-        gather_y(2, y_third, (0, 1))
-        e_pass(0, 1, first_pair[1])
-        e_pass(1, 0, second_pair[0])
-        gather_y(3, y_last, (0,))
-        e_pass(1, 1, second_pair[1])
-        gather_y(3, y_last, (1,))
-        e_rows = [rows_out(banks, nc.scalar.copy) for banks in e_banks]
 
         def add_gathered(total, t, r0):
             width = total.shape[1]
             e_side = e_rows[t][:].indirect(entries(dst_sb, r0, width))
-            y_side = y_at[t, r0 // BANK][:, r0 % BANK : r0 % BANK + width]
-            nc.vector.tensor_tensor(total, e_side, y_side, ADD)
+            for tile_t, first, picked in y_at:
+                if tile_t == t and first <= r0 < first + picked.shape[1]:
+                    nc.vector.tensor_tensor(total, e_side, picked[:, r0 - first : r0 - first + width], ADD)
 
         def sums(r0, width):
             totals = by_vector([P, PACK, width], F32)
             for t in range(PACK):
                 add_gathered(totals[:, t, :], t, r0)
             return totals
+
+        second, third, fourth = BANK, BANK + MIDDLE, BANK + MIDDLE + TAIL
+        SCALAR, VECTOR = True, False
+        w2_mx, e_banks, e_rows = {}, [], []
+        y_rows = [rows_out(y_banks[0], by_vector, nc.vector.tensor_copy)]
+        dealt00 = deal_w2(0, 0)
+        y_rows.append(rows_out(y_banks[1], by_scalar, nc.scalar.copy))
+        gather_y(VECTOR, 0, 0, BANK)
+        y_rows.append(rows_out(y_banks[2], by_scalar, nc.scalar.copy))
+        e_pass(0, 0, dealt00)
+        dealt01 = deal_w2(0, 1)
+        y_rows.append(rows_out(y_banks[3], by_scalar, nc.scalar.copy))
+        dealt10 = deal_w2(1, 0)
+        e_pass(0, 1, dealt01)
+        gather_y(SCALAR, 2, 0, BANK)
+        gather_y(VECTOR, 1, 0, BANK)
+        dealt11 = deal_w2(1, 1)
+        e_rows.append(rows_out(e_banks[0], by_scalar, nc.scalar.copy))
+        e_pass(1, 0, dealt10)
+        e_pass(1, 1, dealt11)
+        e_rows.append(rows_out(e_banks[1], by_scalar, nc.scalar.copy))
+        gather_y(VECTOR, 0, second, BANK)
+        gather_y(SCALAR, 3, 0, BANK)
+        e_rows.append(rows_out(e_banks[2], by_scalar, nc.scalar.copy))
+        e_rows.append(rows_out(e_banks[3], by_scalar, nc.scalar.copy))
+        for t in (1, 2, 3):
+            gather_y(SCALAR, t, second, MIDDLE)
 
         def activate(z_values, totals):
             nc.scalar.activation(
@@ -270,8 +278,8 @@ def tile_picked_hub_silu_p_kernel(
                 )
             return products
 
-        def a_bank_each(tag):
-            return lambda width: [bank[:, :width] for bank in banks_of(tag, ROW_TILES)]
+        def a_bank_each(width):
+            return [bank[:, :width] for bank in banks_of(ROW_TILES)]
 
         out_view = out.rearrange("(a p) r -> p a r", p=P)
 
@@ -282,7 +290,6 @@ def tile_picked_hub_silu_p_kernel(
 
         on_scalar = (by_scalar, nc.scalar.copy)
         on_vector = (by_vector, nc.vector.tensor_copy)
-        second, third, fourth = BANK, BANK + MIDDLE, BANK + MIDDLE + TAIL
 
         half = BANK // 2
         first_totals = held("first_totals", [P, PACK, BANK], F32)
@@ -294,8 +301,12 @@ def tile_picked_hub_silu_p_kernel(
         for r0 in (0, half):
             activate(z_first[:, PACK * r0 : PACK * (r0 + half)], first_totals[:, :, r0 : r0 + half])
 
-        z_second = activated(sums(second, MIDDLE))
-        first_out = last_product(z_first, 0, a_bank_each("product_bank"))
+        second_totals = sums(second, MIDDLE)
+        for t in (2, 3):
+            gather_y(SCALAR, t, third, 2 * TAIL)
+        gather_y(VECTOR, 1, third, 2 * TAIL)
+        z_second = activated(second_totals)
+        first_out = last_product(z_first, 0, a_bank_each)
         last_totals = by_vector([P, PACK, 2 * TAIL], F32)
         for t in range(2):
             add_gathered(last_totals[:, t, :], t, third)
@@ -306,16 +317,16 @@ def tile_picked_hub_silu_p_kernel(
         store(first_out[1], out_view[:, 1, :second], *on_scalar)
         z_third = activated(last_totals[:, :, :TAIL])
         z_fourth = activated(last_totals[:, :, TAIL:])
-        second_out = last_product(z_second, second, a_bank_each("hidden_bank"))
+        second_out = last_product(z_second, second, a_bank_each)
         shared = []
 
         def side_by_side(width):
-            shared.extend(banks_of("product_bank", 1))
+            shared.extend(banks_of(1))
             return [shared[0][:, a * width : (a + 1) * width] for a in range(ROW_TILES)]
 
         last_product(z_third, third, side_by_side)
         third_out = shared[0][:, : ROW_TILES * TAIL].rearrange("p (a r) -> p a r", a=ROW_TILES)
-        fourth_out = last_product(z_fourth, fourth, a_bank_each("product_bank"))
+        fourth_out = last_product(z_fourth, fourth, a_bank_each)
 
         store(second_out[0], out_view[:, 0, second:third], *on_scalar)
         store(second_out[1], out_view[:, 1, second:third], *on_vector)

@@ -157,12 +157,12 @@ def tile_picked_hub_silu_p_kernel(
         w2_raw = [load_weights(behind, "behind_w1", w2, g) for g in range(PASSES)]
         deal(nc.scalar.copy, pairs[1], w1_raw[0], 1, 0, H)
         y_banks = []
-        for u in range(2):
-            quantise_weights(w1_mx, f"w1_plane0{u}", 0, pairs[u], 2 * u, 1)
-            gather_words(1, u * BANK, BANK)
-            for t in (2 * u, 2 * u + 1):
-                y_banks.append(banks_of(S // BANK))
-                hidden_pass(y_banks[t], w1_mx, t, 0)
+        quantise_weights(w1_mx, "w1_plane00", 0, pairs[0], 0, 1)
+        gather_words(1, 0, S)
+        first_pass_pair = pairs[1]
+        for t in range(2):
+            y_banks.append(banks_of(S // BANK))
+            hidden_pass(y_banks[t], w1_mx, t, 0)
 
         pairs = [behind("behind_w3", [P, 2, P, PACK], BF16), held("w1_last_pair", [P, 2, P, PACK], BF16)]
         deal(nc.scalar.copy, pairs[0], w1_raw[1], 0, 0, SCALAR_SHARE)
@@ -180,9 +180,15 @@ def tile_picked_hub_silu_p_kernel(
                 w3_plane[32 * q : 32 * q + 4, :].bitcast(I32), w3_scales[0, 4 * q : 4 * q + 4, :].bitcast(I32)
             )
         quantise_weights(w1_mx, "w1_plane10", 1, pairs[0], 0, 2)
+        quantise_weights(w1_mx, "w1_plane01", 0, first_pass_pair, 2, 1)
         quantise_weights(w1_mx, "w1_plane11", 1, pairs[1], 2, 1)
-        for t in range(PACK):
+
+        def y_tile(t, new_tile, first_copy):
+            if t >= 2:
+                y_banks.append(banks_of(S // BANK))
+                hidden_pass(y_banks[t], w1_mx, t, 0)
             hidden_pass(y_banks[t], w1_mx, t, 1)
+            return rows_out(y_banks[t], new_tile, first_copy)
 
         y_at = []
 
@@ -201,12 +207,15 @@ def tile_picked_hub_silu_p_kernel(
             deal(nc.vector.tensor_copy, pair, w2_raw[g], u, 0, H)
             return pair
 
-        def e_pass(u, g, dealt):
+        def quantise_w2(u, g, dealt):
             quantise_weights(w2_mx, f"w2_plane{g}{u}", g, dealt, 2 * u, 1)
+
+        def e_pair(u, passes):
             for t in (2 * u, 2 * u + 1):
-                if g == 0:
-                    e_banks.append(banks_of(S // BANK))
-                hidden_pass(e_banks[t], w2_mx, t, g)
+                for g in passes:
+                    if g == 0:
+                        e_banks.append(banks_of(S // BANK))
+                    hidden_pass(e_banks[t], w2_mx, t, g)
 
         def add_gathered(total, t, r0):
             width = total.shape[1]
@@ -224,27 +233,30 @@ def tile_picked_hub_silu_p_kernel(
         second, third, fourth = BANK, BANK + MIDDLE, BANK + MIDDLE + TAIL
         SCALAR, VECTOR = True, False
         w2_mx, e_banks, e_rows = {}, [], []
-        y_rows = [rows_out(y_banks[0], by_vector, nc.vector.tensor_copy)]
+        y_rows = [y_tile(0, by_vector, nc.vector.tensor_copy)]
         dealt00 = deal_w2(0, 0)
-        y_rows.append(rows_out(y_banks[1], by_scalar, nc.scalar.copy))
+        y_rows.append(y_tile(1, by_scalar, nc.scalar.copy))
         gather_y(VECTOR, 0, 0, BANK)
-        y_rows.append(rows_out(y_banks[2], by_scalar, nc.scalar.copy))
-        e_pass(0, 0, dealt00)
+        y_rows.append(y_tile(2, by_scalar, nc.scalar.copy))
+        y_rows.append(y_tile(3, by_scalar, nc.scalar.copy))
+        quantise_w2(0, 0, dealt00)
+        e_pair(0, [0])
         dealt01 = deal_w2(0, 1)
-        y_rows.append(rows_out(y_banks[3], by_scalar, nc.scalar.copy))
         dealt10 = deal_w2(1, 0)
-        e_pass(0, 1, dealt01)
+        quantise_w2(0, 1, dealt01)
+        e_pair(0, [1])
         gather_y(SCALAR, 2, 0, BANK)
         gather_y(VECTOR, 1, 0, BANK)
         dealt11 = deal_w2(1, 1)
-        e_rows.append(rows_out(e_banks[0], by_scalar, nc.scalar.copy))
-        e_pass(1, 0, dealt10)
-        e_pass(1, 1, dealt11)
-        e_rows.append(rows_out(e_banks[1], by_scalar, nc.scalar.copy))
+        quantise_w2(1, 0, dealt10)
+        quantise_w2(1, 1, dealt11)
+        e_pair(1, range(PASSES))
         gather_y(VECTOR, 0, second, BANK)
+        for t in range(2):
+            e_rows.append(rows_out(e_banks[t], by_scalar, nc.scalar.copy))
         gather_y(SCALAR, 3, 0, BANK)
-        e_rows.append(rows_out(e_banks[2], by_scalar, nc.scalar.copy))
-        e_rows.append(rows_out(e_banks[3], by_scalar, nc.scalar.copy))
+        for t in range(2, PACK):
+            e_rows.append(rows_out(e_banks[t], by_scalar, nc.scalar.copy))
         for t in (1, 2, 3):
             gather_y(SCALAR, t, second, MIDDLE)
 

@@ -252,12 +252,13 @@ def tile_picked_hub_silu_p_kernel(
         quantise_w2(1, 1, dealt11)
         e_pair(1, range(PASSES))
         gather_y(VECTOR, 0, second, BANK)
+        gather_y(VECTOR, 1, second, MIDDLE)
         for t in range(2):
             e_rows.append(rows_out(e_banks[t], by_scalar, nc.scalar.copy))
         gather_y(SCALAR, 3, 0, BANK)
         for t in range(2, PACK):
             e_rows.append(rows_out(e_banks[t], by_scalar, nc.scalar.copy))
-        for t in (1, 2, 3):
+        for t in (2, 3):
             gather_y(SCALAR, t, second, MIDDLE)
 
         def activate(z_values, totals):

@@ -14,6 +14,7 @@ U8 = mybir.dt.uint8
 FP8X4 = mybir.dt.float8_e4m3fn_x4
 FP4X4 = mybir.dt.float4_e2m1fn_x4
 ADD = mybir.AluOpType.add
+MULT = mybir.AluOpType.mult
 COPY = mybir.ActivationFunctionType.Copy
 SILU = mybir.ActivationFunctionType.Silu
 
@@ -29,9 +30,9 @@ MIDDLE = 256
 TAIL = 128
 BANKS = 8
 SCALAR_SHARE = 160
-VECTOR_TILES = 20
+VECTOR_TILES = 19
 SCALAR_TILES = 16
-LOADS_BEHIND = {"behind_w1": 5, "behind_w3": 4}
+LOADS_BEHIND = {"behind_w1": 5, "behind_w3": 4, "behind_w2": 2}
 
 
 def tile_picked_hub_silu_p_kernel(
@@ -105,11 +106,11 @@ def tile_picked_hub_silu_p_kernel(
                 raw[:, :, c0:c1].rearrange("p j (m t) -> p m j t", t=PACK)[:, :, :, 2 * u : 2 * u + 2],
             )
 
-        def quantise_weights(mx, name, g, dealt, t0, calls):
+        def quantise_weights(mx, name, g, dealt, t0, calls, new_plane=held):
             flat = dealt[:].rearrange("p t m j -> p (t m j)")
             columns = flat.shape[1] // PACK
             codes = by_vector([P, columns], U32)
-            plane = held(name, [P, columns], U8)
+            plane = new_plane(name, [P, columns], U8)
             width = columns // calls
             for c in range(0, columns, width):
                 nc.vector.quantize_mx(
@@ -120,7 +121,7 @@ def tile_picked_hub_silu_p_kernel(
             for c in range(0, columns, P):
                 mx[g, t0 + c // P] = (codes[:, c : c + P], plane[:, c : c + P])
 
-        def hidden_pass(banks, mx, t, g):
+        def hidden_pass(banks, mx, t, g, first=0):
             codes, plane = mx[g, t]
             for b, bank in enumerate(banks):
                 nc.tensor.matmul_mx(
@@ -129,8 +130,8 @@ def tile_picked_hub_silu_p_kernel(
                     lhsT_scale=plane,
                     rhs=x_codes[g, b].bitcast(FP8X4),
                     rhs_scale=x_plane[:, g * S + b * BANK : g * S + (b + 1) * BANK],
-                    start=(g == 0),
-                    stop=(g == PASSES - 1),
+                    start=(g == first),
+                    stop=(g != first),
                 )
 
         def rows_out(banks, new_tile, first_copy):
@@ -202,20 +203,23 @@ def tile_picked_hub_silu_p_kernel(
                 nc.vector.tensor_copy(picked[:], window)
             y_at.append((t, r0, picked))
 
-        def deal_w2(u, g):
-            pair = by_vector([P, 2, P, PACK], BF16)
+        def second_pair(shape, dtype):
+            return keep.tile(shape, dtype, name="second_pair", align_bytes=64)
+
+        def deal_w2(new_tile, u, g):
+            pair = new_tile([P, 2, P, PACK], BF16)
             deal(nc.vector.tensor_copy, pair, w2_raw[g], u, 0, H)
             return pair
 
         def quantise_w2(u, g, dealt):
             quantise_weights(w2_mx, f"w2_plane{g}{u}", g, dealt, 2 * u, 1)
 
-        def e_pair(u, passes):
+        def e_pair(u, passes, first):
             for t in (2 * u, 2 * u + 1):
                 for g in passes:
-                    if g == 0:
+                    if g == first:
                         e_banks.append(banks_of(S // BANK))
-                    hidden_pass(e_banks[t], w2_mx, t, g)
+                    hidden_pass(e_banks[t], w2_mx, t, g, first)
 
         def add_gathered(total, t, r0):
             width = total.shape[1]
@@ -234,32 +238,36 @@ def tile_picked_hub_silu_p_kernel(
         SCALAR, VECTOR = True, False
         w2_mx, e_banks, e_rows = {}, [], []
         y_rows = [y_tile(0, by_vector, nc.vector.tensor_copy)]
-        dealt00 = deal_w2(0, 0)
+        dealt00 = deal_w2(by_vector, 0, 0)
         y_rows.append(y_tile(1, by_scalar, nc.scalar.copy))
         gather_y(VECTOR, 0, 0, BANK)
         y_rows.append(y_tile(2, by_scalar, nc.scalar.copy))
         y_rows.append(y_tile(3, by_scalar, nc.scalar.copy))
         quantise_w2(0, 0, dealt00)
-        e_pair(0, [0])
-        dealt01 = deal_w2(0, 1)
-        dealt10 = deal_w2(1, 0)
+        e_pair(0, [0], 0)
+        dealt01 = deal_w2(by_vector, 0, 1)
+        dealt11 = deal_w2(second_pair, 1, 1)
         quantise_w2(0, 1, dealt01)
-        e_pair(0, [1])
+        e_pair(0, [1], 0)
+        quantise_w2(1, 1, dealt11)
+        e_pair(1, [1], 1)
+        dealt10 = second_pair([P, 2, P, PACK], BF16)
+        for e in range(2):
+            columns = w2_raw[0][:].rearrange("p j (m t) -> p m j t", t=PACK)[:, :, :, 2 + e]
+            nc.gpsimd.tensor_scalar(dealt10[:, e], columns, 1.0, 0.0, MULT, ADD)
         gather_y(SCALAR, 2, 0, BANK)
         gather_y(VECTOR, 1, 0, BANK)
-        dealt11 = deal_w2(1, 1)
-        quantise_w2(1, 0, dealt10)
-        quantise_w2(1, 1, dealt11)
-        e_pair(1, range(PASSES))
         gather_y(VECTOR, 0, second, BANK)
-        gather_y(VECTOR, 1, second, MIDDLE)
+        gather_y(VECTOR, 1, second, BANK)
+        quantise_weights(w2_mx, "behind_w2", 0, dealt10, 2, 1, behind)
+        e_pair(1, [0], 1)
         for t in range(2):
             e_rows.append(rows_out(e_banks[t], by_scalar, nc.scalar.copy))
         gather_y(SCALAR, 3, 0, BANK)
+        gather_y(SCALAR, 2, second, MIDDLE)
         for t in range(2, PACK):
             e_rows.append(rows_out(e_banks[t], by_scalar, nc.scalar.copy))
-        for t in (2, 3):
-            gather_y(SCALAR, t, second, MIDDLE)
+        gather_y(SCALAR, 3, second, MIDDLE)
 
         def activate(z_values, totals):
             nc.scalar.activation(
@@ -305,7 +313,7 @@ def tile_picked_hub_silu_p_kernel(
         on_vector = (by_vector, nc.vector.tensor_copy)
 
         half = BANK // 2
-        first_totals = held("first_totals", [P, PACK, BANK], F32)
+        first_totals = behind("behind_w2", [P, PACK, BANK], F32)
         for t in range(PACK - 1):
             add_gathered(first_totals[:, t, :], t, 0)
         for r0 in (0, half):
@@ -317,7 +325,6 @@ def tile_picked_hub_silu_p_kernel(
         second_totals = sums(second, MIDDLE)
         for t in (2, 3):
             gather_y(SCALAR, t, third, 2 * TAIL)
-        gather_y(VECTOR, 1, third, 2 * TAIL)
         z_second = activated(second_totals)
         first_out = last_product(z_first, 0, a_bank_each)
         last_totals = by_vector([P, PACK, 2 * TAIL], F32)

@@ -28,10 +28,10 @@ LIST = 16
 ROW_TILES = N // P
 MIDDLE = 256
 TAIL = 128
-BANKS = 8
-SCALAR_SHARE = 160
-VECTOR_TILES = 19
-SCALAR_TILES = 16
+BANKS = {"early_bank": 6, "spare_bank": 2}
+SCALAR_SHARE = 192
+VECTOR_TILES = 20
+SCALAR_TILES = 15
 LOADS_BEHIND = {"behind_w1": 5, "behind_w3": 4, "behind_w2": 2}
 
 
@@ -45,7 +45,7 @@ def tile_picked_hub_silu_p_kernel(
         vector_out = ctx.enter_context(tc.tile_pool(name="vector_out", bufs=VECTOR_TILES))
         scalar_out = ctx.enter_context(tc.tile_pool(name="scalar_out", bufs=SCALAR_TILES))
         late_loads = ctx.enter_context(tc.tile_pool(name="late_loads", bufs=1))
-        psum = ctx.enter_context(tc.psum_pool(name="psum", bufs=BANKS))
+        psum = ctx.enter_context(tc.psum_pool(name="psum", bufs=1))
 
         def held(name, shape, dtype):
             return keep.tile(shape, dtype, name=name, align_bytes=64)
@@ -59,8 +59,8 @@ def tile_picked_hub_silu_p_kernel(
         def by_scalar(shape, dtype):
             return scalar_out.tile(shape, dtype, name="by_scalar", align_bytes=64)
 
-        def banks_of(count):
-            return [psum.tile([P, BANK], F32, name="bank") for b in range(count)]
+        def banks_of(count, tag="early_bank"):
+            return [psum.tile([P, BANK], F32, name=tag, bufs=BANKS[tag]) for b in range(count)]
 
         def entries(list_tile, r0, width):
             return list_tile[:, r0 // LIST : (r0 + width) // LIST]
@@ -150,26 +150,26 @@ def tile_picked_hub_silu_p_kernel(
         gather_words(0, 0, S)
 
         w1_mx = {}
-        pairs = [behind("behind_w1", [P, 2, P, PACK], BF16), by_scalar([P, 2, P, PACK], BF16)]
+        pairs = [behind("behind_w1", [P, 2, P, PACK], BF16), by_vector([P, 2, P, PACK], BF16)]
         deal(nc.scalar.copy, pairs[0], w1_raw[0], 0, 0, H)
         w1_raw.append(load_weights(behind, "behind_w1", w1, 1))
         src_sb = behind("behind_w1", [P, S // LIST], U16)
         nc.sync.dma_start(src_sb[:], src)
         w2_raw = [load_weights(behind, "behind_w1", w2, g) for g in range(PASSES)]
-        deal(nc.scalar.copy, pairs[1], w1_raw[0], 1, 0, H)
+        deal(nc.vector.tensor_copy, pairs[1], w1_raw[0], 1, 0, H)
         y_banks = []
         quantise_weights(w1_mx, "w1_plane00", 0, pairs[0], 0, 1)
+        quantise_weights(w1_mx, "w1_plane01", 0, pairs[1], 2, 1)
         gather_words(1, 0, S)
-        first_pass_pair = pairs[1]
-        for t in range(2):
+        for t in range(3):
             y_banks.append(banks_of(S // BANK))
             hidden_pass(y_banks[t], w1_mx, t, 0)
 
         pairs = [behind("behind_w3", [P, 2, P, PACK], BF16), held("w1_last_pair", [P, 2, P, PACK], BF16)]
         deal(nc.scalar.copy, pairs[0], w1_raw[1], 0, 0, SCALAR_SHARE)
         deal(nc.vector.tensor_copy, pairs[0], w1_raw[1], 0, SCALAR_SHARE, H)
-        deal(nc.vector.tensor_copy, pairs[1], w1_raw[1], 1, H // 2, H)
-        deal(nc.scalar.copy, pairs[1], w1_raw[1], 1, 0, H // 2)
+        deal(nc.vector.tensor_copy, pairs[1], w1_raw[1], 1, H - SCALAR_SHARE, H)
+        deal(nc.scalar.copy, pairs[1], w1_raw[1], 1, 0, H - SCALAR_SHARE)
         dst_sb = behind("behind_w3", [P, S // LIST], U16)
         nc.sync.dma_start(dst_sb[:], dst)
         w3_codes = behind("behind_w3", [P, 2 * N], U8)
@@ -181,11 +181,10 @@ def tile_picked_hub_silu_p_kernel(
                 w3_plane[32 * q : 32 * q + 4, :].bitcast(I32), w3_scales[0, 4 * q : 4 * q + 4, :].bitcast(I32)
             )
         quantise_weights(w1_mx, "w1_plane10", 1, pairs[0], 0, 2)
-        quantise_weights(w1_mx, "w1_plane01", 0, first_pass_pair, 2, 1)
         quantise_weights(w1_mx, "w1_plane11", 1, pairs[1], 2, 1)
 
         def y_tile(t, new_tile, first_copy):
-            if t >= 2:
+            if t >= 3:
                 y_banks.append(banks_of(S // BANK))
                 hidden_pass(y_banks[t], w1_mx, t, 0)
             hidden_pass(y_banks[t], w1_mx, t, 1)
@@ -218,7 +217,7 @@ def tile_picked_hub_silu_p_kernel(
             for t in (2 * u, 2 * u + 1):
                 for g in passes:
                     if g == first:
-                        e_banks.append(banks_of(S // BANK))
+                        e_banks.append(banks_of(S // BANK, "spare_bank" if t == 0 else "early_bank"))
                     hidden_pass(e_banks[t], w2_mx, t, g, first)
 
         def add_gathered(total, t, r0):

@@ -350,5 +350,5 @@ def tile_picked_hub_silu_p_kernel(
         store(second_out[0], out_view[:, 0, second:third], *on_scalar)
         store(second_out[1], out_view[:, 1, second:third], *on_vector)
         store(third_out, out_view[:, :, third:fourth], *on_scalar)
-        store(fourth_out[0], out_view[:, 0, fourth:], *on_scalar, nc.scalar)
-        store(fourth_out[1], out_view[:, 1, fourth:], *on_vector)
+        store(fourth_out[0], out_view[:, 0, fourth:], *on_vector)
+        store(fourth_out[1], out_view[:, 1, fourth:], *on_scalar, nc.scalar)

@@ -348,7 +348,9 @@ def tile_picked_hub_silu_p_kernel(
         fourth_out = last_product(z_fourth, fourth, a_bank_each)
 
         store(second_out[0], out_view[:, 0, second:third], *on_scalar)
-        store(second_out[1], out_view[:, 1, second:third], *on_vector)
-        store(third_out, out_view[:, :, third:fourth], *on_scalar)
-        store(fourth_out[0], out_view[:, 0, fourth:], *on_vector)
-        store(fourth_out[1], out_view[:, 1, fourth:], *on_scalar, nc.scalar)
+        store(second_out[1], out_view[:, 1, second:third], *on_scalar)
+        store(third_out, out_view[:, :, third:fourth], *on_vector)
+        last_rows = by_scalar([P, ROW_TILES, TAIL], F32)
+        for a in range(ROW_TILES):
+            nc.scalar.copy(last_rows[:, a, :], fourth_out[a])
+        nc.scalar.dma_start(out_view[:, :, fourth:], last_rows[:])

@@ -270,8 +270,8 @@ def tile_picked_hub_silu_p_kernel(
 
         def activate(z_values, totals):
             nc.scalar.activation(
-                z_values.rearrange("p (c i t) -> p c t i", i=4, t=PACK),
-                totals.rearrange("p t (c i) -> p c t i", i=4),
+                z_values.rearrange("p (c i t) -> p c t i", i=2, t=PACK),
+                totals.rearrange("p t (c i) -> p c t i", i=2),
                 SILU,
             )
 

@@ -31,7 +31,7 @@ TAIL = 128
 BANKS = {"early_bank": 6, "spare_bank": 2}
 SCALAR_SHARE = 192
 VECTOR_TILES = 20
-SCALAR_TILES = 15
+SCALAR_TILES = 14
 LOADS_BEHIND = {"behind_w1": 5, "behind_w3": 4, "behind_w2": 2}
 
 
@@ -50,8 +50,11 @@ def tile_picked_hub_silu_p_kernel(
         def held(name, shape, dtype):
             return keep.tile(shape, dtype, name=name, align_bytes=64)
 
+        def loaded(name, shape, dtype):
+            return keep.tile(shape, dtype, name=name, align_bytes=256)
+
         def behind(tag, shape, dtype):
-            return late_loads.tile(shape, dtype, name=tag, align_bytes=64, bufs=LOADS_BEHIND[tag])
+            return late_loads.tile(shape, dtype, name=tag, align_bytes=256, bufs=LOADS_BEHIND[tag])
 
         def by_vector(shape, dtype):
             return vector_out.tile(shape, dtype, name="by_vector", align_bytes=64)
@@ -66,11 +69,11 @@ def tile_picked_hub_silu_p_kernel(
             return list_tile[:, r0 // LIST : (r0 + width) // LIST]
 
         offs_sb = lists.tile([P, S // LIST], U16, name="offs_sb")
-        x_table = [held(f"x_table{g}", [P, T], U32) for g in range(PASSES)]
-        x_scale_table = held("x_scale_table", [P, T], U8)
+        x_table = [loaded(f"x_table{g}", [P, T], U32) for g in range(PASSES)]
+        x_scale_table = loaded("x_scale_table", [P, T], U8)
         nc.vector.memset(x_scale_table[32:64, :].bitcast(I32), 0)
         nc.vector.memset(x_scale_table[64:, :].bitcast(I32), 0)
-        x_plane = held("x_plane", [P, PASSES * S], U8)
+        x_plane = loaded("x_plane", [P, PASSES * S], U8)
         nc.gpsimd.memset(x_plane[:].bitcast(I32), 0)
 
         warm_in = held("warm_in", [P, 1], F32)
@@ -89,7 +92,7 @@ def tile_picked_hub_silu_p_kernel(
         nc.sync.dma_start(offs_sb[:], offs)
         nc.sync.dma_start(x_scale_table[:32, :].bitcast(I32), x_scales.bitcast(I32).rearrange("g b c -> b g c"))
         load_words(0)
-        w1_raw = [load_weights(held, "w1_raw0", w1, 0)]
+        w1_raw = [load_weights(loaded, "w1_raw0", w1, 0)]
         load_words(1)
 
         x_codes = {}
@@ -266,7 +269,7 @@ def tile_picked_hub_silu_p_kernel(
         gather_y(SCALAR, 2, second, MIDDLE)
         for t in range(2, PACK):
             e_rows.append(rows_out(e_banks[t], by_scalar, nc.scalar.copy))
-        gather_y(SCALAR, 3, second, MIDDLE)
+        gather_y(SCALAR, 3, second, BANK)
 
         def activate(z_values, totals):
             nc.scalar.activation(
@@ -322,8 +325,7 @@ def tile_picked_hub_silu_p_kernel(
             activate(z_first[:, PACK * r0 : PACK * (r0 + half)], first_totals[:, :, r0 : r0 + half])
 
         second_totals = sums(second, MIDDLE)
-        for t in (2, 3):
-            gather_y(SCALAR, t, third, 2 * TAIL)
+        gather_y(SCALAR, 2, third, 2 * TAIL)
         z_second = activated(second_totals)
         first_out = last_product(z_first, 0, a_bank_each)
         last_totals = by_vector([P, PACK, 2 * TAIL], F32)
@@ -351,6 +353,6 @@ def tile_picked_hub_silu_p_kernel(
         store(second_out[1], out_view[:, 1, second:third], *on_scalar)
         store(third_out, out_view[:, :, third:fourth], *on_vector)
         last_rows = by_scalar([P, ROW_TILES, TAIL], F32)
-        for a in range(ROW_TILES):
-            nc.scalar.copy(last_rows[:, a, :], fourth_out[a])
+        nc.scalar.copy(last_rows[:, 0, :], fourth_out[0])
+        nc.vector.tensor_copy(last_rows[:, 1, :], fourth_out[1])
         nc.scalar.dma_start(out_view[:, :, fourth:], last_rows[:])

@@ -57,10 +57,10 @@ def tile_picked_hub_silu_p_kernel(
             return late_loads.tile(shape, dtype, name=tag, align_bytes=256, bufs=LOADS_BEHIND[tag])
 
         def by_vector(shape, dtype):
-            return vector_out.tile(shape, dtype, name="by_vector", align_bytes=64)
+            return vector_out.tile(shape, dtype, name="by_vector", align_bytes=256)
 
         def by_scalar(shape, dtype):
-            return scalar_out.tile(shape, dtype, name="by_scalar", align_bytes=64)
+            return scalar_out.tile(shape, dtype, name="by_scalar", align_bytes=256)
 
         def banks_of(count, tag="early_bank"):
             return [psum.tile([P, BANK], F32, name=tag, bufs=BANKS[tag]) for b in range(count)]
@@ -105,8 +105,8 @@ def tile_picked_hub_silu_p_kernel(
 
         def deal(copy, pair, raw, u, c0, c1):
             copy(
-                pair[:, :, c0 // PACK : c1 // PACK, :].rearrange("p e m j -> p m j e"),
-                raw[:, :, c0:c1].rearrange("p j (m t) -> p m j t", t=PACK)[:, :, :, 2 * u : 2 * u + 2],
+                pair[:, :, c0 // PACK : c1 // PACK, :].rearrange("p e m (h i) -> p m h e i", i=2),
+                raw[:, :, c0:c1].rearrange("p (h i) (m t) -> p m h t i", i=2, t=PACK)[:, :, :, 2 * u : 2 * u + 2, :],
             )
 
         def quantise_weights(mx, name, g, dealt, t0, calls, new_plane=held):

@@ -28,7 +28,7 @@ LIST = 16
 ROW_TILES = N // P
 MIDDLE = 256
 TAIL = 128
-BANKS = {"early_bank": 6, "spare_bank": 2}
+BANKS = {"early_bank": 4, "even_bank": 2, "odd_bank": 2}
 SCALAR_SHARE = 192
 VECTOR_TILES = 20
 SCALAR_TILES = 14
@@ -105,8 +105,8 @@ def tile_picked_hub_silu_p_kernel(
 
         def deal(copy, pair, raw, u, c0, c1):
             copy(
-                pair[:, :, c0 // PACK : c1 // PACK, :].rearrange("p e m (h i) -> p m h e i", i=2),
-                raw[:, :, c0:c1].rearrange("p (h i) (m t) -> p m h t i", i=2, t=PACK)[:, :, :, 2 * u : 2 * u + 2, :],
+                pair[:, :, c0 // PACK : c1 // PACK, :].rearrange("p e m j -> p m j e"),
+                raw[:, :, c0:c1].rearrange("p j (m t) -> p m j t", t=PACK)[:, :, :, 2 * u : 2 * u + 2],
             )
 
         def quantise_weights(mx, name, g, dealt, t0, calls, new_plane=held):
@@ -156,16 +156,17 @@ def tile_picked_hub_silu_p_kernel(
         pairs = [behind("behind_w1", [P, 2, P, PACK], BF16), by_vector([P, 2, P, PACK], BF16)]
         deal(nc.scalar.copy, pairs[0], w1_raw[0], 0, 0, H)
         w1_raw.append(load_weights(behind, "behind_w1", w1, 1))
+        w2_raw = [load_weights(behind, "behind_w1", w2, 0)]
         src_sb = behind("behind_w1", [P, S // LIST], U16)
         nc.sync.dma_start(src_sb[:], src)
-        w2_raw = [load_weights(behind, "behind_w1", w2, g) for g in range(PASSES)]
+        w2_raw.append(load_weights(behind, "behind_w1", w2, 1))
         deal(nc.vector.tensor_copy, pairs[1], w1_raw[0], 1, 0, H)
         y_banks = []
         quantise_weights(w1_mx, "w1_plane00", 0, pairs[0], 0, 1)
         quantise_weights(w1_mx, "w1_plane01", 0, pairs[1], 2, 1)
         gather_words(1, 0, S)
         for t in range(3):
-            y_banks.append(banks_of(S // BANK))
+            y_banks.append(banks_of(S // BANK, "odd_bank" if t == 1 else "early_bank"))
             hidden_pass(y_banks[t], w1_mx, t, 0)
 
         pairs = [behind("behind_w3", [P, 2, P, PACK], BF16), held("w1_last_pair", [P, 2, P, PACK], BF16)]
@@ -220,7 +221,7 @@ def tile_picked_hub_silu_p_kernel(
             for t in (2 * u, 2 * u + 1):
                 for g in passes:
                     if g == first:
-                        e_banks.append(banks_of(S // BANK, "spare_bank" if t == 0 else "early_bank"))
+                        e_banks.append(banks_of(S // BANK, "odd_bank" if t % 2 else "even_bank"))
                     hidden_pass(e_banks[t], w2_mx, t, g, first)
 
         def add_gathered(total, t, r0):
@@ -287,7 +288,7 @@ def tile_picked_hub_silu_p_kernel(
             width = z_values.shape[1] // PACK
             z_codes = by_vector([P, width], U32)
             z_plane = held(f"z_plane{r0}", [P, width], U8)
-            nc.vector.quantize_mx(out=z_codes[:].bitcast(FP8X4), scales=z_plane[:], in_=z_values[:])
+            nc.vector.quantize_mx(out=z_codes[:].bitcast(FP8X4), scales=z_plane[:], in_=z_values[:, :])
             products = places(width)
             for a in range(ROW_TILES):
                 nc.tensor.matmul_mx(
@@ -303,6 +304,12 @@ def tile_picked_hub_silu_p_kernel(
 
         def a_bank_each(width):
             return [bank[:, :width] for bank in banks_of(ROW_TILES)]
+
+        def both_rows(z_values, r0, tag="early_bank"):
+            width = z_values.shape[1] // PACK
+            rows = banks_of(1, tag)[0][:, : ROW_TILES * width].rearrange("p (a r) -> p a r", a=ROW_TILES)
+            last_product(z_values, r0, lambda width: [rows[:, a, :] for a in range(ROW_TILES)])
+            return rows
 
         out_view = out.rearrange("(a p) r -> p a r", p=P)
 
@@ -327,27 +334,20 @@ def tile_picked_hub_silu_p_kernel(
         second_totals = sums(second, MIDDLE)
         gather_y(SCALAR, 2, third, 2 * TAIL)
         z_second = activated(second_totals)
-        first_out = last_product(z_first, 0, a_bank_each)
+        first_out = [both_rows(z_first[:, PACK * r0 : PACK * (r0 + half)], r0) for r0 in (0, half)]
         last_totals = by_vector([P, PACK, 2 * TAIL], F32)
         for t in range(2):
             add_gathered(last_totals[:, t, :], t, third)
         for r0 in (0, TAIL):
             for t in range(2, PACK):
                 add_gathered(last_totals[:, t, r0 : r0 + TAIL], t, third + r0)
-        store(first_out[0], out_view[:, 0, :second], *on_scalar)
-        store(first_out[1], out_view[:, 1, :second], *on_scalar)
+        store(first_out[0], out_view[:, :, :half], *on_scalar)
+        store(first_out[1], out_view[:, :, half:second], *on_scalar)
         z_third = activated(last_totals[:, :, :TAIL])
         z_fourth = activated(last_totals[:, :, TAIL:])
         second_out = last_product(z_second, second, a_bank_each)
-        shared = []
-
-        def side_by_side(width):
-            shared.extend(banks_of(1))
-            return [shared[0][:, a * width : (a + 1) * width] for a in range(ROW_TILES)]
-
-        last_product(z_third, third, side_by_side)
-        third_out = shared[0][:, : ROW_TILES * TAIL].rearrange("p (a r) -> p a r", a=ROW_TILES)
-        fourth_out = last_product(z_fourth, fourth, a_bank_each)
+        third_out = both_rows(z_third, third, "odd_bank")
+        fourth_out = last_product(z_fourth, fourth, lambda width: [bank[:, :width] for bank in banks_of(2, "even_bank")])
 
         store(second_out[0], out_view[:, 0, second:third], *on_scalar)
         store(second_out[1], out_view[:, 1, second:third], *on_scalar)

@@ -89,8 +89,8 @@ def tile_picked_hub_silu_p_kernel(
             nc.sync.dma_start(raw[:], w[g * K_PASS : (g + 1) * K_PASS, :].rearrange("(p j) c -> p j c", j=PACK))
             return raw
 
-        nc.sync.dma_start(offs_sb[:], offs)
         nc.sync.dma_start(x_scale_table[:32, :].bitcast(I32), x_scales.bitcast(I32).rearrange("g b c -> b g c"))
+        nc.sync.dma_start(offs_sb[:], offs)
         load_words(0)
         w1_raw = [load_weights(loaded, "w1_raw0", w1, 0)]
         load_words(1)
@@ -160,7 +160,8 @@ def tile_picked_hub_silu_p_kernel(
         src_sb = behind("behind_w1", [P, S // LIST], U16)
         nc.sync.dma_start(src_sb[:], src)
         w2_raw.append(load_weights(behind, "behind_w1", w2, 1))
-        deal(nc.vector.tensor_copy, pairs[1], w1_raw[0], 1, 0, H)
+        deal(nc.vector.tensor_copy, pairs[1], w1_raw[0], 1, H - SCALAR_SHARE, H)
+        deal(nc.scalar.copy, pairs[1], w1_raw[0], 1, 0, H - SCALAR_SHARE)
         y_banks = []
         quantise_weights(w1_mx, "w1_plane00", 0, pairs[0], 0, 1)
         quantise_weights(w1_mx, "w1_plane01", 0, pairs[1], 2, 1)

@@ -256,9 +256,8 @@ def tile_picked_hub_silu_p_kernel(
         quantise_w2(1, 1, dealt11)
         e_pair(1, [1], 1)
         dealt10 = second_pair([P, 2, P, PACK], BF16)
-        for e in range(2):
-            columns = w2_raw[0][:].rearrange("p j (m t) -> p m j t", t=PACK)[:, :, :, 2 + e]
-            nc.gpsimd.tensor_scalar(dealt10[:, e], columns, 1.0, 0.0, MULT, ADD)
+        columns = w2_raw[0][:].rearrange("p j (m t) -> p t m j", t=PACK)[:, 2:]
+        nc.gpsimd.tensor_scalar(dealt10[:], columns, 1.0, 0.0, MULT, ADD)
         gather_y(SCALAR, 2, 0, BANK)
         gather_y(VECTOR, 1, 0, BANK)
         gather_y(VECTOR, 0, second, BANK)

from contextlib import ExitStack

import concourse.mybir as mybir

K, T, S, H, N = 1024, 2048, 1024, 512, 256
FLOPS = 2 * (2 * K * H * S + H * N * S)

F32 = mybir.dt.float32
BF16 = mybir.dt.bfloat16
I32 = mybir.dt.int32
U32 = mybir.dt.uint32
U16 = mybir.dt.uint16
U8 = mybir.dt.uint8
FP8X4 = mybir.dt.float8_e4m3fn_x4
FP4X4 = mybir.dt.float4_e2m1fn_x4
ADD = mybir.AluOpType.add
MULT = mybir.AluOpType.mult
COPY = mybir.ActivationFunctionType.Copy
SILU = mybir.ActivationFunctionType.Silu

P = 128
PACK = 4
K_PASS = P * PACK
PASSES = K // K_PASS
QUADRANTS = 4
BANK = 512
LIST = 16
ROW_TILES = N // P
MIDDLE = 256
TAIL = 128
BANKS = {"early_bank": 4, "even_bank": 2, "odd_bank": 2}
SCALAR_SHARE = 192
VECTOR_TILES = 20
SCALAR_TILES = 14
LOADS_BEHIND = {"behind_w1": 5, "behind_w3": 4, "behind_w2": 2}


def tile_picked_hub_silu_p_kernel(
    tc, x_words, x_scales, w1, w2, w3_words, w3_scales, offs, src, dst, out
):
    nc = tc.nc
    with ExitStack() as ctx:
        lists = ctx.enter_context(tc.tile_pool(name="lists", bufs=1))
        keep = ctx.enter_context(tc.tile_pool(name="keep", bufs=1))
        vector_out = ctx.enter_context(tc.tile_pool(name="vector_out", bufs=VECTOR_TILES))
        scalar_out = ctx.enter_context(tc.tile_pool(name="scalar_out", bufs=SCALAR_TILES))
        late_loads = ctx.enter_context(tc.tile_pool(name="late_loads", bufs=1))
        psum = ctx.enter_context(tc.psum_pool(name="psum", bufs=1))

        def held(name, shape, dtype):
            return keep.tile(shape, dtype, name=name, align_bytes=64)

        def loaded(name, shape, dtype):
            return keep.tile(shape, dtype, name=name, align_bytes=256)

        def behind(tag, shape, dtype):
            return late_loads.tile(shape, dtype, name=tag, align_bytes=256, bufs=LOADS_BEHIND[tag])

        def by_vector(shape, dtype):
            return vector_out.tile(shape, dtype, name="by_vector", align_bytes=256)

        def by_scalar(shape, dtype):
            return scalar_out.tile(shape, dtype, name="by_scalar", align_bytes=256)

        def banks_of(count, tag="early_bank"):
            return [psum.tile([P, BANK], F32, name=tag, bufs=BANKS[tag]) for b in range(count)]

        def entries(list_tile, r0, width):
            return list_tile[:, r0 // LIST : (r0 + width) // LIST]

        offs_sb = lists.tile([P, S // LIST], U16, name="offs_sb")
        x_table = [loaded(f"x_table{g}", [P, T], U32) for g in range(PASSES)]
        x_scale_table = loaded("x_scale_table", [P, T], U8)
        nc.vector.memset(x_scale_table[32:64, :].bitcast(I32), 0)
        nc.vector.memset(x_scale_table[64:, :].bitcast(I32), 0)
        x_plane = loaded("x_plane", [P, PASSES * S], U8)
        nc.gpsimd.memset(x_plane[:].bitcast(I32), 0)

        warm_in = held("warm_in", [P, 1], F32)
        warm_out = held("warm_out", [P, 1], F32)
        nc.gpsimd.memset(warm_in[:], 0.0)
        nc.scalar.activation(warm_out[:], warm_in[:], SILU)

        def load_words(g):
            nc.sync.dma_start(x_table[g][:].bitcast(I32), x_words[g].rearrange("p n t -> p (n t)").bitcast(I32))

        def load_weights(new_tile, name, w, g):
            raw = new_tile(name, [P, PACK, H], F32)
            nc.sync.dma_start(raw[:], w[g * K_PASS : (g + 1) * K_PASS, :].rearrange("(p j) c -> p j c", j=PACK))
            return raw

        nc.sync.dma_start(x_scale_table[:32, :].bitcast(I32), x_scales.bitcast(I32).rearrange("g b c -> b g c"))
        nc.sync.dma_start(offs_sb[:], offs)
        load_words(0)
        w1_raw = [load_weights(loaded, "w1_raw0", w1, 0)]
        load_words(1)

        x_codes = {}

        def gather_words(g, r0, width):
            words = by_vector([P, width], U32)
            nc.vector.tensor_copy(words[:], x_table[g][:].indirect(entries(offs_sb, r0, width)))
            for c in range(0, width, BANK):
                x_codes[g, (r0 + c) // BANK] = words[:, c : c + BANK]

        def deal(copy, pair, raw, u, c0, c1):
            copy(
                pair[:, :, c0 // PACK : c1 // PACK, :].rearrange("p e m j -> p m j e"),
                raw[:, :, c0:c1].rearrange("p j (m t) -> p m j t", t=PACK)[:, :, :, 2 * u : 2 * u + 2],
            )

        def quantise_weights(mx, name, g, dealt, t0, calls, new_plane=held):
            flat = dealt[:].rearrange("p t m j -> p (t m j)")
            columns = flat.shape[1] // PACK
            codes = by_vector([P, columns], U32)
            plane = new_plane(name, [P, columns], U8)
            width = columns // calls
            for c in range(0, columns, width):
                nc.vector.quantize_mx(
                    out=codes[:, c : c + width].bitcast(FP8X4),
                    scales=plane[:, c : c + width],
                    in_=flat[:, PACK * c : PACK * (c + width)],
                )
            for c in range(0, columns, P):
                mx[g, t0 + c // P] = (codes[:, c : c + P], plane[:, c : c + P])

        def hidden_pass(banks, mx, t, g, first=0):
            codes, plane = mx[g, t]
            for b, bank in enumerate(banks):
                nc.tensor.matmul_mx(
                    out=bank[:],
                    lhsT=codes.bitcast(FP8X4),
                    lhsT_scale=plane,
                    rhs=x_codes[g, b].bitcast(FP8X4),
                    rhs_scale=x_plane[:, g * S + b * BANK : g * S + (b + 1) * BANK],
                    start=(g == first),
                    stop=(g != first),
                )

        def rows_out(banks, new_tile, first_copy):
            rows = new_tile([P, S], F32)
            first_copy(rows[:, :BANK], banks[0][:])
            nc.scalar.copy(rows[:, BANK:S], banks[1][:])
            return rows

        picked_scales = by_vector([P, S], U8)
        nc.vector.tensor_copy(picked_scales[:], x_scale_table[:].indirect(offs_sb[:]))
        for q in (0, 2, 1, 3):
            nc.sync.dma_start(
                x_plane[32 * q : 32 * q + 4, :].bitcast(I32).rearrange("p (g c) -> p g c", g=PASSES),
                picked_scales[8 * q : 8 * q + 8, :].bitcast(I32),
            )
        gather_words(0, 0, S)

        w1_mx = {}
        pairs = [behind("behind_w1", [P, 2, P, PACK], BF16), by_vector([P, 2, P, PACK], BF16)]
        deal(nc.scalar.copy, pairs[0], w1_raw[0], 0, 0, H)
        w1_raw.append(load_weights(behind, "behind_w1", w1, 1))
        w2_raw = [load_weights(behind, "behind_w1", w2, 0)]
        src_sb = behind("behind_w1", [P, S // LIST], U16)
        nc.sync.dma_start(src_sb[:], src)
        w2_raw.append(load_weights(behind, "behind_w1", w2, 1))
        deal(nc.vector.tensor_copy, pairs[1], w1_raw[0], 1, H - SCALAR_SHARE, H)
        deal(nc.scalar.copy, pairs[1], w1_raw[0], 1, 0, H - SCALAR_SHARE)
        y_banks = []
        quantise_weights(w1_mx, "w1_plane00", 0, pairs[0], 0, 1)
        quantise_weights(w1_mx, "w1_plane01", 0, pairs[1], 2, 1)
        gather_words(1, 0, S)
        for t in range(3):
            y_banks.append(banks_of(S // BANK, "odd_bank" if t == 1 else "early_bank"))
            hidden_pass(y_banks[t], w1_mx, t, 0)

        pairs = [behind("behind_w3", [P, 2, P, PACK], BF16), held("w1_last_pair", [P, 2, P, PACK], BF16)]
        deal(nc.scalar.copy, pairs[0], w1_raw[1], 0, 0, SCALAR_SHARE)
        deal(nc.vector.tensor_copy, pairs[0], w1_raw[1], 0, SCALAR_SHARE, H)
        deal(nc.vector.tensor_copy, pairs[1], w1_raw[1], 1, H - SCALAR_SHARE, H)
        deal(nc.scalar.copy, pairs[1], w1_raw[1], 1, 0, H - SCALAR_SHARE)
        dst_sb = behind("behind_w3", [P, S // LIST], U16)
        nc.sync.dma_start(dst_sb[:], dst)
        w3_codes = behind("behind_w3", [P, 2 * N], U8)
        w3_plane = behind("behind_w3", [P, N], U8)
        nc.gpsimd.memset(w3_plane[:].bitcast(I32), 0)
        nc.sync.dma_start(w3_codes[:].bitcast(I32), w3_words[0].bitcast(I32))
        for q in range(QUADRANTS):
            nc.sync.dma_start(
                w3_plane[32 * q : 32 * q + 4, :].bitcast(I32), w3_scales[0, 4 * q : 4 * q + 4, :].bitcast(I32)
            )
        quantise_weights(w1_mx, "w1_plane10", 1, pairs[0], 0, 2)
        quantise_weights(w1_mx, "w1_plane11", 1, pairs[1], 2, 1)

        def y_tile(t, new_tile, first_copy):
            if t >= 3:
                y_banks.append(banks_of(S // BANK))
                hidden_pass(y_banks[t], w1_mx, t, 0)
            hidden_pass(y_banks[t], w1_mx, t, 1)
            return rows_out(y_banks[t], new_tile, first_copy)

        y_at = []

        def gather_y(on_scalar_engine, t, r0, width):
            window = y_rows[t][:].indirect(entries(src_sb, r0, width))
            if on_scalar_engine:
                picked = by_scalar([P, width], F32)
                nc.scalar.activation(picked[:], window, COPY)
            else:
                picked = by_vector([P, width], F32)
                nc.vector.tensor_copy(picked[:], window)
            y_at.append((t, r0, picked))

        def second_pair(shape, dtype):
            return keep.tile(shape, dtype, name="second_pair", align_bytes=64)

        def deal_w2(new_tile, u, g):
            pair = new_tile([P, 2, P, PACK], BF16)
            deal(nc.vector.tensor_copy, pair, w2_raw[g], u, 0, H)
            return pair

        def quantise_w2(u, g, dealt):
            quantise_weights(w2_mx, f"w2_plane{g}{u}", g, dealt, 2 * u, 1)

        def e_pair(u, passes, first):
            for t in (2 * u, 2 * u + 1):
                for g in passes:
                    if g == first:
                        e_banks.append(banks_of(S // BANK, "odd_bank" if t % 2 else "even_bank"))
                    hidden_pass(e_banks[t], w2_mx, t, g, first)

        def add_gathered(total, t, r0):
            width = total.shape[1]
            e_side = e_rows[t][:].indirect(entries(dst_sb, r0, width))
            for tile_t, first, picked in y_at:
                if tile_t == t and first <= r0 < first + picked.shape[1]:
                    nc.vector.tensor_tensor(total, e_side, picked[:, r0 - first : r0 - first + width], ADD)

        def sums(r0, width):
            totals = by_vector([P, PACK, width], F32)
            for t in range(PACK):
                add_gathered(totals[:, t, :], t, r0)
            return totals

        second, third, fourth = BANK, BANK + MIDDLE, BANK + MIDDLE + TAIL
        SCALAR, VECTOR = True, False
        w2_mx, e_banks, e_rows = {}, [], []
        y_rows = [y_tile(0, by_vector, nc.vector.tensor_copy)]
        dealt00 = deal_w2(by_vector, 0, 0)
        y_rows.append(y_tile(1, by_scalar, nc.scalar.copy))
        gather_y(VECTOR, 0, 0, BANK)
        y_rows.append(y_tile(2, by_scalar, nc.scalar.copy))
        y_rows.append(y_tile(3, by_scalar, nc.scalar.copy))
        quantise_w2(0, 0, dealt00)
        e_pair(0, [0], 0)
        dealt01 = deal_w2(by_vector, 0, 1)
        dealt11 = deal_w2(second_pair, 1, 1)
        quantise_w2(0, 1, dealt01)
        e_pair(0, [1], 0)
        quantise_w2(1, 1, dealt11)
        e_pair(1, [1], 1)
        dealt10 = second_pair([P, 2, P, PACK], BF16)
        columns = w2_raw[0][:].rearrange("p j (m t) -> p t m j", t=PACK)[:, 2:]
        nc.gpsimd.tensor_scalar(dealt10[:], columns, 1.0, 0.0, MULT, ADD)
        gather_y(SCALAR, 2, 0, BANK)
        gather_y(VECTOR, 1, 0, BANK)
        gather_y(VECTOR, 0, second, BANK)
        gather_y(VECTOR, 1, second, BANK)
        quantise_weights(w2_mx, "behind_w2", 0, dealt10, 2, 1, behind)
        e_pair(1, [0], 1)
        for t in range(2):
            e_rows.append(rows_out(e_banks[t], by_scalar, nc.scalar.copy))
        gather_y(SCALAR, 3, 0, BANK)
        gather_y(SCALAR, 2, second, MIDDLE)
        for t in range(2, PACK):
            e_rows.append(rows_out(e_banks[t], by_scalar, nc.scalar.copy))
        gather_y(SCALAR, 3, second, BANK)

        def activate(z_values, totals):
            nc.scalar.activation(
                z_values.rearrange("p (c i t) -> p c t i", i=2, t=PACK),
                totals.rearrange("p t (c i) -> p c t i", i=2),
                SILU,
            )

        def activated(totals):
            z_values = by_scalar([P, PACK * totals.shape[2]], BF16)
            activate(z_values[:], totals[:, :, :])
            return z_values

        def last_product(z_values, r0, places):
            width = z_values.shape[1] // PACK
            z_codes = by_vector([P, width], U32)
            z_plane = held(f"z_plane{r0}", [P, width], U8)
            nc.vector.quantize_mx(out=z_codes[:].bitcast(FP8X4), scales=z_plane[:], in_=z_values[:, :])
            products = places(width)
            for a in range(ROW_TILES):
                nc.tensor.matmul_mx(
                    out=products[a],
                    lhsT=w3_codes[:, 2 * a * P : 2 * (a + 1) * P].bitcast(FP4X4),
                    lhsT_scale=w3_plane[:, a * P : (a + 1) * P],
                    rhs=z_codes[:].bitcast(FP8X4),
                    rhs_scale=z_plane[:],
                    start=True,
                    stop=True,
                )
            return products

        def a_bank_each(width):
            return [bank[:, :width] for bank in banks_of(ROW_TILES)]

        def both_rows(z_values, r0, tag="early_bank"):
            width = z_values.shape[1] // PACK
            rows = banks_of(1, tag)[0][:, : ROW_TILES * width].rearrange("p (a r) -> p a r", a=ROW_TILES)
            last_product(z_values, r0, lambda width: [rows[:, a, :] for a in range(ROW_TILES)])
            return rows

        out_view = out.rearrange("(a p) r -> p a r", p=P)

        def store(product, where, new_tile, copy, queue=nc.sync):
            result = new_tile(list(product.shape), F32)
            copy(result[:], product)
            queue.dma_start(where, result[:])

        on_scalar = (by_scalar, nc.scalar.copy)
        on_vector = (by_vector, nc.vector.tensor_copy)

        half = BANK // 2
        first_totals = behind("behind_w2", [P, PACK, BANK], F32)
        for t in range(PACK - 1):
            add_gathered(first_totals[:, t, :], t, 0)
        for r0 in (0, half):
            add_gathered(first_totals[:, PACK - 1, r0 : r0 + half], PACK - 1, r0)
        z_first = by_vector([P, PACK * BANK], BF16)
        for r0 in (0, half):
            activate(z_first[:, PACK * r0 : PACK * (r0 + half)], first_totals[:, :, r0 : r0 + half])

        second_totals = sums(second, MIDDLE)
        gather_y(SCALAR, 2, third, 2 * TAIL)
        z_second = activated(second_totals)
        first_out = [both_rows(z_first[:, PACK * r0 : PACK * (r0 + half)], r0) for r0 in (0, half)]
        last_totals = by_vector([P, PACK, 2 * TAIL], F32)
        for t in range(2):
            add_gathered(last_totals[:, t, :], t, third)
        for r0 in (0, TAIL):
            for t in range(2, PACK):
                add_gathered(last_totals[:, t, r0 : r0 + TAIL], t, third + r0)
        store(first_out[0], out_view[:, :, :half], *on_scalar)
        store(first_out[1], out_view[:, :, half:second], *on_scalar)
        z_third = activated(last_totals[:, :, :TAIL])
        z_fourth = activated(last_totals[:, :, TAIL:])
        second_out = last_product(z_second, second, a_bank_each)
        third_out = both_rows(z_third, third, "odd_bank")
        fourth_out = last_product(z_fourth, fourth, lambda width: [bank[:, :width] for bank in banks_of(2, "even_bank")])

        store(second_out[0], out_view[:, 0, second:third], *on_scalar)
        store(second_out[1], out_view[:, 1, second:third], *on_scalar)
        store(third_out, out_view[:, :, third:fourth], *on_vector)
        last_rows = by_scalar([P, ROW_TILES, TAIL], F32)
        nc.scalar.copy(last_rows[:, 0, :], fourth_out[0])
        nc.vector.tensor_copy(last_rows[:, 1, :], fourth_out[1])
        nc.scalar.dma_start(out_view[:, :, fourth:], last_rows[:])
